import numpy as np, ml_dtypes
CORES = [2,6,10,14,18,22,26,30]
N = 8
import mx_ref
BF = ml_dtypes.bfloat16
def cols(t, e):
    v = np.concatenate([t.reshape(128, -1, 4), np.zeros((128, 1, 4), BF)], axis=1)
    return np.ascontiguousarray(v[:, e]).reshape(128, -1)
def tile(rs):
    return np.stack(rs, axis=2).reshape(128, -1).astype(BF)
def cut(t, i, w=512):
    return t[:, w * i:w * i + w]
def f(rng, *shape):
    return mx_ref.flush((rng.standard_normal(shape, dtype=np.float32) * np.exp2(rng.integers(-2, 3, shape[:-1] + (1,)))).astype(BF))
def wide(rng, *shape, cols=0):
    v = rng.standard_normal(shape, dtype=np.float32) * np.exp2(rng.integers(-12, 13, shape)).astype(np.float32)
    if cols: v *= np.repeat(np.exp2(rng.integers(-cols, cols + 1, shape[:-2] + (1, shape[-1] // 4))) * (rng.random(shape[:-2] + (1, shape[-1] // 4)) > 0.0625), 4, axis=-1).astype(np.float32)
    return mx_ref.flush(v.astype(BF))
T, ST = 512, 128
def flags(rng, n, new):
    s = np.zeros((N, T), bool)
    for r in range(N):
        s[r, 0] = new[r] > 0
        s[r, 1 + rng.permutation(T - 1)[:int(n[r]) - int(new[r])]] = True
    return s
def borders(rng):
    new = rng.integers(0, 2, N); new[0] = 1
    return new
def make(rng, s, far=2, spread=False):
    t = np.zeros((128, 128, 4), np.float32); t[:, :16] = rng.standard_normal((128, 16, 4), dtype=np.float32)
    if spread: t[64:] = 0
    t = mx_ref.flush(t.reshape(128, 512).astype(BF))
    k = (rng.integers(0, 16) + np.cumsum(s.reshape(-1) * rng.integers(1, 16, N * T))) % 16
    c = t.astype(np.float32).reshape(128, 128, 4)[:, k] + rng.standard_normal((128, N * T, 4), dtype=np.float32) * np.float32(0.125)
    if spread: c[64:] = wide(rng, 64, 4 * N * T).astype(np.float32).reshape(64, N * T, 4)
    c = c * np.exp2(rng.integers(-far, far + 1, (N * T, 1))).astype(np.float32)
    x = np.ascontiguousarray(c.reshape(128, N, 4 * T).transpose(1, 0, 2)).astype(BF)
    return {"x": mx_ref.flush(x), "p": np.stack([t] * N), "a": f(rng, N, 128, 2048), "w": f(rng, N, 128, 512), "v": f(rng, N, 128, 512)}
def setup_inputs(rng):
    return make(rng, flags(rng, rng.integers(1, ST + 1, N), borders(rng)))
def setup_inputs_border(rng):
    return make(rng, flags(rng, rng.integers(1, ST + 1, N), np.arange(N) == 0))
def setup_inputs_dense(rng):
    n = np.full(N, ST); n[0] = ST - rng.integers(1, N)
    return make(rng, flags(rng, n, borders(rng)))
def setup_inputs_one(rng):
    return make(rng, flags(rng, np.ones(N, int), np.arange(N) == 0))
def setup_inputs_spread(rng):
    return make(rng, flags(rng, rng.integers(1, ST + 1, N), borders(rng)), far=8, spread=True)
def setup_inputs_ties(rng):
    d = setup_inputs(rng)
    m = np.cumsum(flags(rng, rng.integers(1, ST + 1, N), borders(rng)).reshape(-1)) - 1; n = int(m[-1]) + 1
    u = np.zeros((128, 8, 4), np.float32); u[:64] = rng.choice([-1, 1], (64, 8, 4)) * rng.uniform(0.75, 1.25, (64, 8, 4))
    g = np.zeros((128, 1, 4), np.float32); g[64:] = rng.choice([-1, 1], (64, 1, 4))
    t = np.zeros((128, 128, 4), np.float32); t[:, :8] = u + g; t[:, 8:16] = u + g
    k = np.cumsum(rng.integers(1, 8, n)) % 8
    big = int(np.argmax(np.bincount(m)))
    k = (k - k[big]) % 8
    neg = rng.permutation(n) % 2
    c = u[:, k[m]] + g * np.where(neg[m] > 0, -2, 1).astype(np.float32)[:, None] + rng.standard_normal((128, N * T, 4), dtype=np.float32) * np.float32(0.125)
    c = c * np.exp2(rng.integers(-2, 3, (N * T, 1))).astype(np.float32)
    zero = (k[m] == 0) & (rng.random(N * T) < 0.25); zero[np.flatnonzero(m == big)[1]] = True
    c[:, zero] = 0
    d["x"] = mx_ref.flush(np.ascontiguousarray(c.reshape(128, N, 4 * T).transpose(1, 0, 2)).astype(BF))
    d["p"] = np.stack([mx_ref.flush(t.reshape(128, 512).astype(BF))] * N)
    return d
def labels(x, p):
    return np.stack([np.argmax(mx_ref.matmul(mx_ref.quantize(p[r]), mx_ref.quantize(x[r]))[:16] + np.float32(0.0), axis=0) for r in range(N)])
def starts(l):
    e = l.reshape(-1)
    return np.concatenate([[True], e[1:] != e[:-1]])
def check_inputs(d):
    b = []
    for r in range(N):
        if not np.array_equal(d["p"][r], d["p"][0]): b.append("p (the same on all ranks)")
        if d["p"][r][:, 64:].astype(np.float32).any(): b.append("p (zero columns)")
    n = starts(labels(d["x"], d["p"])).reshape(N, T).sum(axis=1)
    if n.min() < 1 or n.max() > ST: b.append("x (runs that start on a rank)")
    return b
def reference(x, p, a, w, v):
    l = labels(x, p); s = starts(l)
    m = np.add.accumulate(s.astype(int)) - 1
    first = np.flatnonzero(s)
    seq = np.concatenate([x[r] for r in range(N)], axis=1)
    h = []
    for r in range(N):
        e = np.full(ST, -1); mine = first[r::N]; e[:len(mine)] = mine
        c = mx_ref.quantize(cols(seq, e))
        h.append(tile([np.maximum(mx_ref.matmul(mx_ref.quantize(np.ascontiguousarray(cut(a[r], i))), c), np.float32(0)) * np.float32(0.05) for i in range(4)]))
    h = np.concatenate(h, axis=1)
    y = np.zeros((N, 128, T), np.float32); lb = np.zeros((N, 2, T), np.float32)
    for r in range(N):
        k = m[r * T:r * T + T]
        hk = mx_ref.quantize(cols(h, (k % N) * ST + k // N))
        y[r] = mx_ref.matmul(mx_ref.quantize(w[r]), mx_ref.quantize(x[r])) + mx_ref.matmul(mx_ref.quantize(v[r]), hk)
        lb[r, 0] = l[r]; lb[r, 1] = k
    return {"y": y, "lb": lb}

@@ -1,0 +1,422 @@
+from concourse.bass import DstId, RemoteDMATransfer
+from concourse.mybir import dt, AluOpType, AxisListType, ActivationFunctionType
+
+N = 8
+S = 18
+NC = N * S
+ROOM = 160
+FW = ROOM + 512 + 128
+UW = N * 32
+
+F32, BF, I32, U16, C8, U8 = "float32", "bfloat16", "int32", "uint16", "float8_e4m3fn_x4", "uint8"
+
+
+def _sb(n, d):
+    return ("sbuf", [128, n], d)
+
+
+SCRATCH = {
+    "ps": ("psum", [128, 4096], F32),
+    "xs": _sb(2048, BF), "pt": _sb(576, BF), "at": _sb(2048, BF), "wt": _sb(512, BF), "vt": _sb(512, BF),
+    "qx": _sb(512, C8), "sx": _sb(512, U8), "qp": _sb(144, C8), "sp": _sb(144, U8),
+    "qa": _sb(512, C8), "sa": _sb(512, U8), "qw": _sb(128, C8), "sw": _sb(128, U8), "qv": _sb(128, C8), "sv": _sb(128, U8),
+    "ct": _sb(592, BF), "qc": _sb(NC + 126, C8), "sc": _sb(NC + 126, U8), "lt": _sb(512, BF), "ql": _sb(128, C8),
+    "sl": _sb(128, U8), "ht": _sb(576, BF), "qh": _sb(NC + 126, C8), "sh": _sb(NC + 126, U8),
+    "pi": _sb(1, I32), "pj": _sb(4, I32), "pf": _sb(4, F32), "j4i": _sb(32, I32), "j4m": _sb(32, I32), "j4": _sb(32, F32),
+    "trash": _sb(32, F32), "vali": _sb(256, F32), "val": _sb(256, F32), "prmi": _sb(8, I32), "prm": _sb(8, U16),
+    "ypi": _sb(128, I32), "msk": _sb(128, F32), "d0": _sb(128, F32), "c0": _sb(1, F32), "c1": _sb(1, F32),
+    "c2": _sb(1, F32), "c3": _sb(1, F32), "kr": _sb(1, F32), "th": _sb(1, F32), "lane": _sb(1, F32), "g64": _sb(1, F32),
+    "rst": _sb(2, F32), "reset": _sb(128, F32), "one2": _sb(128, BF), "one": _sb(32, F32), "kw": _sb(32, F32),
+    "z": _sb(288, F32), "mx": _sb(256, F32), "nn": _sb(256, BF), "ss": _sb(256, BF), "gg": _sb(64, F32), "h2": _sb(64, F32),
+    "fl": _sb(32, F32), "cc": _sb(64, F32), "cct": _sb(64, F32), "z1": _sb(1, F32), "z2": _sb(1, F32), "dm": _sb(32, F32),
+    "dmt": _sb(32, F32), "enc": _sb(1, F32), "e16": _sb(2, U16), "owni": _sb(1, I32),
+    "fj": _sb(32, F32), "lj": _sb(1, F32), "dm2": _sb(32, F32), "dm2t": _sb(32, F32), "last": _sb(1, F32),
+    "lastl": _sb(2, U16), "iw": _sb(32, F32), "nfe": _sb(32, F32), "nfd": _sb(32, F32),
+    "offf": _sb(16, F32), "offl": _sb(16, U16), "ff": _sb(FW, F32),
+    "mk": _sb(128, F32), "sg": _sb(128, F32), "u0": _sb(32, F32), "ut": _sb(32, F32), "us": _sb(32, F32), "uu": _sb(UW, F32),
+    "m16": _sb(8, U16), "mi": _sb(8, I32), "fi": _sb(8, I32), "la": _sb(8, I32), "c7": _sb(8, I32), "c7f": _sb(8, F32),
+    "ne": _sb(8, F32), "sb": _sb(8, F32), "ci": _sb(8, I32), "cif": _sb(8, F32), "sbb": _sb(8, F32), "nf0": _sb(1, F32),
+    "ro": _sb(2, U16), "lst": _sb(32, U16),
+    "tcs": _sb(32, F32), "cdw": _sb(32, F32), "cd": _sb(64, F32),
+    "tc": _sb(64, F32), "ii": _sb(64, I32), "t1": _sb(64, I32), "kk": _sb(64, I32), "k18": _sb(64, F32), "fx": _sb(64, F32),
+    "s1": _sb(64, F32), "s2": _sb(64, F32), "fin": _sb(32, U16), "lb0": _sb(32, F32), "lb1": _sb(32, F32),
+    "wx": _sb(512, F32), "vw": _sb(NC, F32), "yt": _sb(512, F32),
+}
+SEMAPHORES = ["kv", "ks", "kt", "kg", "dp", "dx0", "dx1", "dx2", "dx3", "da0", "da1", "dw", "dv", "dy0", "dy1", "dy2",
+              "dl0", "dl1", "e0", "e1", "e2", "l0", "l1", "l2"]
+
+
+def _mask(es):
+    return sum(1 << e for e in es)
+
+
+def _near(core, d, off_engines, topo):
+    return [e for e in topo.engines(core, d) if e not in off_engines][:2]
+
+
+def _plan(core, cores, topo):
+    ch = topo.chip(core)
+    off = [d for d in cores if topo.chip(d) != ch]
+    off.sort(key=lambda d: (0 if topo.mates(ch, topo.chip(d)) else 1 if topo.same_plane(ch, topo.chip(d)) else 2, d))
+    eo = topo.engines(core, off[0])
+    plan = {}
+    for i, d in enumerate(off):
+        j = 4 * (i - 4)
+        plan[d] = ([eo[2 * i]], [eo[2 * i + 1]]) if i < 4 else (eo[j + 1:j + 4:2], eo[j:j + 4:2])
+    for d in cores:
+        if d != core and topo.chip(d) == ch:
+            plan[d] = (_near(core, d, eo, topo),) * 2
+    return plan
+
+
+def _plan0(core, cores, topo):
+    ch = topo.chip(core)
+    eo = [topo.engines(core, d) for d in cores if topo.chip(d) != ch][0]
+    return {d: eo if topo.chip(d) != ch else _near(core, d, eo, topo) for d in cores[cores.index(core) + 1:]}
+
+
+def _ahead(core, cores, topo):
+    return all(topo.chip(d) == topo.chip(core) for d in cores[cores.index(core) + 1:])
+
+
+def rank_program(g, core, T, topo):
+    r = T.rank_of(core)
+    if r is None:
+        return
+    A, X, AF = AluOpType, AxisListType.X, ActivationFunctionType
+    cores = list(T.cores)
+    vec, sca, ten, syn = g.vector, g.scalar, g.tensor, g.sync
+    queue = {"v": vec, "s": sca, "t": ten, "g": g, "y": syn}
+    cnt, known = {}, {}
+
+    def done(ins, sem, n=1):
+        ins.then_inc(T.sem[sem], n)
+        cnt[sem] = cnt.get(sem, 0) + n
+        return (sem, cnt[sem])
+
+    def need(qn, *toks):
+        for s, v in toks:
+            if known.get((qn, s), 0) < v:
+                queue[qn].wait_ge(T.sem[s], v)
+                known[(qn, s)] = v
+
+    def V(f, *args, w=()):
+        need("v", *w)
+        return done(f(*args), "kv")
+
+    def ts(out, i, a, b, o0, o1=None, w=()):
+        need("v", *w)
+        if o1 is None:
+            return done(vec.tensor_scalar(out, i, a, None, o0), "kv")
+        return done(vec.tensor_scalar(out, i, a, b, o0, o1), "kv")
+
+    def io(out, pattern, base, cm):
+        return done(g.iota(out, pattern, base, cm, allow_small_or_imprecise_dtypes=True), "kg")
+
+    def sc(out, in_, w=()):
+        need("s", *w)
+        return done(sca.activation(out, in_, AF.Copy), "ks")
+
+    def si(out, in_, bias, scale, w=()):
+        need("s", *w)
+        return done(sca.activation(out, in_, AF.Identity, bias, scale), "ks")
+
+    tt, cp, ms, rd, scn, tr, qz = (vec.tensor_tensor, vec.tensor_copy, vec.memset, vec.tensor_reduce,
+                                   vec.tensor_tensor_scan, vec.transpose, vec.quantize_mx)
+
+    def load(qn, out, in_, sem):
+        return done(queue[qn].dma_start(out, in_), sem, 16)
+
+    dx = {}
+    dx[0] = load("y", T.xs[:, 0:512], T.x[:, 0:512], "dx0")
+    dp = load("s", T.pt[:, 0:128], T.p[:, 0:128], "dp")
+    dx[2] = load("s", T.xs[:, 1024:1536], T.x[:, 1024:1536], "dx2")
+    dx[1] = load("y", T.xs[:, 512:1024], T.x[:, 512:1024], "dx1")
+    dx[3] = load("s", T.xs[:, 1536:2048], T.x[:, 1536:2048], "dx3")
+    da = [load("s", T.at[:, 0:1024], T.a[:, 0:1024], "da0")]
+    ahead = _ahead(core, cores, topo)
+    if ahead:
+        da.append(load("s", T.at[:, 1024:2048], T.a[:, 1024:2048], "da1"))
+        dv = load("s", T.vt[:], T.v[:], "dv")
+        dw = load("s", T.wt[:], T.w[:], "dw")
+
+    kpi = io(T.pi[:], [[1, 1]], 0, 1)
+    kj4 = io(T.j4i[:], [[4, 32]], 0, 128)
+    kone = io(T.one[:], [[0, 32]], 1, 0)
+    kypi = io(T.ypi[:], [[0, 32], [1, 4]], 0, 0)
+    kprm = io(T.prmi[:], [[1, 8]], 0, 8)
+    kgg = io(T.gg[:], [[0, 64]], 0, 0)
+    io(T.z[:, 24:32], [[0, 8]], 0, 0)
+    kc = io(T.one2[:], [[0, 128]], 1, 0)
+    kval = io(T.vali[:], [[128, 16], [4, 16]], 0, 0)
+    io(T.iw[:], [[0, 32]], 0, 0)
+    kff = io(T.ff[:, 0:ROOM], [[0, ROOM]], 0, 0)
+    if ahead:
+        kff = io(T.lt[:], [[0, 512]], 0, 0)
+    c = V(ms, T.reset[:], 0.0)
+    ts(T.pj[:, 0:1], T.pi[:], 31, None, A.bitwise_and, w=(kpi,))
+    ts(T.pj[:, 1:2], T.pi[:], 15, None, A.bitwise_and)
+    ts(T.pj[:, 2:3], T.pi[:], 3, None, A.bitwise_and)
+    c2 = ts(T.pj[:, 3:4], T.pi[:], 2, 3, A.logical_shift_right, A.bitwise_and)
+    V(ms, T.reset[:, 0:128:16], -5e29, w=(c,))
+    cpf = V(cp, T.pf[:], T.pj[:], w=(c2,))
+    c = ts(T.j4m[:], T.j4i[:], 4095, None, A.bitwise_and, w=(kj4,))
+    ckr = ts(T.kr[:], T.pf[:, 0:1], 16.0, None, A.is_lt, w=(cpf,))
+    cg = V(tt, T.lane[:], T.pf[:, 0:1], T.pf[:, 1:2], A.subtract)
+    cj4 = V(cp, T.j4[:], T.j4m[:], w=(c,))
+    ts(T.c0[:], T.pf[:, 0:1], 0.0, -1.0, A.is_equal, A.mult)
+    ts(T.c1[:], T.pf[:, 0:1], 17.0, 16.0 / 256, A.is_equal, A.mult)
+    ts(T.c3[:], T.pf[:, 0:1], 17.0, -17.0 / 256, A.is_equal, A.mult)
+    ts(T.c2[:], T.pf[:, 0:1], 16.0, 1.0 / 256, A.is_equal, A.mult)
+    tcol, rho = T.pf[:, 2:3], T.pf[:, 3:4]
+    ts(T.msk[:], T.ypi[:], rho, None, A.is_equal, w=(kypi,))
+    ts(T.d0[:], T.ypi[:], 0.0, None, A.not_equal)
+    c2 = ts(T.prmi[:], T.prmi[:], 127, None, A.bitwise_and, w=(kprm,))
+    V(ms, T.gg[:, 0:1], 99.0, w=(kgg,))
+    V(cp, T.prm[:], T.prmi[:], w=(c2,))
+    turn = 4.0 * ((r + 1) % N) + 4.0 * N * r
+    si(T.th[:], T.pf[:, 2:3], 0.0, 0.5, w=(cpf,))
+    si(T.rst[:, 0:1], T.pf[:, 1:2], -0.25 * turn, -0.25)
+    si(T.rst[:, 1:2], T.pf[:, 1:2], -0.25 * (turn + 16.0), -0.25)
+    need("s", kone, ckr)
+    si(T.kw[:], T.one[:], 0.0, T.kr[:])
+    kg64 = si(T.g64[:], T.lane[:], 0.0, 4.0, w=(cg,))
+    si(T.trash[:], T.j4[:], float(ROOM), 0.25, w=(cj4,))
+    kval = si(T.val[:], T.vali[:], T.g64[:], 1.0, w=(kval, kg64))
+
+    c = V(cp, T.pt[:, 128:256], T.pt[:, 0:128], w=(dp,))
+    V(cp, T.pt[:, 512:576], T.pt[:, 0:64])
+    c = V(cp, T.pt[:, 256:512], T.pt[:, 0:256], w=(c,))
+    kqp = V(qz, T.qp[:], T.sp[:], T.pt[:], w=(c,))
+
+    kqx, ksc, kch = {}, {}, {}
+
+    def pack(i):
+        b, h = i % 2, i // 2
+        kqx[i] = V(qz, T.qx[:, 128 * i:128 * i + 128], T.sx[:, 128 * i:128 * i + 128], T.xs[:, 512 * i:512 * i + 512],
+                   w=(dx[i],))
+        need("t", kqp, kqx[i])
+        ksc[b] = done(ten.matmul_mx(T.ps[:, 512 * b:512 * b + 128], T.qp[:, 16 * h:16 * h + 128],
+                                    T.sp[:, 16 * h:16 * h + 128], T.qx[:, 128 * i:128 * i + 128],
+                                    T.sx[:, 128 * i:128 * i + 128], h == 0, h == 1), "kt")
+
+    def step(b, n):
+        k = slice(128 * b, 128 * b + 128)
+        z, before = T.z[:, 32 + 128 * b:160 + 128 * b], T.z[:, 31 + 128 * b:159 + 128 * b]
+        if n == 0:
+            kch[b] = V(tr, z, T.ps[:, 512 * b:512 * b + 128], w=(ksc[b],))
+        elif n == 1:
+            kch[b] = V(scn, T.mx[:, k], before, T.reset[:], 0.0, A.max, A.add, w=(kch[b], kc))
+        elif n == 2:
+            kch[b] = V(tt, T.nn[:, k], z, T.mx[:, k], A.is_le, w=(kch[b],))
+        else:
+            kch[b] = V(scn, T.ss[:, k], T.nn[:, k], T.one2[:], 0.0, A.mult, A.add, w=(kch[b],))
+        return kch[b]
+
+    pack(0), pack(2), step(0, 0), step(0, 1), pack(1), pack(3), step(0, 2), step(1, 0), step(0, 3), step(1, 1)
+    V(cp, T.gg[:, 17:18], T.ss[:, 15:16], w=(kch[0],))
+    step(1, 2)
+    c = step(1, 3)
+    for h in (0, 1):
+        V(cp, T.gg[:, 1 + 8 * h:9 + 8 * h], T.ss[:, 16 * h + 15:256:32], w=(c,))
+        c2 = V(cp, T.gg[:, 32 + 8 * h:40 + 8 * h], T.ss[:, 16 * h + 15:256:32])
+    c = V(tr, T.h2[:], T.gg[:], w=(c2,))
+    here, prev = T.h2[:, 32:64], T.h2[:, 31:63]
+    kfl = V(tt, T.fl[:], here, prev, A.not_equal, w=(c,))
+    kz1 = ts(T.z1[:], T.h2[:, 0:1], T.c1[:], T.c3[:], A.mult, A.add)
+    cs = T.cc[:, 0:32]
+    kcs = V(scn, cs, T.one[:], T.fl[:], T.c0[:], A.mult, A.add, w=(kfl,))
+    kz2 = ts(T.z2[:], T.h2[:, 31:32], T.c2[:], T.z1[:], A.mult, A.add, w=(kz1,))
+    c = ts(T.dm[:], T.kw[:], T.cc[:, 31:32], T.z2[:], A.mult, A.add, w=(kz2, kcs, kval))
+    knf = V(tt, T.nfe[:], here, prev, A.is_equal)
+    kdm = V(tr, T.dmt[:], T.dm[:], w=(c,))
+    knf = V(tt, T.nfd[:], T.nfe[:], T.trash[:], A.mult, w=(knf,))
+    ken = V(rd, T.enc[:], T.dmt[:], X, A.add, w=(kdm,))
+    ke16 = ts(T.e16[:, 0:1], T.enc[:], 256.0, None, A.mult, w=(ken,))
+    kcx = V(tt, T.cc[:, 32:64], cs, T.nfd[:], A.max, w=(knf,))
+    kfj = V(tt, T.fj[:], T.fl[:], T.j4[:], A.mult)
+
+    arrive = {"e0": 0, "e1": 0, "e2": 0}
+    for s in cores:
+        if s != core:
+            n = sum(len(es) for es in _plan(s, cores, topo)[core])
+            arrive["e0"] += len(_plan0(s, cores, topo).get(core, []))
+            arrive["e1"] += n * (2 if _ahead(s, cores, topo) else 1)
+            arrive["e2"] += n
+
+    def did(d):
+        rid, pid, _ = topo.addr(d)
+        return DstId(rid=rid, pnc=pid)
+
+    groups = {}
+    for d, e in _plan0(core, cores, topo).items():
+        groups.setdefault(tuple(e), []).append(d)
+    if groups:
+        need("g", ke16)
+        g.remote_dma_fused(
+            [RemoteDMATransfer(dst_ids=[did(d) for d in ds], dma_engine_mask=_mask(e), remote_sem=T.sem.e0,
+                               srcs=[T.e16[:, 0:1]], dsts=[T.m16[:, r:r + 1] for d in ds]) for e, ds in groups.items()],
+            local_sem=T.sem.l0)
+        cnt["l0"] = sum(len(e) for e in groups)
+    if not ahead:
+        need("y", ("l0", cnt["l0"]))
+        da.append(load("y", T.at[:, 1024:2048], T.a[:, 1024:2048], "da1"))
+
+    plan = _plan(core, cores, topo)
+
+    def exchange(codes, plane, first, width, at, rsem, lsem):
+        land = (T.qc, T.sc) if rsem == "e1" else (T.qh, T.sh)
+        for part in (0, 1):
+            tl = []
+            for d, es in plan.items():
+                k = first[d]
+                slot = NC + S * (((r - T.rank_of(d)) % N) - 1) + at
+                if part == 0:
+                    src, dst = codes[:, k:k + width].bitcast(dt.uint8), land[0][:, slot:slot + width].bitcast(dt.uint8)
+                else:
+                    src, dst = plane[:, k:k + width], land[1][:, slot:slot + width]
+                tl.append(RemoteDMATransfer(dst_ids=[did(d)], dma_engine_mask=_mask(es[part]), remote_sem=T.sem[rsem],
+                                            srcs=[src], dsts=[dst]))
+                cnt[lsem] = cnt.get(lsem, 0) + len(es[part])
+            g.remote_dma_fused(tl, local_sem=T.sem[lsem])
+
+    V(scn, T.iw[:, 1:17], T.one[:, 0:16], T.dmt[:, 0:16], 0.0, A.mult, A.add, w=(kdm, kff))
+    kiw = V(tr, T.cct[:], T.cc[:], w=(kcx,))
+    klj = V(rd, T.lj[:], T.fj[:], X, A.max, w=(kfj,))
+    kof = V(tt, T.offf[:], T.cct[:, 32:48], T.iw[:, 0:16], A.add, w=(kiw,))
+    klj = ts(T.dm2[:], T.one[:], T.lj[:], None, A.mult, w=(klj,))
+    kof = V(cp, T.offl[:], T.offf[:], w=(kof,))
+    klj = V(tr, T.dm2t[:], T.dm2[:], w=(klj,))
+    if r:
+        V(cp, T.owni[:], T.e16[:, 0:1], w=(ke16,))
+    klj = V(rd, T.last[:], T.dm2t[:, 0:16], X, A.max, w=(klj,))
+    klast = ts(T.lastl[:, 0:1], tcol, T.last[:], None, A.add, w=(klj,))
+    c = V(cp, T.ff[:, 0:FW].indirect(T.offl[:]), T.val[:], w=(kof,))
+    need("s", klast, kff, dx[0], dx[1], dx[2], dx[3])
+    if ahead:
+        klt = sc(T.lt[:, 0:16], T.xs[:, 0:2048].indirect(T.lastl[:, 0:1]))
+        klt = V(qz, T.ql[:], T.sl[:], T.lt[:], w=(klt,))
+        need("g", klt)
+        exchange(T.ql, T.sl, {d: 0 for d in plan}, 2, 16, "e1", "l1")
+    for b in range(N):
+        klb = sc(T.ct[:, 72 * b + 64:72 * b + 80], T.xs[:, 0:2048].indirect(T.lastl[:, 0:1]))
+    c = V(tt, T.mk[:], T.ff[:, 0:128].indirect(T.prm[:, 0:8]), T.msk[:], A.mult, w=(c,))
+    if r:
+        ts(T.fi[:, r:r + 1], T.owni[:], 4, 15, A.logical_shift_right, A.bitwise_and)
+    c = V(scn, T.sg[:], T.d0[:], T.mk[:], 0.0, A.mult, A.add, w=(c,))
+    c = ts(T.u0[:], T.sg[:, 3:128:4], T.th[:], None, A.add, w=(c,))
+    c = V(tr, T.ut[:], T.u0[:], w=(c,))
+    V(tt, T.us[:, 0:16], T.ut[:, 0:16], T.ut[:, 16:32], A.add, w=(c,))
+    c = V(tt, T.us[:, 16:32], T.ut[:, 0:16], T.ut[:, 16:32], A.add)
+    kuu = [V(tr, T.uu[:, 0:32], T.us[:], w=(c,))]
+    nb = min(r + 2, N)
+    for b in range(1, nb):
+        if b % 2:
+            kv = V(cp, T.uu[:, 32 * b:32 * b + 32], T.uu[:, 0:32], w=(kuu[0],))
+        else:
+            ks = sc(T.uu[:, 32 * b:32 * b + 32], T.uu[:, 0:32], w=(kuu[0],))
+    kuu = [kv] + ([ks] if nb > 2 else [])
+
+    if r == 0:
+        V(ms, T.nf0[:], 0.0)
+        sb = sbb = T.sb[:, 0:1]
+        c = V(ms, sb, 0.0)
+    else:
+        need("v", ("e0", arrive["e0"]))
+        cnt["e0"] = arrive["e0"]
+        sb, sbb = T.sb[:, r - 1:r], T.sbb[:, r - 1:r]
+        c = V(cp, T.mi[:, 0:r], T.m16[:, 0:r])
+        if r > 1:
+            ts(T.fi[:, 1:r], T.mi[:, 1:r], 4, 15, A.logical_shift_right, A.bitwise_and, w=(c,))
+        c = ts(T.la[:, 0:r], T.mi[:, 0:r], 15, None, A.bitwise_and, w=(c,))
+        c2 = ts(T.c7[:, 0:r], T.mi[:, 0:r], 8, 7, A.logical_shift_right, A.bitwise_and)
+        V(tt, T.ne[:, 0:r], T.fi[:, 1:r + 1], T.la[:, 0:r], A.not_equal, w=(c,))
+        c = V(cp, T.c7f[:, 0:r], T.c7[:, 0:r], w=(c2,))
+        c = V(scn, T.sb[:, 0:r], T.c7f[:, 0:r], T.ne[:, 0:r], 0.0, A.add, A.add, w=(c,))
+    c = ts(T.ro[:], T.rst[:], sb, -4.0, A.add, A.mult, w=(c,))
+    klst = V(cp, T.lst[:], T.uu[:, 0:32 * nb].indirect(T.ro[:, 0:2]), w=(c, *kuu))
+    need("s", klst, klb)
+    for b in range(5, N):
+        kcs2 = sc(T.ct[:, 72 * b:72 * b + 64], T.xs[:, 0:2048].indirect(T.lst[:, 4 * b:4 * b + 4]))
+    for b in range(0, 5):
+        c = V(cp, T.ct[:, 72 * b:72 * b + 64], T.xs[:, 0:2048].indirect(T.lst[:, 4 * b:4 * b + 4]), w=(klst, klb))
+    kqc = V(qz, T.qc[:, 0:NC], T.sc[:, 0:NC], T.ct[:, 0:4 * NC], w=(c, kcs2))
+    need("g", kqc)
+    exchange(T.qc, T.sc, {d: S * ((T.rank_of(d) - r - 1) % N) for d in plan}, 16 if ahead else S, 0, "e1", "l1")
+    if not ahead:
+        need("y", ("l1", cnt["l1"]))
+        dv = load("y", T.vt[:], T.v[:], "dv")
+        dw = load("y", T.wt[:], T.w[:], "dw")
+
+    kqa = {}
+    for i in range(4):
+        kqa[i] = V(qz, T.qa[:, 128 * i:128 * i + 128], T.sa[:, 128 * i:128 * i + 128], T.at[:, 512 * i:512 * i + 512],
+                   w=(da[i // 2],))
+    kcd = V(tt, T.tcs[:], T.cct[:, 0:32], T.iw[:], A.add)
+    if r:
+        c = ts(T.ci[:, 0:r], T.mi[:, 0:r], 8, None, A.logical_shift_right)
+        V(tt, T.nf0[:], T.fi[:, r:r + 1], T.la[:, r - 1:r], A.is_equal)
+    kcd = V(tr, T.cdw[:], T.tcs[:], w=(kcd,))
+    if r:
+        c = V(cp, T.cif[:, 0:r], T.ci[:, 0:r], w=(c,))
+    ts(T.lb0[:], here, -1.0, 16.0, A.mult, A.add)
+    if r:
+        c = V(scn, T.sbb[:, 0:r], T.cif[:, 0:r], T.ne[:, 0:r], 0.0, A.add, A.add, w=(c,))
+    for i in range(4):
+        kcp = V(cp, T.cd[:, 16 * i:16 * i + 16], T.cdw[:, 16 * (i // 2):16 * (i // 2) + 16], w=(kcd,))
+    klb1 = ts(T.lb1[:], T.cdw[:], sbb, None, A.add, w=(c,))
+    need("y", klb1)
+    done(syn.dma_start(T.lb[0:1, :], T.lb0[0:16, :]), "dl0", 16)
+    done(syn.dma_start(T.lb[1:2, :], T.lb1[0:16, :]), "dl1", 16)
+
+    need("t", ("e1", arrive["e1"]), kqc)
+    cnt["e1"] = arrive["e1"]
+    kh = []
+    for i in range(4):
+        need("t", kqa[i])
+        o = T.ps[:, 2048 + 512 * i:2048 + 512 * i + NC]
+        m = done(ten.matmul_mx(o, T.qa[:, 128 * i:128 * i + 128], T.sa[:, 128 * i:128 * i + 128],
+                               T.qc[:, NC - S:NC + 126], T.sc[:, NC - S:NC + 126], True, True), "kt")
+        if i % 2 == 0:
+            need("s", m)
+            kh.append(done(sca.activation(T.ht[:, i:576:4], o, AF.Relu, 0.0, 0.05), "ks"))
+        else:
+            kh.append(ts(T.ht[:, i:576:4], o, 0.0, 0.05, A.max, A.mult, w=(m,)))
+    kqh = V(qz, T.qh[:, 0:NC], T.sh[:, 0:NC], T.ht[:], w=kh)
+    need("g", kqh)
+    exchange(T.qh, T.sh, {d: S * ((T.rank_of(d) - r) % N) - 1 for d in plan}, S, 0, "e2", "l2")
+
+    c = V(tr, T.tc[:], T.cd[:], w=(kcp,))
+    ts(T.ii[:], T.tc[:], 0.125, -0.4375, A.mult, A.add, w=(c,))
+    c = ts(T.t1[:], T.tc[:], sb, float(N - r), A.add, A.add)
+    ts(T.fx[:], T.tc[:], 0.0, T.nf0[:], A.is_equal, A.mult)
+    c = ts(T.kk[:], T.t1[:], 7, None, A.bitwise_and, w=(c,))
+    kqv = V(qz, T.qv[:], T.sv[:], T.vt[:], w=(dv,))
+    need("t", kqh, kqv)
+    m = done(ten.matmul_mx(T.ps[:, 1536:1536 + NC], T.qv[:], T.sv[:], T.qh[:, 0:NC], T.sh[:, 0:NC], True, True), "kt")
+    c = ts(T.k18[:], T.kk[:], float(S), 1.0, A.mult, A.add, w=(c,))
+    kqw = V(qz, T.qw[:], T.sw[:], T.wt[:], w=(dw,))
+    need("t", kqw, *kqx.values())
+    kwx = done(ten.matmul_mx(T.ps[:, 1024:1536], T.qw[:], T.sw[:], T.qx[:], T.sx[:], True, True), "kt")
+    kwxs = sc(T.wx[:], T.ps[:, 1024:1536], w=(kwx,))
+    c = V(tt, T.s1[:], T.k18[:], T.ii[:], A.add, w=(c,))
+    V(cp, T.vw[:, 0:1], T.ps[:, 1536 + NC - 2:1536 + NC - 1], w=(m,))
+    c = V(tt, T.s2[:], T.s1[:], T.fx[:], A.subtract, w=(c,))
+    V(cp, T.vw[:, 1:S], T.ps[:, 1536:1536 + S - 1])
+    V(cp, T.fin[:, 0:32:2], T.s2[:, 0:16], w=(c,))
+    kfin = V(cp, T.fin[:, 1:32:2], T.s2[:, 32:48])
+
+    need("t", ("e2", arrive["e2"]))
+    cnt["e2"] = arrive["e2"]
+    m = done(ten.matmul_mx(T.ps[:, 0:128], T.qv[:], T.sv[:], T.qh[:, NC - 2:NC + 126], T.sh[:, NC - 2:NC + 126], True, True), "kt")
+    c = V(cp, T.vw[:, S:NC], T.ps[:, 2:128], w=(m,))
+    for h, (k, e) in enumerate(((0, 128), (128, 320), (320, 512))):
+        c = V(tt, T.yt[:, k:e], T.vw[:, 0:NC].indirect(T.fin[:, k // 16:e // 16]), T.wx[:, k:e], A.add,
+              w=(c, kwxs, kfin) if h == 0 else ())
+        qn = "ysy"[h]
+        need(qn, c)
+        done(queue[qn].dma_start(T.y[:, k:e], T.yt[:, k:e]), "dy%d" % h, 16)
+
+    for s in SEMAPHORES:
+        if cnt.get(s):
+            need("g", (s, cnt[s]))

@@ -2,11 +2,13 @@ from concourse.bass import DstId, RemoteDMATransfer
 from concourse.mybir import dt, AluOpType, AxisListType, ActivationFunctionType
 
 N = 8
-S = 18
+S = 16
+S2 = 18
 NC = N * S
-ROOM = 160
-FW = ROOM + 512 + 128
-UW = N * 32
+ROOM = 136
+GAP = 160
+FW = 19 * GAP
+UW = 9 * 32
 
 F32, BF, I32, U16, C8, U8 = "float32", "bfloat16", "int32", "uint16", "float8_e4m3fn_x4", "uint8"
 
@@ -20,30 +22,28 @@ SCRATCH = {
     "xs": _sb(2048, BF), "pt": _sb(576, BF), "at": _sb(2048, BF), "wt": _sb(512, BF), "vt": _sb(512, BF),
     "qx": _sb(512, C8), "sx": _sb(512, U8), "qp": _sb(144, C8), "sp": _sb(144, U8),
     "qa": _sb(512, C8), "sa": _sb(512, U8), "qw": _sb(128, C8), "sw": _sb(128, U8), "qv": _sb(128, C8), "sv": _sb(128, U8),
-    "ct": _sb(592, BF), "qc": _sb(NC + 126, C8), "sc": _sb(NC + 126, U8), "lt": _sb(512, BF), "ql": _sb(128, C8),
-    "sl": _sb(128, U8), "ht": _sb(576, BF), "qh": _sb(NC + 126, C8), "sh": _sb(NC + 126, U8),
-    "pi": _sb(1, I32), "pj": _sb(4, I32), "pf": _sb(4, F32), "j4i": _sb(32, I32), "j4m": _sb(32, I32), "j4": _sb(32, F32),
-    "trash": _sb(32, F32), "vali": _sb(256, F32), "val": _sb(256, F32), "prmi": _sb(8, I32), "prm": _sb(8, U16),
-    "ypi": _sb(128, I32), "msk": _sb(128, F32), "d0": _sb(128, F32), "c0": _sb(1, F32), "c1": _sb(1, F32),
-    "c2": _sb(1, F32), "c3": _sb(1, F32), "kr": _sb(1, F32), "th": _sb(1, F32), "lane": _sb(1, F32), "g64": _sb(1, F32),
-    "rst": _sb(2, F32), "reset": _sb(128, F32), "one2": _sb(128, BF), "one": _sb(32, F32), "kw": _sb(32, F32),
-    "z": _sb(288, F32), "mx": _sb(256, F32), "nn": _sb(256, BF), "ss": _sb(256, BF), "gg": _sb(64, F32), "h2": _sb(64, F32),
-    "fl": _sb(32, F32), "cc": _sb(64, F32), "cct": _sb(64, F32), "z1": _sb(1, F32), "z2": _sb(1, F32), "dm": _sb(32, F32),
-    "dmt": _sb(32, F32), "enc": _sb(1, F32), "e16": _sb(2, U16), "owni": _sb(1, I32),
-    "fj": _sb(32, F32), "lj": _sb(1, F32), "dm2": _sb(32, F32), "dm2t": _sb(32, F32), "last": _sb(1, F32),
-    "lastl": _sb(2, U16), "iw": _sb(32, F32), "nfe": _sb(32, F32), "nfd": _sb(32, F32),
+    "ct": _sb(512, BF), "qc": _sb(NC + 112, C8), "sc": _sb(NC + 112, U8),
+    "ht": _sb(512, BF), "qh": _sb(NC + 126, C8), "sh": _sb(NC + 126, U8),
+    "pi": _sb(1, I32), "pj": _sb(4, I32), "pf": _sb(4, F32), "io32": _sb(32, F32), "trash": _sb(32, F32),
+    "vali": _sb(256, F32), "val": _sb(256, F32), "prm": _sb(8, U16), "ypi": _sb(128, F32), "yab": _sb(128, F32),
+    "msk": _sb(128, F32), "d0": _sb(128, F32), "c0": _sb(1, F32), "m0": _sb(1, F32), "m31": _sb(1, F32), "k0": _sb(1, F32),
+    "lane": _sb(1, F32), "vb": _sb(1, F32), "tb": _sb(1, F32), "pb": _sb(1, F32), "nrho": _sb(1, F32),
+    "rst": _sb(2, F32), "reset": _sb(128, F32), "one2": _sb(128, BF), "one": _sb(64, F32),
+    "z": _sb(288, F32), "mx": _sb(256, F32), "nn": _sb(256, BF), "ss": _sb(544, BF), "h2": _sb(64, BF),
+    "fl": _sb(64, F32), "cc": _sb(96, F32), "cct": _sb(64, F32), "zf": _sb(1, F32), "dmt": _sb(32, F32),
+    "hs": _sb(1, F32), "e16": _sb(2, U16), "iw": _sb(20, F32), "nfe": _sb(32, F32), "nfd": _sb(32, F32),
     "offf": _sb(16, F32), "offl": _sb(16, U16), "ff": _sb(FW, F32),
-    "mk": _sb(128, F32), "sg": _sb(128, F32), "u0": _sb(32, F32), "ut": _sb(32, F32), "us": _sb(32, F32), "uu": _sb(UW, F32),
+    "mk": _sb(128, F32), "sg": _sb(128, F32), "ut": _sb(32, F32), "us": _sb(32, F32), "uu": _sb(UW, F32),
     "m16": _sb(8, U16), "mi": _sb(8, I32), "fi": _sb(8, I32), "la": _sb(8, I32), "c7": _sb(8, I32), "c7f": _sb(8, F32),
-    "ne": _sb(8, F32), "sb": _sb(8, F32), "ci": _sb(8, I32), "cif": _sb(8, F32), "sbb": _sb(8, F32), "nf0": _sb(1, F32),
+    "ne": _sb(8, F32), "sb": _sb(8, F32), "ci": _sb(8, I32), "cif": _sb(8, F32), "sbb": _sb(8, F32), "nx": _sb(1, F32),
     "ro": _sb(2, U16), "lst": _sb(32, U16),
-    "tcs": _sb(32, F32), "cdw": _sb(32, F32), "cd": _sb(64, F32),
+    "tcs": _sb(64, F32), "cdw": _sb(64, F32), "cd": _sb(64, F32),
     "tc": _sb(64, F32), "ii": _sb(64, I32), "t1": _sb(64, I32), "kk": _sb(64, I32), "k18": _sb(64, F32), "fx": _sb(64, F32),
-    "s1": _sb(64, F32), "s2": _sb(64, F32), "fin": _sb(32, U16), "lb0": _sb(32, F32), "lb1": _sb(32, F32),
-    "wx": _sb(512, F32), "vw": _sb(NC, F32), "yt": _sb(512, F32),
+    "s1": _sb(64, F32), "s2": _sb(64, F32), "fin": _sb(32, U16), "lb1": _sb(32, F32),
+    "wx": _sb(512, F32), "vw": _sb(N * S2, F32), "yt": _sb(512, F32),
 }
-SEMAPHORES = ["kv", "ks", "kt", "kg", "dp", "dx0", "dx1", "dx2", "dx3", "da0", "da1", "dw", "dv", "dy0", "dy1", "dy2",
-              "dl0", "dl1", "e0", "e1", "e2", "l0", "l1", "l2"]
+SEMAPHORES = ["kv", "ks", "kt", "kg", "dp", "dx0", "dx1", "dx2", "dx3", "da0", "da1", "dw", "dv",
+              "dl0", "dl1", "e0", "e1", "e2", "l0", "l1", "l2", "dy0", "dy1", "dy2"]
 
 
 def _mask(es):
@@ -69,14 +69,15 @@ def _plan(core, cores, topo):
     return plan
 
 
+def _alone(core, cores, topo):
+    return all(topo.chip(d) == topo.chip(core) for d in cores[cores.index(core) + 1:])
+
+
 def _plan0(core, cores, topo):
     ch = topo.chip(core)
     eo = [topo.engines(core, d) for d in cores if topo.chip(d) != ch][0]
-    return {d: eo if topo.chip(d) != ch else _near(core, d, eo, topo) for d in cores[cores.index(core) + 1:]}
-
-
-def _ahead(core, cores, topo):
-    return all(topo.chip(d) == topo.chip(core) for d in cores[cores.index(core) + 1:])
+    return {d: eo if topo.chip(d) != ch or _alone(core, cores, topo) else _near(core, d, eo, topo)
+            for d in reversed(cores[cores.index(core) + 1:])}
 
 
 def rank_program(g, core, T, topo):
@@ -117,9 +118,9 @@ def rank_program(g, core, T, topo):
         need("s", *w)
         return done(sca.activation(out, in_, AF.Copy), "ks")
 
-    def si(out, in_, bias, scale, w=()):
+    def si(out, in_, bias, scale, func=AF.Identity, w=()):
         need("s", *w)
-        return done(sca.activation(out, in_, AF.Identity, bias, scale), "ks")
+        return done(sca.activation(out, in_, func, bias, scale), "ks")
 
     tt, cp, ms, rd, scn, tr, qz = (vec.tensor_tensor, vec.tensor_copy, vec.memset, vec.tensor_reduce,
                                    vec.tensor_tensor_scan, vec.transpose, vec.quantize_mx)
@@ -127,67 +128,61 @@ def rank_program(g, core, T, topo):
     def load(qn, out, in_, sem):
         return done(queue[qn].dma_start(out, in_), sem, 16)
 
-    dx = {}
-    dx[0] = load("y", T.xs[:, 0:512], T.x[:, 0:512], "dx0")
     dp = load("s", T.pt[:, 0:128], T.p[:, 0:128], "dp")
-    dx[2] = load("s", T.xs[:, 1024:1536], T.x[:, 1024:1536], "dx2")
-    dx[1] = load("y", T.xs[:, 512:1024], T.x[:, 512:1024], "dx1")
-    dx[3] = load("s", T.xs[:, 1536:2048], T.x[:, 1536:2048], "dx3")
-    da = [load("s", T.at[:, 0:1024], T.a[:, 0:1024], "da0")]
-    ahead = _ahead(core, cores, topo)
-    if ahead:
-        da.append(load("s", T.at[:, 1024:2048], T.a[:, 1024:2048], "da1"))
-        dv = load("s", T.vt[:], T.v[:], "dv")
-        dw = load("s", T.wt[:], T.w[:], "dw")
+    dx = {i: load("y", T.xs[:, 512 * i:512 * i + 512], T.x[:, 512 * i:512 * i + 512], "dx%d" % i) for i in (0, 2, 1, 3)}
+    da = [load("y", T.at[:, 0:1024], T.a[:, 0:1024], "da0")]
+    alone = _alone(core, cores, topo)
+    if alone:
+        da.append(load("y", T.at[:, 1024:2048], T.a[:, 1024:2048], "da1"))
+        dv = load("y", T.vt[:], T.v[:], "dv")
+        dw = load("y", T.wt[:], T.w[:], "dw")
 
     kpi = io(T.pi[:], [[1, 1]], 0, 1)
-    kj4 = io(T.j4i[:], [[4, 32]], 0, 128)
-    kone = io(T.one[:], [[0, 32]], 1, 0)
+    kone = io(T.one[:], [[0, 64]], 1, 0)
+    kz = io(T.z[:, 24:32], [[0, 8]], 0, 0)
+    kio = io(T.io32[:], [[1, 32]], 0, 0)
     kypi = io(T.ypi[:], [[0, 32], [1, 4]], 0, 0)
-    kprm = io(T.prmi[:], [[1, 8]], 0, 8)
-    kgg = io(T.gg[:], [[0, 64]], 0, 0)
-    io(T.z[:, 24:32], [[0, 8]], 0, 0)
-    kc = io(T.one2[:], [[0, 128]], 1, 0)
-    kval = io(T.vali[:], [[128, 16], [4, 16]], 0, 0)
-    io(T.iw[:], [[0, 32]], 0, 0)
+    kfl0 = io(T.fl[:, 32:64], [[0, 32]], 0, 0)
+    kval = io(T.vali[:], [[128, 8], [1024, 2], [4, 16]], 0, 0)
     kff = io(T.ff[:, 0:ROOM], [[0, ROOM]], 0, 0)
-    if ahead:
-        kff = io(T.lt[:], [[0, 512]], 0, 0)
     c = V(ms, T.reset[:], 0.0)
+    V(ms, T.ss[:, 15:544:16], 0.0)
+    c = V(ms, T.one2[:], 1.0)
     ts(T.pj[:, 0:1], T.pi[:], 31, None, A.bitwise_and, w=(kpi,))
     ts(T.pj[:, 1:2], T.pi[:], 15, None, A.bitwise_and)
     ts(T.pj[:, 2:3], T.pi[:], 3, None, A.bitwise_and)
     c2 = ts(T.pj[:, 3:4], T.pi[:], 2, 3, A.logical_shift_right, A.bitwise_and)
     V(ms, T.reset[:, 0:128:16], -5e29, w=(c,))
+    V(ms, T.ss[:, 47:48], 99.0)
     cpf = V(cp, T.pf[:], T.pj[:], w=(c2,))
-    c = ts(T.j4m[:], T.j4i[:], 4095, None, A.bitwise_and, w=(kj4,))
-    ckr = ts(T.kr[:], T.pf[:, 0:1], 16.0, None, A.is_lt, w=(cpf,))
-    cg = V(tt, T.lane[:], T.pf[:, 0:1], T.pf[:, 1:2], A.subtract)
-    cj4 = V(cp, T.j4[:], T.j4m[:], w=(c,))
-    ts(T.c0[:], T.pf[:, 0:1], 0.0, -1.0, A.is_equal, A.mult)
-    ts(T.c1[:], T.pf[:, 0:1], 17.0, 16.0 / 256, A.is_equal, A.mult)
-    ts(T.c3[:], T.pf[:, 0:1], 17.0, -17.0 / 256, A.is_equal, A.mult)
-    ts(T.c2[:], T.pf[:, 0:1], 16.0, 1.0 / 256, A.is_equal, A.mult)
-    tcol, rho = T.pf[:, 2:3], T.pf[:, 3:4]
-    ts(T.msk[:], T.ypi[:], rho, None, A.is_equal, w=(kypi,))
-    ts(T.d0[:], T.ypi[:], 0.0, None, A.not_equal)
-    c2 = ts(T.prmi[:], T.prmi[:], 127, None, A.bitwise_and, w=(kprm,))
-    V(ms, T.gg[:, 0:1], 99.0, w=(kgg,))
-    V(cp, T.prm[:], T.prmi[:], w=(c2,))
-    turn = 4.0 * ((r + 1) % N) + 4.0 * N * r
-    si(T.th[:], T.pf[:, 2:3], 0.0, 0.5, w=(cpf,))
-    si(T.rst[:, 0:1], T.pf[:, 1:2], -0.25 * turn, -0.25)
-    si(T.rst[:, 1:2], T.pf[:, 1:2], -0.25 * (turn + 16.0), -0.25)
-    need("s", kone, ckr)
-    si(T.kw[:], T.one[:], 0.0, T.kr[:])
-    kg64 = si(T.g64[:], T.lane[:], 0.0, 4.0, w=(cg,))
-    si(T.trash[:], T.j4[:], float(ROOM), 0.25, w=(cj4,))
-    kval = si(T.val[:], T.vali[:], T.g64[:], 1.0, w=(kval, kg64))
+    V(ms, T.ne[:], 0.0)
+    p32, p16, tcol, rho = (T.pf[:, i:i + 1] for i in range(4))
+    ts(T.m0[:], p32, 0.0, -256.0, A.is_equal, A.mult, w=(cpf,))
+    c = ts(T.m31[:], p32, 31.0, -1.0, A.is_equal, A.mult)
+    cg = V(tt, T.lane[:], p32, p16, A.subtract)
+    ts(T.c0[:], p32, 2.0, -1.0, A.is_equal, A.mult)
+    ts(T.one[:, 32:33], p32, 2.0, None, A.is_ge, w=(kone,))
+    ts(T.k0[:], T.m0[:], T.m31[:], -16.0, A.add, A.mult, w=(c,))
 
-    c = V(cp, T.pt[:, 128:256], T.pt[:, 0:128], w=(dp,))
-    V(cp, T.pt[:, 512:576], T.pt[:, 0:64])
-    c = V(cp, T.pt[:, 256:512], T.pt[:, 0:256], w=(c,))
-    kqp = V(qz, T.qp[:], T.sp[:], T.pt[:], w=(c,))
+    kp = sc(T.pt[:, 256:384], T.pt[:, 0:128], w=(dp,))
+    V(cp, T.pt[:, 128:256], T.pt[:, 0:128], w=(dp,))
+    V(cp, T.pt[:, 384:512], T.pt[:, 0:128])
+    c = V(cp, T.pt[:, 512:576], T.pt[:, 0:64])
+    kqp = V(qz, T.qp[:], T.sp[:], T.pt[:], w=(c, kp))
+
+    turn = N * r + N - 1 + (r + 1) % N
+    nb = (turn + 15) // N
+    kpb = si(T.pb[:], p16, 1.0, 8.0, w=(cpf,))
+    si(T.rst[:, 0:1], p16, -1.0 * turn, -0.25)
+    si(T.rst[:, 1:2], p16, -1.0 * turn - 4.0, -0.25)
+    ktb = si(T.tb[:], p32, 0.0, float(GAP))
+    knr = si(T.nrho[:], rho, 0.0, -1.0)
+    kvb = si(T.vb[:], T.lane[:], tcol, 4.0, w=(cg,))
+    ktrash = si(T.trash[:], T.io32[:], T.tb[:], 1.0, w=(kio, ktb))
+    c = si(T.yab[:], T.ypi[:], T.nrho[:], 1.0, AF.Abs, w=(kypi, knr))
+    si(T.d0[:], T.ypi[:], 0.0, 1.0, AF.Sign)
+    si(T.msk[:], T.yab[:], 1.0, -1.0, AF.Relu, w=(c,))
+    kval = si(T.val[:], T.vali[:], T.vb[:], 1.0, w=(kval, kvb))
 
     kqx, ksc, kch = {}, {}, {}
 
@@ -206,42 +201,44 @@ def rank_program(g, core, T, topo):
         if n == 0:
             kch[b] = V(tr, z, T.ps[:, 512 * b:512 * b + 128], w=(ksc[b],))
         elif n == 1:
-            kch[b] = V(scn, T.mx[:, k], before, T.reset[:], 0.0, A.max, A.add, w=(kch[b], kc))
+            kch[b] = V(scn, T.mx[:, k], before, T.reset[:], 0.0, A.max, A.add, w=(kch[b], kz))
         elif n == 2:
             kch[b] = V(tt, T.nn[:, k], z, T.mx[:, k], A.is_le, w=(kch[b],))
         else:
-            kch[b] = V(scn, T.ss[:, k], T.nn[:, k], T.one2[:], 0.0, A.mult, A.add, w=(kch[b],))
+            kch[b] = V(scn, T.ss[:, 64 + 128 * b:192 + 128 * b], T.nn[:, k], T.one2[:], 0.0, A.mult, A.add, w=(kch[b],))
         return kch[b]
 
-    pack(0), pack(2), step(0, 0), step(0, 1), pack(1), pack(3), step(0, 2), step(1, 0), step(0, 3), step(1, 1)
-    V(cp, T.gg[:, 17:18], T.ss[:, 15:16], w=(kch[0],))
+    def slots(first, n, step=1):
+        k = 16 * (first + 4) + 15
+        return T.ss[:, k:k + 16 * step * (n - 1) + 1:16 * step]
+
+    pack(0), pack(2)
+    kprm = ts(T.prm[:], T.io32[:, 0:8], T.pb[:], None, A.add, w=(kpb, kio))
+    pack(1), step(0, 0), step(0, 1), pack(3), step(0, 2), step(1, 0), step(0, 3), step(1, 1)
+    kzf = ts(T.zf[:], slots(0, 1), T.m0[:], T.k0[:], A.mult, A.add, w=(kch[0],))
     step(1, 2)
     c = step(1, 3)
-    for h in (0, 1):
-        V(cp, T.gg[:, 1 + 8 * h:9 + 8 * h], T.ss[:, 16 * h + 15:256:32], w=(c,))
-        c2 = V(cp, T.gg[:, 32 + 8 * h:40 + 8 * h], T.ss[:, 16 * h + 15:256:32])
-    c = V(tr, T.h2[:], T.gg[:], w=(c2,))
+    c2 = V(cp, slots(-1, 1), slots(14, 1), w=(c,))
+    ts(T.fl[:, 32:33], slots(15, 1), T.m31[:], T.zf[:], A.mult, A.add, w=(kzf, kfl0))
+    V(tr, T.h2[:, 32:64], slots(-2, 32), w=(c2,))
+    c = V(tr, T.h2[:, 0:32], slots(-4, 32))
     here, prev = T.h2[:, 32:64], T.h2[:, 31:63]
-    kfl = V(tt, T.fl[:], here, prev, A.not_equal, w=(c,))
-    kz1 = ts(T.z1[:], T.h2[:, 0:1], T.c1[:], T.c3[:], A.mult, A.add)
-    cs = T.cc[:, 0:32]
-    kcs = V(scn, cs, T.one[:], T.fl[:], T.c0[:], A.mult, A.add, w=(kfl,))
-    kz2 = ts(T.z2[:], T.h2[:, 31:32], T.c2[:], T.z1[:], A.mult, A.add, w=(kz1,))
-    c = ts(T.dm[:], T.kw[:], T.cc[:, 31:32], T.z2[:], A.mult, A.add, w=(kz2, kcs, kval))
+    kfl = V(tt, T.fl[:, 0:32], here, prev, A.not_equal, w=(c,))
     knf = V(tt, T.nfe[:], here, prev, A.is_equal)
-    kdm = V(tr, T.dmt[:], T.dm[:], w=(c,))
-    knf = V(tt, T.nfd[:], T.nfe[:], T.trash[:], A.mult, w=(knf,))
-    ken = V(rd, T.enc[:], T.dmt[:], X, A.add, w=(kdm,))
-    ke16 = ts(T.e16[:, 0:1], T.enc[:], 256.0, None, A.mult, w=(ken,))
-    kcx = V(tt, T.cc[:, 32:64], cs, T.nfd[:], A.max, w=(knf,))
-    kfj = V(tt, T.fj[:], T.fl[:], T.j4[:], A.mult)
+    kcs = V(scn, T.cc[:, 32:96], T.one[:], T.fl[:], T.c0[:], A.mult, A.add, w=(kfl,))
+    knf = V(tt, T.nfd[:], T.nfe[:], T.trash[:], A.mult, w=(knf, kval))
+    kdm = V(tr, T.dmt[:], T.cc[:, 64:96], w=(kcs,))
+    kcx = V(tt, T.cc[:, 0:32], T.cc[:, 32:64], T.nfd[:], A.max, w=(knf,))
+    khs = V(rd, T.hs[:], T.dmt[:, 0:18], X, A.add, w=(kdm,))
+    kiw = V(scn, T.iw[:, 2:19:2], T.one[:, 0:9], T.dmt[:, 0:17:2], 128.0, A.mult, A.add)
+    ke16 = ts(T.e16[:, 0:1], T.hs[:], 16.0, T.dmt[:, 31:32], A.mult, A.add, w=(khs,))
 
     arrive = {"e0": 0, "e1": 0, "e2": 0}
     for s in cores:
         if s != core:
             n = sum(len(es) for es in _plan(s, cores, topo)[core])
             arrive["e0"] += len(_plan0(s, cores, topo).get(core, []))
-            arrive["e1"] += n * (2 if _ahead(s, cores, topo) else 1)
+            arrive["e1"] += n
             arrive["e2"] += n
 
     def did(d):
@@ -258,115 +255,95 @@ def rank_program(g, core, T, topo):
                                srcs=[T.e16[:, 0:1]], dsts=[T.m16[:, r:r + 1] for d in ds]) for e, ds in groups.items()],
             local_sem=T.sem.l0)
         cnt["l0"] = sum(len(e) for e in groups)
-    if not ahead:
+    if not alone:
         need("y", ("l0", cnt["l0"]))
         da.append(load("y", T.at[:, 1024:2048], T.a[:, 1024:2048], "da1"))
 
     plan = _plan(core, cores, topo)
 
-    def exchange(codes, plane, first, width, at, rsem, lsem):
-        land = (T.qc, T.sc) if rsem == "e1" else (T.qh, T.sh)
+    def exchange(codes, plane, first, width, rsem, lsem):
         for part in (0, 1):
             tl = []
             for d, es in plan.items():
                 k = first[d]
-                slot = NC + S * (((r - T.rank_of(d)) % N) - 1) + at
+                slot = NC + width * (((r - T.rank_of(d)) % N) - 1)
                 if part == 0:
-                    src, dst = codes[:, k:k + width].bitcast(dt.uint8), land[0][:, slot:slot + width].bitcast(dt.uint8)
+                    src, dst = codes[:, k:k + width].bitcast(dt.uint8), codes[:, slot:slot + width].bitcast(dt.uint8)
                 else:
-                    src, dst = plane[:, k:k + width], land[1][:, slot:slot + width]
+                    src, dst = plane[:, k:k + width], plane[:, slot:slot + width]
                 tl.append(RemoteDMATransfer(dst_ids=[did(d)], dma_engine_mask=_mask(es[part]), remote_sem=T.sem[rsem],
                                             srcs=[src], dsts=[dst]))
                 cnt[lsem] = cnt.get(lsem, 0) + len(es[part])
             g.remote_dma_fused(tl, local_sem=T.sem[lsem])
 
-    V(scn, T.iw[:, 1:17], T.one[:, 0:16], T.dmt[:, 0:16], 0.0, A.mult, A.add, w=(kdm, kff))
-    kiw = V(tr, T.cct[:], T.cc[:], w=(kcx,))
-    klj = V(rd, T.lj[:], T.fj[:], X, A.max, w=(kfj,))
-    kof = V(tt, T.offf[:], T.cct[:, 32:48], T.iw[:, 0:16], A.add, w=(kiw,))
-    klj = ts(T.dm2[:], T.one[:], T.lj[:], None, A.mult, w=(klj,))
-    kof = V(cp, T.offl[:], T.offf[:], w=(kof,))
-    klj = V(tr, T.dm2t[:], T.dm2[:], w=(klj,))
-    if r:
-        V(cp, T.owni[:], T.e16[:, 0:1], w=(ke16,))
-    klj = V(rd, T.last[:], T.dm2t[:, 0:16], X, A.max, w=(klj,))
-    klast = ts(T.lastl[:, 0:1], tcol, T.last[:], None, A.add, w=(klj,))
-    c = V(cp, T.ff[:, 0:FW].indirect(T.offl[:]), T.val[:], w=(kof,))
-    need("s", klast, kff, dx[0], dx[1], dx[2], dx[3])
-    if ahead:
-        klt = sc(T.lt[:, 0:16], T.xs[:, 0:2048].indirect(T.lastl[:, 0:1]))
-        klt = V(qz, T.ql[:], T.sl[:], T.lt[:], w=(klt,))
-        need("g", klt)
-        exchange(T.ql, T.sl, {d: 0 for d in plan}, 2, 16, "e1", "l1")
-    for b in range(N):
-        klb = sc(T.ct[:, 72 * b + 64:72 * b + 80], T.xs[:, 0:2048].indirect(T.lastl[:, 0:1]))
-    c = V(tt, T.mk[:], T.ff[:, 0:128].indirect(T.prm[:, 0:8]), T.msk[:], A.mult, w=(c,))
-    if r:
-        ts(T.fi[:, r:r + 1], T.owni[:], 4, 15, A.logical_shift_right, A.bitwise_and)
+    kct = V(tr, T.cct[:], T.cc[:, 0:64], w=(kcx,))
+    kiw = V(scn, T.iw[:, 3:18:2], T.one[:, 0:8], T.dmt[:, 1:16:2], T.iw[:, 18:19], A.mult, A.add, w=(kiw,))
+    V(cp, T.mi[:, r:r + 1], T.e16[:, 0:1], w=(ke16,))
+    c = V(tt, T.offf[:], T.cct[:, 2:18], T.iw[:, 2:18], A.add, w=(kiw,))
+    c = ts(T.offl[:], T.offf[:], T.hs[:], None, A.subtract, w=(c,))
+    c = V(cp, T.ff[:, 0:FW].indirect(T.offl[:]), T.val[:], w=(c, kff))
+    c = V(tt, T.mk[:], T.ff[:, 0:ROOM].indirect(T.prm[:, 0:8]), T.msk[:], A.mult, w=(c,))
     c = V(scn, T.sg[:], T.d0[:], T.mk[:], 0.0, A.mult, A.add, w=(c,))
-    c = ts(T.u0[:], T.sg[:, 3:128:4], T.th[:], None, A.add, w=(c,))
-    c = V(tr, T.ut[:], T.u0[:], w=(c,))
+    c = V(tr, T.ut[:], T.sg[:, 3:128:4], w=(c,))
     V(tt, T.us[:, 0:16], T.ut[:, 0:16], T.ut[:, 16:32], A.add, w=(c,))
     c = V(tt, T.us[:, 16:32], T.ut[:, 0:16], T.ut[:, 16:32], A.add)
-    kuu = [V(tr, T.uu[:, 0:32], T.us[:], w=(c,))]
-    nb = min(r + 2, N)
-    for b in range(1, nb):
-        if b % 2:
-            kv = V(cp, T.uu[:, 32 * b:32 * b + 32], T.uu[:, 0:32], w=(kuu[0],))
+    V(tr, T.uu[:, 0:32], T.us[:], w=(c,))
+    c = V(tr, T.uu[:, 32:64], T.us[:])
+    kuu = [c]
+    for i, b in enumerate(range(2, nb, 2)):
+        n = 32 * min(2, nb - b)
+        if i % 2:
+            kuu.append(V(cp, T.uu[:, 32 * b:32 * b + n], T.uu[:, 0:n], w=(c,)))
         else:
-            ks = sc(T.uu[:, 32 * b:32 * b + 32], T.uu[:, 0:32], w=(kuu[0],))
-    kuu = [kv] + ([ks] if nb > 2 else [])
+            kuu.append(sc(T.uu[:, 32 * b:32 * b + n], T.uu[:, 0:n], w=(c,)))
 
-    if r == 0:
-        V(ms, T.nf0[:], 0.0)
-        sb = sbb = T.sb[:, 0:1]
-        c = V(ms, sb, 0.0)
-    else:
+    if r:
         need("v", ("e0", arrive["e0"]))
         cnt["e0"] = arrive["e0"]
-        sb, sbb = T.sb[:, r - 1:r], T.sbb[:, r - 1:r]
         c = V(cp, T.mi[:, 0:r], T.m16[:, 0:r])
-        if r > 1:
-            ts(T.fi[:, 1:r], T.mi[:, 1:r], 4, 15, A.logical_shift_right, A.bitwise_and, w=(c,))
-        c = ts(T.la[:, 0:r], T.mi[:, 0:r], 15, None, A.bitwise_and, w=(c,))
-        c2 = ts(T.c7[:, 0:r], T.mi[:, 0:r], 8, 7, A.logical_shift_right, A.bitwise_and)
+        ts(T.fi[:, 0:r + 1], T.mi[:, 0:r + 1], 12, None, A.logical_shift_right, w=(c,))
+        c = ts(T.la[:, 0:r], T.mi[:, 0:r], 15, None, A.bitwise_and)
+    c2 = ts(T.c7[:, 0:r + 1], T.mi[:, 0:r + 1], 4, 7, A.logical_shift_right, A.bitwise_and)
+    if r:
         V(tt, T.ne[:, 0:r], T.fi[:, 1:r + 1], T.la[:, 0:r], A.not_equal, w=(c,))
-        c = V(cp, T.c7f[:, 0:r], T.c7[:, 0:r], w=(c2,))
-        c = V(scn, T.sb[:, 0:r], T.c7f[:, 0:r], T.ne[:, 0:r], 0.0, A.add, A.add, w=(c,))
+    c = V(cp, T.c7f[:, 0:r + 1], T.c7[:, 0:r + 1], w=(c2,))
+    c = V(scn, T.sb[:, 0:r + 1], T.c7f[:, 0:r + 1], T.ne[:, 0:r + 1], 0.0, A.add, A.add, w=(c,))
+    sb, sbb = T.sb[:, r:r + 1], T.sbb[:, r:r + 1]
     c = ts(T.ro[:], T.rst[:], sb, -4.0, A.add, A.mult, w=(c,))
     klst = V(cp, T.lst[:], T.uu[:, 0:32 * nb].indirect(T.ro[:, 0:2]), w=(c, *kuu))
-    need("s", klst, klb)
-    for b in range(5, N):
-        kcs2 = sc(T.ct[:, 72 * b:72 * b + 64], T.xs[:, 0:2048].indirect(T.lst[:, 4 * b:4 * b + 4]))
-    for b in range(0, 5):
-        c = V(cp, T.ct[:, 72 * b:72 * b + 64], T.xs[:, 0:2048].indirect(T.lst[:, 4 * b:4 * b + 4]), w=(klst, klb))
-    kqc = V(qz, T.qc[:, 0:NC], T.sc[:, 0:NC], T.ct[:, 0:4 * NC], w=(c, kcs2))
+    cut = 20
+    kcs2 = sc(T.ct[:, 16 * cut:512], T.xs[:, 0:2048].indirect(T.lst[:, cut:32]), w=(klst, *dx.values()))
+    c = V(cp, T.ct[:, 0:16 * cut], T.xs[:, 0:2048].indirect(T.lst[:, 0:cut]), w=(klst,))
+    kqc = V(qz, T.qc[:, 0:NC], T.sc[:, 0:NC], T.ct[:], w=(c, kcs2))
     need("g", kqc)
-    exchange(T.qc, T.sc, {d: S * ((T.rank_of(d) - r - 1) % N) for d in plan}, 16 if ahead else S, 0, "e1", "l1")
-    if not ahead:
+    exchange(T.qc, T.sc, {d: S * ((T.rank_of(d) - r - 1) % N) for d in plan}, S, "e1", "l1")
+    if not alone:
         need("y", ("l1", cnt["l1"]))
         dv = load("y", T.vt[:], T.v[:], "dv")
         dw = load("y", T.wt[:], T.w[:], "dw")
 
     kqa = {}
+    c0 = V(ms, T.tcs[:], 0.0)
     for i in range(4):
         kqa[i] = V(qz, T.qa[:, 128 * i:128 * i + 128], T.sa[:, 128 * i:128 * i + 128], T.at[:, 512 * i:512 * i + 512],
                    w=(da[i // 2],))
-    kcd = V(tt, T.tcs[:], T.cct[:, 0:32], T.iw[:], A.add)
-    if r:
-        c = ts(T.ci[:, 0:r], T.mi[:, 0:r], 8, None, A.logical_shift_right)
-        V(tt, T.nf0[:], T.fi[:, r:r + 1], T.la[:, r - 1:r], A.is_equal)
+    c = ts(T.ci[:, 0:r + 1], T.mi[:, 0:r + 1], 4, 255, A.logical_shift_right, A.bitwise_and)
+    for h in (0, 1):
+        V(tt, T.tcs[:, 8 * h:8 * h + 8], T.cct[:, 34 + h:50:2], T.iw[:, 2 + h:18:2], A.add, w=(c0,))
+        kcd = ts(T.tcs[:, 32 + 8 * h:40 + 8 * h], slots(h, 8, 2), -1.0, 16.0, A.mult, A.add)
+    c = V(cp, T.cif[:, 0:r + 1], T.ci[:, 0:r + 1], w=(c,))
     kcd = V(tr, T.cdw[:], T.tcs[:], w=(kcd,))
+    c = V(scn, T.sbb[:, 0:r + 1], T.cif[:, 0:r + 1], T.ne[:, 0:r + 1], -128.0, A.add, A.add, w=(c,))
     if r:
-        c = V(cp, T.cif[:, 0:r], T.ci[:, 0:r], w=(c,))
-    ts(T.lb0[:], here, -1.0, 16.0, A.mult, A.add)
-    if r:
-        c = V(scn, T.sbb[:, 0:r], T.cif[:, 0:r], T.ne[:, 0:r], 0.0, A.add, A.add, w=(c,))
+        ts(T.nx[:], T.ne[:, r - 1:r], 200.0, T.cif[:, r:r + 1], A.mult, A.add)
+    else:
+        V(ms, T.nx[:], 999.0)
     for i in range(4):
-        kcp = V(cp, T.cd[:, 16 * i:16 * i + 16], T.cdw[:, 16 * (i // 2):16 * (i // 2) + 16], w=(kcd,))
-    klb1 = ts(T.lb1[:], T.cdw[:], sbb, None, A.add, w=(c,))
+        kcp = ts(T.cd[:, 16 * i:16 * i + 16], T.cdw[:, 16 * (i // 2):16 * (i // 2) + 16], T.hs[:], None, A.subtract,
+                 w=(kcd,))
+    klb1 = ts(T.lb1[:], T.cdw[:, 0:32], T.hs[:], sbb, A.subtract, A.add, w=(c,))
     need("y", klb1)
-    done(syn.dma_start(T.lb[0:1, :], T.lb0[0:16, :]), "dl0", 16)
+    done(syn.dma_start(T.lb[0:1, :], T.cdw[0:16, 32:64]), "dl0", 16)
     done(syn.dma_start(T.lb[1:2, :], T.lb1[0:16, :]), "dl1", 16)
 
     need("t", ("e1", arrive["e1"]), kqc)
@@ -376,47 +353,47 @@ def rank_program(g, core, T, topo):
         need("t", kqa[i])
         o = T.ps[:, 2048 + 512 * i:2048 + 512 * i + NC]
         m = done(ten.matmul_mx(o, T.qa[:, 128 * i:128 * i + 128], T.sa[:, 128 * i:128 * i + 128],
-                               T.qc[:, NC - S:NC + 126], T.sc[:, NC - S:NC + 126], True, True), "kt")
+                               T.qc[:, NC - S:2 * NC - S], T.sc[:, NC - S:2 * NC - S], True, True), "kt")
         if i % 2 == 0:
             need("s", m)
-            kh.append(done(sca.activation(T.ht[:, i:576:4], o, AF.Relu, 0.0, 0.05), "ks"))
+            kh.append(done(sca.activation(T.ht[:, i:512:4], o, AF.Relu, 0.0, 0.05), "ks"))
         else:
-            kh.append(ts(T.ht[:, i:576:4], o, 0.0, 0.05, A.max, A.mult, w=(m,)))
+            kh.append(ts(T.ht[:, i:512:4], o, 0.0, 0.05, A.max, A.mult, w=(m,)))
     kqh = V(qz, T.qh[:, 0:NC], T.sh[:, 0:NC], T.ht[:], w=kh)
     need("g", kqh)
-    exchange(T.qh, T.sh, {d: S * ((T.rank_of(d) - r) % N) - 1 for d in plan}, S, 0, "e2", "l2")
+    exchange(T.qh, T.sh, {d: S * ((T.rank_of(d) - r) % N) - 2 for d in plan}, S2, "e2", "l2")
 
     c = V(tr, T.tc[:], T.cd[:], w=(kcp,))
-    ts(T.ii[:], T.tc[:], 0.125, -0.4375, A.mult, A.add, w=(c,))
+    ts(T.ii[:], T.tc[:], 0.125, 0.4375, A.mult, A.add, w=(c,))
     c = ts(T.t1[:], T.tc[:], sb, float(N - r), A.add, A.add)
-    ts(T.fx[:], T.tc[:], 0.0, T.nf0[:], A.is_equal, A.mult)
+    c2 = ts(T.fx[:], T.tc[:], T.nx[:], 128.0, A.add, A.not_equal)
     c = ts(T.kk[:], T.t1[:], 7, None, A.bitwise_and, w=(c,))
     kqv = V(qz, T.qv[:], T.sv[:], T.vt[:], w=(dv,))
     need("t", kqh, kqv)
     m = done(ten.matmul_mx(T.ps[:, 1536:1536 + NC], T.qv[:], T.sv[:], T.qh[:, 0:NC], T.sh[:, 0:NC], True, True), "kt")
-    c = ts(T.k18[:], T.kk[:], float(S), 1.0, A.mult, A.add, w=(c,))
+    c = ts(T.k18[:], T.kk[:], float(S2), 1.0, A.mult, A.add, w=(c,))
+    c2 = V(tt, T.s1[:], T.ii[:], T.fx[:], A.mult, w=(c2,))
     kqw = V(qz, T.qw[:], T.sw[:], T.wt[:], w=(dw,))
     need("t", kqw, *kqx.values())
     kwx = done(ten.matmul_mx(T.ps[:, 1024:1536], T.qw[:], T.sw[:], T.qx[:], T.sx[:], True, True), "kt")
     kwxs = sc(T.wx[:], T.ps[:, 1024:1536], w=(kwx,))
-    c = V(tt, T.s1[:], T.k18[:], T.ii[:], A.add, w=(c,))
-    V(cp, T.vw[:, 0:1], T.ps[:, 1536 + NC - 2:1536 + NC - 1], w=(m,))
-    c = V(tt, T.s2[:], T.s1[:], T.fx[:], A.subtract, w=(c,))
-    V(cp, T.vw[:, 1:S], T.ps[:, 1536:1536 + S - 1])
+    c = V(tt, T.s2[:], T.s1[:], T.k18[:], A.add, w=(c, c2))
+    V(cp, T.vw[:, 0:2], T.ps[:, 1536 + NC - 2:1536 + NC], w=(m,))
+    V(cp, T.vw[:, 2:S2], T.ps[:, 1536:1536 + S])
     V(cp, T.fin[:, 0:32:2], T.s2[:, 0:16], w=(c,))
     kfin = V(cp, T.fin[:, 1:32:2], T.s2[:, 32:48])
 
     need("t", ("e2", arrive["e2"]))
     cnt["e2"] = arrive["e2"]
     m = done(ten.matmul_mx(T.ps[:, 0:128], T.qv[:], T.sv[:], T.qh[:, NC - 2:NC + 126], T.sh[:, NC - 2:NC + 126], True, True), "kt")
-    c = V(cp, T.vw[:, S:NC], T.ps[:, 2:128], w=(m,))
+    c = V(cp, T.vw[:, S2:N * S2], T.ps[:, 2:128], w=(m,))
     for h, (k, e) in enumerate(((0, 128), (128, 320), (320, 512))):
-        c = V(tt, T.yt[:, k:e], T.vw[:, 0:NC].indirect(T.fin[:, k // 16:e // 16]), T.wx[:, k:e], A.add,
+        c = V(tt, T.yt[:, k:e], T.vw[:, 0:N * S2].indirect(T.fin[:, k // 16:e // 16]), T.wx[:, k:e], A.add,
               w=(c, kwxs, kfin) if h == 0 else ())
         qn = "ysy"[h]
         need(qn, c)
         done(queue[qn].dma_start(T.y[:, k:e], T.yt[:, k:e]), "dy%d" % h, 16)
 
     for s in SEMAPHORES:
-        if cnt.get(s):
+        if cnt.get(s) and all(known.get((qn, s), 0) < cnt[s] for qn in queue):
             need("g", (s, cnt[s]))

@@ -22,14 +22,14 @@ SCRATCH = {
     "xs": _sb(2048, BF), "pt": _sb(576, BF), "at": _sb(2048, BF), "wt": _sb(512, BF), "vt": _sb(512, BF),
     "qx": _sb(512, C8), "sx": _sb(512, U8), "qp": _sb(144, C8), "sp": _sb(144, U8),
     "qa": _sb(512, C8), "sa": _sb(512, U8), "qw": _sb(128, C8), "sw": _sb(128, U8), "qv": _sb(128, C8), "sv": _sb(128, U8),
-    "ct": _sb(512, BF), "qc": _sb(NC + 112, C8), "sc": _sb(NC + 112, U8),
+    "ct": _sb(1024, BF), "qc": _sb(2 * NC + 112, C8), "sc": _sb(2 * NC + 112, U8),
     "ht": _sb(512, BF), "qh": _sb(NC + 126, C8), "sh": _sb(NC + 126, U8),
     "pi": _sb(1, I32), "pj": _sb(4, I32), "pf": _sb(4, F32), "io32": _sb(32, F32), "trash": _sb(32, F32),
     "vali": _sb(256, F32), "val": _sb(256, F32), "prm": _sb(8, U16), "ypi": _sb(128, F32), "yab": _sb(128, F32),
     "msk": _sb(128, F32), "d0": _sb(128, F32), "c0": _sb(1, F32), "m0": _sb(1, F32), "m31": _sb(1, F32), "k0": _sb(1, F32),
     "lane": _sb(1, F32), "vb": _sb(1, F32), "tb": _sb(1, F32), "pb": _sb(1, F32), "nrho": _sb(1, F32),
     "rst": _sb(2, F32), "reset": _sb(128, F32), "one2": _sb(128, BF), "one": _sb(64, F32),
-    "z": _sb(288, F32), "mx": _sb(256, F32), "nn": _sb(256, BF), "ss": _sb(544, BF), "h2": _sb(64, BF),
+    "z": _sb(320, F32), "mx": _sb(256, F32), "nn": _sb(256, BF), "ss": _sb(544, BF), "h2": _sb(64, BF),
     "fl": _sb(64, F32), "cc": _sb(96, F32), "cct": _sb(64, F32), "zf": _sb(1, F32), "dmt": _sb(32, F32),
     "hs": _sb(1, F32), "e16": _sb(2, U16), "iw": _sb(20, F32), "nfe": _sb(32, F32), "nfd": _sb(32, F32),
     "offf": _sb(16, F32), "offl": _sb(16, U16), "ff": _sb(FW, F32),
@@ -69,15 +69,34 @@ def _plan(core, cores, topo):
     return plan
 
 
+def _halves(core, cores, topo):
+    r = cores.index(core)
+    order = cores[r + 1:] + cores[:r]
+    off = [d for d in order if topo.chip(d) != topo.chip(core)]
+    eo = topo.engines(core, off[0])
+    halves = []
+    for h in (0, 1):
+        a, b = eo[h::2], eo[1 - h::2]
+        plan = dict(zip(off[3 * h:3 * h + 3], ((a[:2], b[:2]), (a[2:], b[2:]), (b, a))))
+        halves.append({d: plan.get(d) or (_near(core, d, eo, topo),) * 2 for d in order
+                       if d in plan or (h and d not in off)})
+    return halves
+
+
 def _alone(core, cores, topo):
     return all(topo.chip(d) == topo.chip(core) for d in cores[cores.index(core) + 1:])
+
+
+def _beside(core, cores, topo):
+    return any(topo.chip(d) == topo.chip(core) for d in cores[cores.index(core) + 1:])
 
 
 def _plan0(core, cores, topo):
     ch = topo.chip(core)
     eo = [topo.engines(core, d) for d in cores if topo.chip(d) != ch][0]
-    return {d: eo if topo.chip(d) != ch or _alone(core, cores, topo) else _near(core, d, eo, topo)
-            for d in reversed(cores[cores.index(core) + 1:])}
+    later = cores[cores.index(core) + 1:]
+    later.sort(key=lambda d: (not _alone(d, cores, topo), _beside(d, cores, topo), -cores.index(d)))
+    return {d: eo if topo.chip(d) != ch or _alone(core, cores, topo) else _near(core, d, eo, topo) for d in later}
 
 
 def rank_program(g, core, T, topo):
@@ -125,21 +144,23 @@ def rank_program(g, core, T, topo):
     tt, cp, ms, rd, scn, tr, qz = (vec.tensor_tensor, vec.tensor_copy, vec.memset, vec.tensor_reduce,
                                    vec.tensor_tensor_scan, vec.transpose, vec.quantize_mx)
 
+    def vc(out, in_, w=()):
+        return V(cp, out, in_, w=w)
+
     def load(qn, out, in_, sem):
         return done(queue[qn].dma_start(out, in_), sem, 16)
 
     dp = load("s", T.pt[:, 0:128], T.p[:, 0:128], "dp")
-    dx = {i: load("y", T.xs[:, 512 * i:512 * i + 512], T.x[:, 512 * i:512 * i + 512], "dx%d" % i) for i in (0, 2, 1, 3)}
+    dx = {i: load("y", T.xs[:, 512 * i:512 * i + 512], T.x[:, 512 * i:512 * i + 512], "dx%d" % i) for i in (1, 3, 0, 2)}
     da = [load("y", T.at[:, 0:1024], T.a[:, 0:1024], "da0")]
-    alone = _alone(core, cores, topo)
-    if alone:
+    dw = load("y", T.wt[:], T.w[:], "dw")
+    dv = load("y", T.vt[:], T.v[:], "dv")
+    if r == N - 1:
         da.append(load("y", T.at[:, 1024:2048], T.a[:, 1024:2048], "da1"))
-        dv = load("y", T.vt[:], T.v[:], "dv")
-        dw = load("y", T.wt[:], T.w[:], "dw")
 
     kpi = io(T.pi[:], [[1, 1]], 0, 1)
     kone = io(T.one[:], [[0, 64]], 1, 0)
-    kz = io(T.z[:, 24:32], [[0, 8]], 0, 0)
+    kz = io(T.z[:, 31:192:160], [[0, 2]], 0, 0)
     kio = io(T.io32[:], [[1, 32]], 0, 0)
     kypi = io(T.ypi[:], [[0, 32], [1, 4]], 0, 0)
     kfl0 = io(T.fl[:, 32:64], [[0, 32]], 0, 0)
@@ -195,51 +216,61 @@ def rank_program(g, core, T, topo):
                                     T.sp[:, 16 * h:16 * h + 128], T.qx[:, 128 * i:128 * i + 128],
                                     T.sx[:, 128 * i:128 * i + 128], h == 0, h == 1), "kt")
 
-    def step(b, n):
-        k = slice(128 * b, 128 * b + 128)
-        z, before = T.z[:, 32 + 128 * b:160 + 128 * b], T.z[:, 31 + 128 * b:159 + 128 * b]
+    def step(b, n, a=0, e=128):
+        k = slice(128 * b + a, 128 * b + e)
+        z, before = T.z[:, 32 + 160 * b + a:32 + 160 * b + e], T.z[:, 31 + 160 * b + a:31 + 160 * b + e]
         if n == 0:
-            kch[b] = V(tr, z, T.ps[:, 512 * b:512 * b + 128], w=(ksc[b],))
+            c = V(tr, z, T.ps[:, 512 * b + a:512 * b + e], w=(ksc[b],))
         elif n == 1:
-            kch[b] = V(scn, T.mx[:, k], before, T.reset[:], 0.0, A.max, A.add, w=(kch[b], kz))
+            c = V(scn, T.mx[:, k], before, T.reset[:, a:e], 0.0, A.max, A.add, w=(kch[b, a], kz))
         elif n == 2:
-            kch[b] = V(tt, T.nn[:, k], z, T.mx[:, k], A.is_le, w=(kch[b],))
+            c = V(tt, T.nn[:, k], z, T.mx[:, k], A.is_le, w=(kch[b, a],))
         else:
-            kch[b] = V(scn, T.ss[:, 64 + 128 * b:192 + 128 * b], T.nn[:, k], T.one2[:], 0.0, A.mult, A.add, w=(kch[b],))
-        return kch[b]
+            c = V(scn, T.ss[:, 64 + k.start:64 + k.stop], T.nn[:, k], T.one2[:, a:e], 0.0, A.mult, A.add, w=(kch[b, a],))
+        kch[b, a] = c
+        return c
+
+    def both(n):
+        step(0, n, 0, 64)
+        return step(0, n, 64, 128)
 
     def slots(first, n, step=1):
         k = 16 * (first + 4) + 15
         return T.ss[:, k:k + 16 * step * (n - 1) + 1:16 * step]
 
-    pack(0), pack(2)
-    kprm = ts(T.prm[:], T.io32[:, 0:8], T.pb[:], None, A.add, w=(kpb, kio))
-    pack(1), step(0, 0), step(0, 1), pack(3), step(0, 2), step(1, 0), step(0, 3), step(1, 1)
-    kzf = ts(T.zf[:], slots(0, 1), T.m0[:], T.k0[:], A.mult, A.add, w=(kch[0],))
-    step(1, 2)
-    c = step(1, 3)
-    c2 = V(cp, slots(-1, 1), slots(14, 1), w=(c,))
-    ts(T.fl[:, 32:33], slots(15, 1), T.m31[:], T.zf[:], A.mult, A.add, w=(kzf, kfl0))
-    V(tr, T.h2[:, 32:64], slots(-2, 32), w=(c2,))
+    pack(1), pack(3), pack(0), step(1, 0), pack(2), step(1, 1)
+    ts(T.prm[:], T.io32[:, 0:8], T.pb[:], None, A.add, w=(kpb, kio))
+    step(1, 2), both(0), step(1, 3), both(1)
+    kzf = ts(T.zf[:], slots(15, 1), T.m31[:], T.k0[:], A.mult, A.add, w=(kch[1, 0],))
+    V(cp, slots(-1, 1), slots(14, 1))
+    both(2)
+    c = both(3)
+    V(tr, T.h2[:, 32:64], slots(-2, 32), w=(c,))
     c = V(tr, T.h2[:, 0:32], slots(-4, 32))
+    ts(T.fl[:, 32:33], slots(0, 1), T.m0[:], T.zf[:], A.mult, A.add, w=(kzf, kfl0))
     here, prev = T.h2[:, 32:64], T.h2[:, 31:63]
-    kfl = V(tt, T.fl[:, 0:32], here, prev, A.not_equal, w=(c,))
-    knf = V(tt, T.nfe[:], here, prev, A.is_equal)
-    kcs = V(scn, T.cc[:, 32:96], T.one[:], T.fl[:], T.c0[:], A.mult, A.add, w=(kfl,))
-    knf = V(tt, T.nfd[:], T.nfe[:], T.trash[:], A.mult, w=(knf, kval))
-    kdm = V(tr, T.dmt[:], T.cc[:, 64:96], w=(kcs,))
-    kcx = V(tt, T.cc[:, 0:32], T.cc[:, 32:64], T.nfd[:], A.max, w=(knf,))
-    khs = V(rd, T.hs[:], T.dmt[:, 0:18], X, A.add, w=(kdm,))
-    kiw = V(scn, T.iw[:, 2:19:2], T.one[:, 0:9], T.dmt[:, 0:17:2], 128.0, A.mult, A.add)
-    ke16 = ts(T.e16[:, 0:1], T.hs[:], 16.0, T.dmt[:, 31:32], A.mult, A.add, w=(khs,))
+    k = {}
+    chain = [
+        lambda: k.update(fl=V(tt, T.fl[:, 0:32], here, prev, A.not_equal, w=(c,))),
+        lambda: k.update(cs=V(scn, T.cc[:, 32:96], T.one[:], T.fl[:], T.c0[:], A.mult, A.add, w=(k["fl"],))),
+        lambda: k.update(dm=V(tr, T.dmt[:], T.cc[:, 64:96], w=(k["cs"],))),
+        lambda: k.update(hs=V(rd, T.hs[:], T.dmt[:, 0:18], X, A.add, w=(k["dm"],))),
+        lambda: k.update(e16=ts(T.e16[:, 0:1], T.hs[:], 16.0, T.dmt[:, 31:32], A.mult, A.add, w=(k["hs"],)))]
+    beside = [
+        lambda: k.update(nf=V(tt, T.nfe[:], here, prev, A.is_equal, w=(c,))),
+        lambda: k.update(nf=V(tt, T.nfd[:], T.nfe[:], T.trash[:], A.mult, w=(k["nf"], kval))),
+        lambda: k.update(cx=V(tt, T.cc[:, 0:32], T.cc[:, 32:64], T.nfd[:], A.max, w=(k["nf"],))),
+        lambda: k.update(iw=V(scn, T.iw[:, 2:19:2], T.one[:, 0:9], T.dmt[:, 0:17:2], 128.0, A.mult, A.add))]
+    for f in [f for pair in zip(chain, beside) for f in pair] + chain[-1:]:
+        f()
+    ke16, kcx, kiw = k["e16"], k["cx"], k["iw"]
 
     arrive = {"e0": 0, "e1": 0, "e2": 0}
     for s in cores:
         if s != core:
-            n = sum(len(es) for es in _plan(s, cores, topo)[core])
             arrive["e0"] += len(_plan0(s, cores, topo).get(core, []))
-            arrive["e1"] += n
-            arrive["e2"] += n
+            arrive["e1"] += sum(len(es) for half in _halves(s, cores, topo) for es in half.get(core, ()))
+            arrive["e2"] += sum(len(es) for es in _plan(s, cores, topo)[core])
 
     def did(d):
         rid, pid, _ = topo.addr(d)
@@ -250,23 +281,22 @@ def rank_program(g, core, T, topo):
         groups.setdefault(tuple(e), []).append(d)
     if groups:
         need("g", ke16)
-        g.remote_dma_fused(
-            [RemoteDMATransfer(dst_ids=[did(d) for d in ds], dma_engine_mask=_mask(e), remote_sem=T.sem.e0,
-                               srcs=[T.e16[:, 0:1]], dsts=[T.m16[:, r:r + 1] for d in ds]) for e, ds in groups.items()],
-            local_sem=T.sem.l0)
+        tl = [RemoteDMATransfer(dst_ids=[did(d) for d in ds], dma_engine_mask=_mask(e), remote_sem=T.sem.e0,
+                                srcs=[T.e16[:, 0:1]], dsts=[T.m16[:, r:r + 1] for d in ds]) for e, ds in groups.items()]
+        for part in ([tl[:1], tl[1:]] if r == 0 else [tl]):
+            g.remote_dma_fused(part, local_sem=T.sem.l0)
         cnt["l0"] = sum(len(e) for e in groups)
-    if not alone:
         need("y", ("l0", cnt["l0"]))
         da.append(load("y", T.at[:, 1024:2048], T.a[:, 1024:2048], "da1"))
 
-    plan = _plan(core, cores, topo)
+    kct0 = io(T.ct[:, 192:704], [[0, 512]], 0, 0)
 
-    def exchange(codes, plane, first, width, rsem, lsem):
+    def exchange(plan, codes, plane, first, width, land, rsem, lsem):
         for part in (0, 1):
             tl = []
             for d, es in plan.items():
                 k = first[d]
-                slot = NC + width * (((r - T.rank_of(d)) % N) - 1)
+                slot = land + width * (((r - T.rank_of(d)) % N) - 1)
                 if part == 0:
                     src, dst = codes[:, k:k + width].bitcast(dt.uint8), codes[:, slot:slot + width].bitcast(dt.uint8)
                 else:
@@ -284,44 +314,58 @@ def rank_program(g, core, T, topo):
     c = V(cp, T.ff[:, 0:FW].indirect(T.offl[:]), T.val[:], w=(c, kff))
     c = V(tt, T.mk[:], T.ff[:, 0:ROOM].indirect(T.prm[:, 0:8]), T.msk[:], A.mult, w=(c,))
     c = V(scn, T.sg[:], T.d0[:], T.mk[:], 0.0, A.mult, A.add, w=(c,))
-    c = V(tr, T.ut[:], T.sg[:, 3:128:4], w=(c,))
-    V(tt, T.us[:, 0:16], T.ut[:, 0:16], T.ut[:, 16:32], A.add, w=(c,))
-    c = V(tt, T.us[:, 16:32], T.ut[:, 0:16], T.ut[:, 16:32], A.add)
-    V(tr, T.uu[:, 0:32], T.us[:], w=(c,))
-    c = V(tr, T.uu[:, 32:64], T.us[:])
-    kuu = [c]
-    for i, b in enumerate(range(2, nb, 2)):
-        n = 32 * min(2, nb - b)
-        if i % 2:
-            kuu.append(V(cp, T.uu[:, 32 * b:32 * b + n], T.uu[:, 0:n], w=(c,)))
-        else:
-            kuu.append(sc(T.uu[:, 32 * b:32 * b + n], T.uu[:, 0:n], w=(c,)))
 
+    u = c
     if r:
         need("v", ("e0", arrive["e0"]))
         cnt["e0"] = arrive["e0"]
         c = V(cp, T.mi[:, 0:r], T.m16[:, 0:r])
-        ts(T.fi[:, 0:r + 1], T.mi[:, 0:r + 1], 12, None, A.logical_shift_right, w=(c,))
-        c = ts(T.la[:, 0:r], T.mi[:, 0:r], 15, None, A.bitwise_and)
-    c2 = ts(T.c7[:, 0:r + 1], T.mi[:, 0:r + 1], 4, 7, A.logical_shift_right, A.bitwise_and)
+    u = V(tr, T.ut[:], T.sg[:, 3:128:4], w=(u,))
+    c2 = ts(T.c7[:, 0:r + 1], T.mi[:, 0:r + 1], 4, 7, A.logical_shift_right, A.bitwise_and, w=(c,))
     if r:
-        V(tt, T.ne[:, 0:r], T.fi[:, 1:r + 1], T.la[:, 0:r], A.not_equal, w=(c,))
+        ts(T.fi[:, 0:r + 1], T.mi[:, 0:r + 1], 12, None, A.logical_shift_right)
+        c3 = ts(T.la[:, 0:r], T.mi[:, 0:r], 15, None, A.bitwise_and)
+    V(tt, T.us[:, 0:16], T.ut[:, 0:16], T.ut[:, 16:32], A.add, w=(u,))
+    u = V(tt, T.us[:, 16:32], T.ut[:, 0:16], T.ut[:, 16:32], A.add)
     c = V(cp, T.c7f[:, 0:r + 1], T.c7[:, 0:r + 1], w=(c2,))
+    if r:
+        c = V(tt, T.ne[:, 0:r], T.fi[:, 1:r + 1], T.la[:, 0:r], A.not_equal, w=(c3,))
+    nt = max(2, (nb + 2) // 3)
+    for b in range(nt):
+        u2 = V(tr, T.uu[:, 32 * b:32 * b + 32], T.us[:], w=(u,))
     c = V(scn, T.sb[:, 0:r + 1], T.c7f[:, 0:r + 1], T.ne[:, 0:r + 1], 0.0, A.add, A.add, w=(c,))
     sb, sbb = T.sb[:, r:r + 1], T.sbb[:, r:r + 1]
+    kuu = [u2] + [f(T.uu[:, 32 * b:32 * min(b + nt, nb)], T.uu[:, 0:32 * min(nt, nb - b)], w=(u2,))
+                  for f, b in zip((sc, vc), range(nt, nb, nt))]
     c = ts(T.ro[:], T.rst[:], sb, -4.0, A.add, A.mult, w=(c,))
     klst = V(cp, T.lst[:], T.uu[:, 0:32 * nb].indirect(T.ro[:, 0:2]), w=(c, *kuu))
-    cut = 20
-    kcs2 = sc(T.ct[:, 16 * cut:512], T.xs[:, 0:2048].indirect(T.lst[:, cut:32]), w=(klst, *dx.values()))
-    c = V(cp, T.ct[:, 0:16 * cut], T.xs[:, 0:2048].indirect(T.lst[:, 0:cut]), w=(klst,))
-    kqc = V(qz, T.qc[:, 0:NC], T.sc[:, 0:NC], T.ct[:], w=(c, kcs2))
-    need("g", kqc)
-    exchange(T.qc, T.sc, {d: S * ((T.rank_of(d) - r - 1) % N) for d in plan}, S, "e1", "l1")
-    if not alone:
-        need("y", ("l1", cnt["l1"]))
-        dv = load("y", T.vt[:], T.v[:], "dv")
-        dw = load("y", T.wt[:], T.w[:], "dw")
+    halves = _halves(core, cores, topo)
+    blocks = [(T.rank_of(d) - r - 1) % N for half in halves for d in half] + [N - 1]
+    at = {b: S * i + (0 if i < 3 else NC) for i, b in enumerate(blocks)}
 
+    def pick(f, bs, w):
+        for b in bs:
+            if b - 1 not in bs:
+                n = next(j for j in range(1, N + 1) if b + j not in bs)
+                c = f(T.ct[:, 4 * at[b]:4 * (at[b] + S * n)], T.xs[:, 0:2048].indirect(T.lst[:, 4 * b:4 * (b + n)]), w=w)
+        return c
+
+    ks1 = pick(sc, blocks[2:3], (klst, kct0, *dx.values()))
+    ks2 = pick(sc, blocks[3:5], ())
+    c = pick(vc, blocks[0:2], (klst, kct0))
+    kqc = V(qz, T.qc[:, 0:NC], T.sc[:, 0:NC], T.ct[:, 0:512], w=(c, ks1))
+    need("g", kqc)
+    exchange(halves[0], T.qc, T.sc, {d: at[(T.rank_of(d) - r - 1) % N] for d in halves[0]}, S, 2 * NC, "e1", "l1")
+    c = pick(vc, blocks[5:8], ())
+    kqc = V(qz, T.qc[:, NC:2 * NC], T.sc[:, NC:2 * NC], T.ct[:, 512:1024], w=(c, ks2))
+    need("g", kqc)
+    exchange(halves[1], T.qc, T.sc, {d: at[(T.rank_of(d) - r - 1) % N] for d in halves[1]}, S, 2 * NC, "e1", "l1")
+
+    kqw = V(qz, T.qw[:], T.sw[:], T.wt[:], w=(dw,))
+    need("t", kqw, *kqx.values())
+    kwx = done(ten.matmul_mx(T.ps[:, 1024:1536], T.qw[:], T.sw[:], T.qx[:], T.sx[:], True, True), "kt")
+    kwxs = sc(T.wx[:], T.ps[:, 1024:1536], w=(kwx,))
+    kqv = V(qz, T.qv[:], T.sv[:], T.vt[:], w=(dv,))
     kqa = {}
     c0 = V(ms, T.tcs[:], 0.0)
     for i in range(4):
@@ -353,7 +397,7 @@ def rank_program(g, core, T, topo):
         need("t", kqa[i])
         o = T.ps[:, 2048 + 512 * i:2048 + 512 * i + NC]
         m = done(ten.matmul_mx(o, T.qa[:, 128 * i:128 * i + 128], T.sa[:, 128 * i:128 * i + 128],
-                               T.qc[:, NC - S:2 * NC - S], T.sc[:, NC - S:2 * NC - S], True, True), "kt")
+                               T.qc[:, 2 * NC - S:3 * NC - S], T.sc[:, 2 * NC - S:3 * NC - S], True, True), "kt")
         if i % 2 == 0:
             need("s", m)
             kh.append(done(sca.activation(T.ht[:, i:512:4], o, AF.Relu, 0.0, 0.05), "ks"))
@@ -361,22 +405,18 @@ def rank_program(g, core, T, topo):
             kh.append(ts(T.ht[:, i:512:4], o, 0.0, 0.05, A.max, A.mult, w=(m,)))
     kqh = V(qz, T.qh[:, 0:NC], T.sh[:, 0:NC], T.ht[:], w=kh)
     need("g", kqh)
-    exchange(T.qh, T.sh, {d: S * ((T.rank_of(d) - r) % N) - 2 for d in plan}, S2, "e2", "l2")
+    plan = _plan(core, cores, topo)
+    exchange(plan, T.qh, T.sh, {d: S * ((T.rank_of(d) - r) % N) - 2 for d in plan}, S2, NC, "e2", "l2")
 
     c = V(tr, T.tc[:], T.cd[:], w=(kcp,))
     ts(T.ii[:], T.tc[:], 0.125, 0.4375, A.mult, A.add, w=(c,))
     c = ts(T.t1[:], T.tc[:], sb, float(N - r), A.add, A.add)
     c2 = ts(T.fx[:], T.tc[:], T.nx[:], 128.0, A.add, A.not_equal)
     c = ts(T.kk[:], T.t1[:], 7, None, A.bitwise_and, w=(c,))
-    kqv = V(qz, T.qv[:], T.sv[:], T.vt[:], w=(dv,))
     need("t", kqh, kqv)
     m = done(ten.matmul_mx(T.ps[:, 1536:1536 + NC], T.qv[:], T.sv[:], T.qh[:, 0:NC], T.sh[:, 0:NC], True, True), "kt")
     c = ts(T.k18[:], T.kk[:], float(S2), 1.0, A.mult, A.add, w=(c,))
     c2 = V(tt, T.s1[:], T.ii[:], T.fx[:], A.mult, w=(c2,))
-    kqw = V(qz, T.qw[:], T.sw[:], T.wt[:], w=(dw,))
-    need("t", kqw, *kqx.values())
-    kwx = done(ten.matmul_mx(T.ps[:, 1024:1536], T.qw[:], T.sw[:], T.qx[:], T.sx[:], True, True), "kt")
-    kwxs = sc(T.wx[:], T.ps[:, 1024:1536], w=(kwx,))
     c = V(tt, T.s2[:], T.s1[:], T.k18[:], A.add, w=(c, c2))
     V(cp, T.vw[:, 0:2], T.ps[:, 1536 + NC - 2:1536 + NC], w=(m,))
     V(cp, T.vw[:, 2:S2], T.ps[:, 1536:1536 + S])

@@ -8,6 +8,9 @@ NC = N * S
 ROOM = 136
 GAP = 160
 FW = 19 * GAP
+AHEAD = (1, 4, 3, 3, 3, 3, 4, 4)
+WIDE = (1, 2)
+CUT = 320
 UW = 9 * 32
 
 F32, BF, I32, U16, C8, U8 = "float32", "bfloat16", "int32", "uint16", "float8_e4m3fn_x4", "uint8"
@@ -22,17 +25,17 @@ SCRATCH = {
     "xs": _sb(2048, BF), "pt": _sb(576, BF), "at": _sb(2048, BF), "wt": _sb(512, BF), "vt": _sb(512, BF),
     "qx": _sb(512, C8), "sx": _sb(512, U8), "qp": _sb(144, C8), "sp": _sb(144, U8),
     "qa": _sb(512, C8), "sa": _sb(512, U8), "qw": _sb(128, C8), "sw": _sb(128, U8), "qv": _sb(128, C8), "sv": _sb(128, U8),
-    "ct": _sb(1024, BF), "qc": _sb(2 * NC + 112, C8), "sc": _sb(2 * NC + 112, U8),
-    "ht": _sb(512, BF), "qh": _sb(NC + 126, C8), "sh": _sb(NC + 126, U8),
+    "ct": _sb(832, BF), "qc": _sb(2 * NC + 112, C8), "sc": _sb(2 * NC + 112, U8),
+    "ht": _sb(896, BF), "qh": _sb(2 * NC + 126, C8), "sh": _sb(2 * NC + 126, U8),
     "pi": _sb(1, I32), "pj": _sb(4, I32), "pf": _sb(4, F32), "io32": _sb(32, F32), "trash": _sb(32, F32),
-    "vali": _sb(256, F32), "val": _sb(256, F32), "prm": _sb(8, U16), "ypi": _sb(128, F32), "yab": _sb(128, F32),
+    "vali": _sb(128, F32), "val": _sb(128, F32), "prm": _sb(8, U16), "ypi": _sb(128, F32), "yab": _sb(128, F32),
     "msk": _sb(128, F32), "d0": _sb(128, F32), "c0": _sb(1, F32), "m0": _sb(1, F32), "m31": _sb(1, F32), "k0": _sb(1, F32),
-    "lane": _sb(1, F32), "vb": _sb(1, F32), "tb": _sb(1, F32), "pb": _sb(1, F32), "nrho": _sb(1, F32),
+    "lane": _sb(6, F32), "vb": _sb(1, F32), "uh": _sb(32, F32), "tb": _sb(1, F32), "pb": _sb(4, F32), "nrho": _sb(1, F32),
     "rst": _sb(2, F32), "reset": _sb(128, F32), "one2": _sb(128, BF), "one": _sb(64, F32),
     "z": _sb(320, F32), "mx": _sb(256, F32), "nn": _sb(256, BF), "ss": _sb(544, BF), "h2": _sb(64, BF),
-    "fl": _sb(64, F32), "cc": _sb(96, F32), "cct": _sb(64, F32), "zf": _sb(1, F32), "dmt": _sb(32, F32),
-    "hs": _sb(1, F32), "e16": _sb(2, U16), "iw": _sb(20, F32), "nfe": _sb(32, F32), "nfd": _sb(32, F32),
-    "offf": _sb(16, F32), "offl": _sb(16, U16), "ff": _sb(FW, F32),
+    "fl": _sb(64, F32), "cc": _sb(128, F32), "cct": _sb(96, F32), "zf": _sb(1, F32), "dmt": _sb(65, F32),
+    "hs": _sb(1, F32), "e16": _sb(2, U16), "iw": _sb(25, F32), "nfe": _sb(32, F32), "nfd": _sb(32, F32),
+    "offf": _sb(8, F32), "offl": _sb(8, U16), "ff": _sb(FW, F32),
     "mk": _sb(128, F32), "sg": _sb(128, F32), "ut": _sb(32, F32), "us": _sb(32, F32), "uu": _sb(UW, F32),
     "m16": _sb(8, U16), "mi": _sb(8, I32), "fi": _sb(8, I32), "la": _sb(8, I32), "c7": _sb(8, I32), "c7f": _sb(8, F32),
     "ne": _sb(8, F32), "sb": _sb(8, F32), "ci": _sb(8, I32), "cif": _sb(8, F32), "sbb": _sb(8, F32), "nx": _sb(1, F32),
@@ -40,10 +43,10 @@ SCRATCH = {
     "tcs": _sb(64, F32), "cdw": _sb(64, F32), "cd": _sb(64, F32),
     "tc": _sb(64, F32), "ii": _sb(64, I32), "t1": _sb(64, I32), "kk": _sb(64, I32), "k18": _sb(64, F32), "fx": _sb(64, F32),
     "s1": _sb(64, F32), "s2": _sb(64, F32), "fin": _sb(32, U16), "lb1": _sb(32, F32),
-    "wx": _sb(512, F32), "vw": _sb(N * S2, F32), "yt": _sb(512, F32),
+    "wx": _sb(CUT, F32), "vw": _sb(N * S2, F32), "yt": _sb(512, F32), "yg": _sb(512 - CUT, F32), "nhs": _sb(1, F32),
 }
 SEMAPHORES = ["kv", "ks", "kt", "kg", "dp", "dx0", "dx1", "dx2", "dx3", "da0", "da1", "dw", "dv",
-              "dl0", "dl1", "e0", "e1", "e2", "l0", "l1", "l2", "dy0", "dy1", "dy2"]
+              "dl0", "dl1", "e0", "e10", "e11", "e20", "e21", "l0", "l1", "l2", "dy0", "dy1", "dy2"]
 
 
 def _mask(es):
@@ -51,36 +54,29 @@ def _mask(es):
 
 
 def _near(core, d, off_engines, topo):
-    return [e for e in topo.engines(core, d) if e not in off_engines][:2]
+    return [e for e in topo.engines(core, d) if e not in off_engines][::2]
 
 
-def _plan(core, cores, topo):
-    ch = topo.chip(core)
-    off = [d for d in cores if topo.chip(d) != ch]
-    off.sort(key=lambda d: (0 if topo.mates(ch, topo.chip(d)) else 1 if topo.same_plane(ch, topo.chip(d)) else 2, d))
-    eo = topo.engines(core, off[0])
-    plan = {}
-    for i, d in enumerate(off):
-        j = 4 * (i - 4)
-        plan[d] = ([eo[2 * i]], [eo[2 * i + 1]]) if i < 4 else (eo[j + 1:j + 4:2], eo[j:j + 4:2])
-    for d in cores:
-        if d != core and topo.chip(d) == ch:
-            plan[d] = (_near(core, d, eo, topo),) * 2
-    return plan
-
-
-def _halves(core, cores, topo):
+def _early(core, cores, topo):
     r = cores.index(core)
-    order = cores[r + 1:] + cores[:r]
+    order = [cores[r - i] for i in range(1, len(cores))]
     off = [d for d in order if topo.chip(d) != topo.chip(core)]
-    eo = topo.engines(core, off[0])
-    halves = []
-    for h in (0, 1):
-        a, b = eo[h::2], eo[1 - h::2]
-        plan = dict(zip(off[3 * h:3 * h + 3], ((a[:2], b[:2]), (a[2:], b[2:]), (b, a))))
-        halves.append({d: plan.get(d) or (_near(core, d, eo, topo),) * 2 for d in order
-                       if d in plan or (h and d not in off)})
-    return halves
+    return order[:order.index(off[1 if r == len(cores) - 1 else 3]) + 1]
+
+
+def _parts(core, cores, topo, step):
+    r = cores.index(core)
+    order = [cores[(r + step * i) % len(cores)] for i in range(1, len(cores))]
+    parts = []
+    for first in (True, False):
+        ds = [d for d in order if first == (d in _early(core, cores, topo) if step < 0 else core in _early(d, cores, topo))]
+        off = [d for d in ds if topo.chip(d) != topo.chip(core)]
+        eo = topo.engines(core, off[0])
+        a, b, n = eo[0::2], eo[1::2], len(eo) // len(off)
+        shares = [(a[:2], b[:2]), (a[2:], b[2:]), (b, a)] if len(off) == 3 else [(eo[n * i:][:n],) * 2 for i in range(len(off))]
+        parts.append({d: shares[off.index(d)] if d in off else (_near(core, d, eo, topo)[:2 if first else 4],) * 2
+                      for d in ds})
+    return parts
 
 
 def _alone(core, cores, topo):
@@ -96,7 +92,7 @@ def _plan0(core, cores, topo):
     eo = [topo.engines(core, d) for d in cores if topo.chip(d) != ch][0]
     later = cores[cores.index(core) + 1:]
     later.sort(key=lambda d: (not _alone(d, cores, topo), _beside(d, cores, topo), -cores.index(d)))
-    return {d: eo if topo.chip(d) != ch or _alone(core, cores, topo) else _near(core, d, eo, topo) for d in later}
+    return {d: _near(core, d, eo, topo)[:2] if topo.chip(d) == ch and core == cores[0] else eo for d in later}
 
 
 def rank_program(g, core, T, topo):
@@ -150,24 +146,34 @@ def rank_program(g, core, T, topo):
     def load(qn, out, in_, sem):
         return done(queue[qn].dma_start(out, in_), sem, 16)
 
-    dp = load("s", T.pt[:, 0:128], T.p[:, 0:128], "dp")
+    dp = load("s", T.pt[:, 0:64], T.p[:, 0:64], "dp")
     dx = {i: load("y", T.xs[:, 512 * i:512 * i + 512], T.x[:, 512 * i:512 * i + 512], "dx%d" % i) for i in (1, 3, 0, 2)}
     da = [load("y", T.at[:, 0:1024], T.a[:, 0:1024], "da0")]
     dw = load("y", T.wt[:], T.w[:], "dw")
-    dv = load("y", T.vt[:], T.v[:], "dv")
-    if r == N - 1:
+
+    def later_loads():
         da.append(load("y", T.at[:, 1024:2048], T.a[:, 1024:2048], "da1"))
+        return load("y", T.vt[:], T.v[:], "dv")
+
+    if r == N - 1:
+        dv = later_loads()
 
     kpi = io(T.pi[:], [[1, 1]], 0, 1)
-    kone = io(T.one[:], [[0, 64]], 1, 0)
-    kz = io(T.z[:, 31:192:160], [[0, 2]], 0, 0)
     kio = io(T.io32[:], [[1, 32]], 0, 0)
+    kz = io(T.z[:, 31:192:160], [[0, 2]], 0, 0)
+    io(T.one[:, 1:64], [[0, 63]], 1, 0)
+    kone = io(T.one[:, 0:1], [[0, 1]], -1, 0)
     kypi = io(T.ypi[:], [[0, 32], [1, 4]], 0, 0)
+    io(T.ne[:], [[0, 8]], 0, 0)
+    io(T.dmt[:, 32:33], [[0, 1]], 0, 0)
     kfl0 = io(T.fl[:, 32:64], [[0, 32]], 0, 0)
-    kval = io(T.vali[:], [[128, 8], [1024, 2], [4, 16]], 0, 0)
+    io(T.tcs[:], [[0, 64]], 0, 0)
+    kpp = io(T.lane[:, 4:5], [[0, 1]], 0, 1)
+    kval = io(T.vali[:], [[128, 8], [4, 16]], 512, 0)
     kff = io(T.ff[:, 0:ROOM], [[0, ROOM]], 0, 0)
     c = V(ms, T.reset[:], 0.0)
     V(ms, T.ss[:, 15:544:16], 0.0)
+    kp0 = V(ms, T.pt[:, 64:128], 0.0)
     c = V(ms, T.one2[:], 1.0)
     ts(T.pj[:, 0:1], T.pi[:], 31, None, A.bitwise_and, w=(kpi,))
     ts(T.pj[:, 1:2], T.pi[:], 15, None, A.bitwise_and)
@@ -176,34 +182,36 @@ def rank_program(g, core, T, topo):
     V(ms, T.reset[:, 0:128:16], -5e29, w=(c,))
     V(ms, T.ss[:, 47:48], 99.0)
     cpf = V(cp, T.pf[:], T.pj[:], w=(c2,))
-    V(ms, T.ne[:], 0.0)
     p32, p16, tcol, rho = (T.pf[:, i:i + 1] for i in range(4))
-    ts(T.m0[:], p32, 0.0, -256.0, A.is_equal, A.mult, w=(cpf,))
-    c = ts(T.m31[:], p32, 31.0, -1.0, A.is_equal, A.mult)
-    cg = V(tt, T.lane[:], p32, p16, A.subtract)
-    ts(T.c0[:], p32, 2.0, -1.0, A.is_equal, A.mult)
-    ts(T.one[:, 32:33], p32, 2.0, None, A.is_ge, w=(kone,))
-    ts(T.k0[:], T.m0[:], T.m31[:], -16.0, A.add, A.mult, w=(c,))
 
-    kp = sc(T.pt[:, 256:384], T.pt[:, 0:128], w=(dp,))
+    kp = sc(T.pt[:, 256:384], T.pt[:, 0:128], w=(dp, kp0))
     V(cp, T.pt[:, 128:256], T.pt[:, 0:128], w=(dp,))
     V(cp, T.pt[:, 384:512], T.pt[:, 0:128])
-    c = V(cp, T.pt[:, 512:576], T.pt[:, 0:64])
-    kqp = V(qz, T.qp[:], T.sp[:], T.pt[:], w=(c, kp))
+    kpv = V(cp, T.pt[:, 512:576], T.pt[:, 0:64])
 
     turn = N * r + N - 1 + (r + 1) % N
     nb = (turn + 15) // N
-    kpb = si(T.pb[:], p16, 1.0, 8.0, w=(cpf,))
+    kpb = si(T.pb[:, 0:1], p16, 1.0, 8.0, w=(cpf,))
+    si(T.m0[:], p32, 256.0, -256.0, AF.Relu)
+    c = si(T.m31[:], p32, -30.0, 1.0, AF.Relu)
+    c2 = si(T.pb[:, 1:2], p16, -2.0, 1.0, AF.Abs)
+    c3 = si(T.pb[:, 2:3], p32, -1.5, 1.0, AF.Sign)
+    c = si(T.pb[:, 3:4], T.m0[:], T.m31[:], 1.0, w=(c,))
+    si(T.c0[:], T.pb[:, 1:2], 1.0, -1.0, AF.Relu, w=(c2,))
+    si(T.one[:, 32:33], T.pb[:, 2:3], 0.0, 1.0, AF.Relu, w=(c3, kone))
+    si(T.k0[:], T.pb[:, 3:4], 0.0, -1.0, w=(c,))
     si(T.rst[:, 0:1], p16, -1.0 * turn, -0.25)
     si(T.rst[:, 1:2], p16, -1.0 * turn - 4.0, -0.25)
     ktb = si(T.tb[:], p32, 0.0, float(GAP))
     knr = si(T.nrho[:], rho, 0.0, -1.0)
-    kvb = si(T.vb[:], T.lane[:], tcol, 4.0, w=(cg,))
+    kla = si(T.lane[:, 0:1], p16, tcol, -4.0)
     ktrash = si(T.trash[:], T.io32[:], T.tb[:], 1.0, w=(kio, ktb))
     c = si(T.yab[:], T.ypi[:], T.nrho[:], 1.0, AF.Abs, w=(kypi, knr))
     si(T.d0[:], T.ypi[:], 0.0, 1.0, AF.Sign)
     si(T.msk[:], T.yab[:], 1.0, -1.0, AF.Relu, w=(c,))
-    kval = si(T.val[:], T.vali[:], T.vb[:], 1.0, w=(kval, kvb))
+    si(T.lane[:, 2:3], p32, T.lane[:, 0:1], 4.0, w=(kla,))
+    c = si(T.lane[:, 5:6], T.lane[:, 4:5], -63.5, 1.0, AF.Sign, w=(kpp,))
+    kvb = si(T.vb[:], T.lane[:, 5:6], T.lane[:, 2:3], 512.0, w=(c,))
 
     kqx, ksc, kch = {}, {}, {}
 
@@ -211,7 +219,9 @@ def rank_program(g, core, T, topo):
         b, h = i % 2, i // 2
         kqx[i] = V(qz, T.qx[:, 128 * i:128 * i + 128], T.sx[:, 128 * i:128 * i + 128], T.xs[:, 512 * i:512 * i + 512],
                    w=(dx[i],))
-        need("t", kqp, kqx[i])
+        if "p" not in kch:
+            kch["p"] = V(qz, T.qp[:], T.sp[:], T.pt[:], w=(kpv, kp))
+        need("t", kch["p"], kqx[i])
         ksc[b] = done(ten.matmul_mx(T.ps[:, 512 * b:512 * b + 128], T.qp[:, 16 * h:16 * h + 128],
                                     T.sp[:, 16 * h:16 * h + 128], T.qx[:, 128 * i:128 * i + 128],
                                     T.sx[:, 128 * i:128 * i + 128], h == 0, h == 1), "kt")
@@ -239,200 +249,255 @@ def rank_program(g, core, T, topo):
         return T.ss[:, k:k + 16 * step * (n - 1) + 1:16 * step]
 
     pack(1), pack(3), pack(0), step(1, 0), pack(2), step(1, 1)
-    ts(T.prm[:], T.io32[:, 0:8], T.pb[:], None, A.add, w=(kpb, kio))
-    step(1, 2), both(0), step(1, 3), both(1)
-    kzf = ts(T.zf[:], slots(15, 1), T.m31[:], T.k0[:], A.mult, A.add, w=(kch[1, 0],))
-    V(cp, slots(-1, 1), slots(14, 1))
-    both(2)
-    c = both(3)
-    V(tr, T.h2[:, 32:64], slots(-2, 32), w=(c,))
-    c = V(tr, T.h2[:, 0:32], slots(-4, 32))
-    ts(T.fl[:, 32:33], slots(0, 1), T.m0[:], T.zf[:], A.mult, A.add, w=(kzf, kfl0))
+    ts(T.prm[:], T.io32[:, 0:8], T.pb[:, 0:1], None, A.add, w=(kpb, kio))
+    kch[1, 64] = kch[1, 0]
+    step(1, 2, 0, 64), both(0)
+    kch[1, 0] = step(1, 2, 64, 128)
+    both(1), step(1, 3)
+    kch[0, 0] = both(2)
+    ksl = sc(slots(-1, 1), slots(14, 1), w=(kch[1, 0],))
+    kzf = si(T.zf[:], slots(15, 1), T.k0[:], T.m31[:])
+    c = step(0, 3)
+    kz2 = si(T.fl[:, 32:33], slots(0, 1), T.zf[:], T.m0[:], w=(c, kzf, kfl0))
+    kval = si(T.val[:], T.vali[:], T.vb[:], 1.0, w=(kval, kvb))
+    V(tr, T.h2[:, 0:32], slots(-4, 32), w=(c, ksl))
+    c = V(tr, T.h2[:, 32:64], slots(-2, 32))
     here, prev = T.h2[:, 32:64], T.h2[:, 31:63]
-    k = {}
-    chain = [
-        lambda: k.update(fl=V(tt, T.fl[:, 0:32], here, prev, A.not_equal, w=(c,))),
-        lambda: k.update(cs=V(scn, T.cc[:, 32:96], T.one[:], T.fl[:], T.c0[:], A.mult, A.add, w=(k["fl"],))),
-        lambda: k.update(dm=V(tr, T.dmt[:], T.cc[:, 64:96], w=(k["cs"],))),
-        lambda: k.update(hs=V(rd, T.hs[:], T.dmt[:, 0:18], X, A.add, w=(k["dm"],))),
-        lambda: k.update(e16=ts(T.e16[:, 0:1], T.hs[:], 16.0, T.dmt[:, 31:32], A.mult, A.add, w=(k["hs"],)))]
-    beside = [
-        lambda: k.update(nf=V(tt, T.nfe[:], here, prev, A.is_equal, w=(c,))),
-        lambda: k.update(nf=V(tt, T.nfd[:], T.nfe[:], T.trash[:], A.mult, w=(k["nf"], kval))),
-        lambda: k.update(cx=V(tt, T.cc[:, 0:32], T.cc[:, 32:64], T.nfd[:], A.max, w=(k["nf"],))),
-        lambda: k.update(iw=V(scn, T.iw[:, 2:19:2], T.one[:, 0:9], T.dmt[:, 0:17:2], 128.0, A.mult, A.add))]
-    for f in [f for pair in zip(chain, beside) for f in pair] + chain[-1:]:
-        f()
-    ke16, kcx, kiw = k["e16"], k["cx"], k["iw"]
+    before = [T.iw[:, 0:8], T.iw[:, 17:25]]
+    sb, sbb = T.sb[:, r:r + 1], T.sbb[:, r:r + 1]
+    half = (slice(0, 64), slice(64, 128))
+    nt = max(2, (nb + 2) // 3)
+    mo = 4 - r if r in WIDE else 0
+    mi = T.mi[:, mo:mo + r + 1]
+    k = {"h2": c}
 
-    arrive = {"e0": 0, "e1": 0, "e2": 0}
+    def first_label(out, number, w=()):
+        return ts(out, number, 1.0 / 4096, 0.5 / 4096 - 0.5, A.mult, A.add, w=w)
+
+    def landed():
+        wait("v", "e0")
+        if r in WIDE:
+            if r > 1:
+                ts(T.fi[:, 1:r], T.mi[:, mo + 1:mo + r], 12, None, A.logical_shift_right)
+            return k["own"]
+        c = V(cp, T.mi[:, 0:r], T.m16[:, 0:r])
+        if r > 1:
+            first_label(T.fi[:, 1:r], T.m16[:, 1:r])
+        return c
+
+    def again(f, b):
+        return f(T.uu[:, 32 * b:32 * min(b + nt, nb)], T.uu[:, 0:32 * min(nt, nb - b)], w=(k["uu"],))
+
+    call = {
+        "fl": lambda: V(tt, T.fl[:, 0:32], here, prev, A.not_equal, w=(k["h2"],)),
+        "cs": lambda: V(scn, T.cc[:, 64:128], T.one[:], T.fl[:], T.c0[:], A.mult, A.add, w=(k["fl"], kz2)),
+        "dm": lambda: V(tr, T.dmt[:, 0:32], T.cc[:, 96:128], w=(k["cs"],)),
+        "hs": lambda: V(rd, T.hs[:], T.dmt[:, 0:18], X, A.add, w=(k["dm"],)),
+        "e16": lambda: ts(T.e16[:, 0:1], T.hs[:], 16.0, T.dmt[:, 31:32], A.mult, A.add, w=(k["hs"],)),
+        "nf": lambda: V(tt, T.nfe[:], here, prev, A.is_equal),
+        "nd": lambda: V(tt, T.nfd[:], T.nfe[:], T.trash[:], A.mult, w=(k["nf"], ktrash)),
+        "d2": lambda: V(tr, T.dmt[:, 33:65], T.cc[:, 96:128]),
+        "cx": lambda: V(tt, T.cc[:, 32:64], T.cc[:, 64:96], T.nfd[:], A.max, w=(k["nd"],)),
+        "iw": lambda: V(scn, T.iw[:], T.one[:, 33:58], T.dmt[:, 0:49:2], 128.0, A.mult, A.add, w=(k["d2"],)),
+        "ct": lambda: V(tr, T.cct[:, 0:64], T.cc[:, 32:96], w=(k["cx"],)),
+        "of": lambda: [V(tt, T.offf[p, :], T.cct[p, 2 + h:18:2], T.iw[p, 17 * h:17 * h + 8], A.add, w=(k["ct"], k["iw"]))
+                       for h, p in enumerate(half)][-1],
+        "ol": lambda: ts(T.offl[:], T.offf[:], T.hs[:], None, A.subtract, w=(k["of"],)),
+        "ff": lambda: V(cp, T.ff[:, 0:FW].indirect(T.offl[:]), T.val[:], w=(k["ol"], kff, kval)),
+        "mk": lambda: V(tt, T.mk[:], T.ff[:, 0:ROOM].indirect(T.prm[:, 0:8]), T.msk[:], A.mult, w=(k["ff"],)),
+        "sg": lambda: V(scn, T.sg[:], T.d0[:], T.mk[:], 0.0, A.mult, A.add, w=(k["mk"],)),
+        "uh": lambda: [V(tt, T.uh[p, :], T.sg[0:64, 3:128:4], T.sg[64:128, 3:128:4], A.add, w=(k["sg"],))
+                       for p in half][-1],
+        "ut": lambda: V(tr, T.ut[:], T.uh[:], w=(k["uh"],)),
+        "us": lambda: [V(tt, T.us[:, a:a + 16], T.ut[:, 0:16], T.ut[:, 16:32], A.add, w=(k["ut"],)) for a in (0, 16)][-1],
+        "uu": lambda: [V(tr, T.uu[:, 32 * b:32 * b + 32], T.us[:], w=(k["us"],)) for b in range(nt)][-1],
+        "u2": lambda: again(sc, nt) if nb > nt else k["uu"],
+        "u3": lambda: again(vc, 2 * nt) if nb > 2 * nt else k["uu"],
+        "own": lambda: ts(T.mi[:, mo + r:mo + r + 1], T.hs[:], 16.0, T.dmt[:, 31:32], A.mult, A.add, w=(k["hs"],)),
+        "fo": lambda: ts(T.fi[:, r:r + 1], T.dmt[:, 0:1], 1.0 / 256, None, A.mult),
+        "mi": lambda: landed() if r else k["own"],
+        "la": lambda: ts(T.la[:, 0:r], T.mi[:, mo:mo + r], 15, None, A.bitwise_and, w=(k["mi"],)) if r else k["mi"],
+        "c7": lambda: ts(T.c7[:, 0:r + 1], mi, 4, 7, A.logical_shift_right, A.bitwise_and, w=(k["mi"],)),
+        "ne": lambda: V(tt, T.ne[:, 0:r], T.fi[:, 1:r + 1], T.la[:, 0:r], A.not_equal, w=(k["la"],)) if r else k["la"],
+        "cf": lambda: V(cp, T.c7f[:, 0:r + 1], T.c7[:, 0:r + 1], w=(k["c7"],)),
+        "sb": lambda: V(scn, T.sb[:, 0:r + 1], T.c7f[:, 0:r + 1], T.ne[:, 0:r + 1], 0.0, A.add, A.add, w=(k["cf"],)),
+        "ro": lambda: ts(T.ro[:], T.rst[:], sb, -4.0, A.add, A.mult, w=(k["sb"],)),
+        "lst": lambda: V(cp, T.lst[:], T.uu[:, 0:32 * nb].indirect(T.ro[:, 0:2]), w=(k["ro"], k["u2"], k["u3"])),
+    }
+
+    def run(names):
+        for name in names.split():
+            k[name] = call[name]()
+
+    run("fl nf cs nd dm d2" + (" hs cx e16 own iw ct" if r < 2 else " hs cx e16 iw ct" if r < N - 1 else " cx hs iw ct"))
+
+    arrive = {"e0": 0, "e10": 0, "e11": 0, "e20": 0, "e21": 0}
     for s in cores:
         if s != core:
             arrive["e0"] += len(_plan0(s, cores, topo).get(core, []))
-            arrive["e1"] += sum(len(es) for half in _halves(s, cores, topo) for es in half.get(core, ()))
-            arrive["e2"] += sum(len(es) for es in _plan(s, cores, topo)[core])
+            for name, step in (("e1", -1), ("e2", 1)):
+                for h, part in enumerate(_parts(s, cores, topo, step)):
+                    arrive[name + str(h)] += sum(len(es) for es in part.get(core, ()))
+
+    def wait(qn, sem, *toks):
+        need(qn, (sem, arrive[sem]), *toks)
+        cnt[sem] = arrive[sem]
 
     def did(d):
         rid, pid, _ = topo.addr(d)
         return DstId(rid=rid, pnc=pid)
 
-    groups = {}
-    for d, e in _plan0(core, cores, topo).items():
-        groups.setdefault(tuple(e), []).append(d)
-    if groups:
-        need("g", ke16)
-        tl = [RemoteDMATransfer(dst_ids=[did(d) for d in ds], dma_engine_mask=_mask(e), remote_sem=T.sem.e0,
-                                srcs=[T.e16[:, 0:1]], dsts=[T.m16[:, r:r + 1] for d in ds]) for e, ds in groups.items()]
-        for part in ([tl[:1], tl[1:]] if r == 0 else [tl]):
-            g.remote_dma_fused(part, local_sem=T.sem.l0)
-        cnt["l0"] = sum(len(e) for e in groups)
+    for wide in (False, True):
+        groups = {}
+        for d, e in _plan0(core, cores, topo).items():
+            if (T.rank_of(d) in WIDE) == wide:
+                groups.setdefault(tuple(e), []).append(d)
+        if groups:
+            need("g", k["own" if wide else "e16"])
+            src = T.mi[:, mo + r:mo + r + 1] if wide else T.e16[:, 0:1]
+            dst = {d: T.mi[:, 4 - j + r:5 - j + r] if wide else T.m16[:, r:r + 1] for j, d in enumerate(cores)}
+            g.remote_dma_fused([RemoteDMATransfer(dst_ids=[did(d) for d in ds], dma_engine_mask=_mask(e),
+                                                  remote_sem=T.sem.e0, srcs=[src], dsts=[dst[d] for d in ds])
+                                for e, ds in groups.items()], local_sem=T.sem.l0)
+            cnt["l0"] = cnt.get("l0", 0) + sum(len(e) for e in groups)
+    if r < N - 1:
         need("y", ("l0", cnt["l0"]))
-        da.append(load("y", T.at[:, 1024:2048], T.a[:, 1024:2048], "da1"))
+        dv = later_loads()
 
-    kct0 = io(T.ct[:, 192:704], [[0, 512]], 0, 0)
+    out, back = _parts(core, cores, topo, -1), _parts(core, cores, topo, 1)
+    na, nx = len(out[0]), len(back[0])
+    kzero = io(T.ct[:, 64 * na:64 * na + 320], [[0, 320]], 0, 0)
 
-    def exchange(plan, codes, plane, first, width, land, rsem, lsem):
-        for part in (0, 1):
+    def exchange(part, step, codes, plane, first, width, rsem, lsem):
+        for scales in (0, 1):
             tl = []
-            for d, es in plan.items():
-                k = first[d]
-                slot = land + width * (((r - T.rank_of(d)) % N) - 1)
-                if part == 0:
-                    src, dst = codes[:, k:k + width].bitcast(dt.uint8), codes[:, slot:slot + width].bitcast(dt.uint8)
-                else:
+            for d, es in part.items():
+                n = step * (T.rank_of(d) - r) % N
+                k, slot = first(n), 2 * NC + width * (n - 1)
+                if scales:
                     src, dst = plane[:, k:k + width], plane[:, slot:slot + width]
-                tl.append(RemoteDMATransfer(dst_ids=[did(d)], dma_engine_mask=_mask(es[part]), remote_sem=T.sem[rsem],
+                else:
+                    src, dst = codes[:, k:k + width].bitcast(dt.uint8), codes[:, slot:slot + width].bitcast(dt.uint8)
+                tl.append(RemoteDMATransfer(dst_ids=[did(d)], dma_engine_mask=_mask(es[scales]), remote_sem=T.sem[rsem],
                                             srcs=[src], dsts=[dst]))
-                cnt[lsem] = cnt.get(lsem, 0) + len(es[part])
+                cnt[lsem] = cnt.get(lsem, 0) + len(es[scales])
             g.remote_dma_fused(tl, local_sem=T.sem[lsem])
 
-    kct = V(tr, T.cct[:], T.cc[:, 0:64], w=(kcx,))
-    kiw = V(scn, T.iw[:, 3:18:2], T.one[:, 0:8], T.dmt[:, 1:16:2], T.iw[:, 18:19], A.mult, A.add, w=(kiw,))
-    V(cp, T.mi[:, r:r + 1], T.e16[:, 0:1], w=(ke16,))
-    c = V(tt, T.offf[:], T.cct[:, 2:18], T.iw[:, 2:18], A.add, w=(kiw,))
-    c = ts(T.offl[:], T.offf[:], T.hs[:], None, A.subtract, w=(c,))
-    c = V(cp, T.ff[:, 0:FW].indirect(T.offl[:]), T.val[:], w=(c, kff))
-    c = V(tt, T.mk[:], T.ff[:, 0:ROOM].indirect(T.prm[:, 0:8]), T.msk[:], A.mult, w=(c,))
-    c = V(scn, T.sg[:], T.d0[:], T.mk[:], 0.0, A.mult, A.add, w=(c,))
+    run("of ol ff fo" if r < 2 else "of ol own ff fo")
+    rest = "mk sg uh ut us uu u2,u3".split()
+    steps = ("mi,la,c7 ne,cf sb ro" if r in WIDE else "mi la,c7 ne,cf sb ro").split()
+    ahead = AHEAD[list(_plan0(cores[1], cores, topo)).index(core) + 2 if r > 1 else r]
+    run(" ".join(rest[:ahead]).replace(",", " "))
+    for i in range(max(len(steps), len(rest) - ahead)):
+        run(" ".join(steps[i:i + 1] + rest[ahead + i:ahead + i + 1]).replace(",", " "))
+    run("lst")
+    klst = k["lst"]
 
-    u = c
-    if r:
-        need("v", ("e0", arrive["e0"]))
-        cnt["e0"] = arrive["e0"]
-        c = V(cp, T.mi[:, 0:r], T.m16[:, 0:r])
-    u = V(tr, T.ut[:], T.sg[:, 3:128:4], w=(u,))
-    c2 = ts(T.c7[:, 0:r + 1], T.mi[:, 0:r + 1], 4, 7, A.logical_shift_right, A.bitwise_and, w=(c,))
-    if r:
-        ts(T.fi[:, 0:r + 1], T.mi[:, 0:r + 1], 12, None, A.logical_shift_right)
-        c3 = ts(T.la[:, 0:r], T.mi[:, 0:r], 15, None, A.bitwise_and)
-    V(tt, T.us[:, 0:16], T.ut[:, 0:16], T.ut[:, 16:32], A.add, w=(u,))
-    u = V(tt, T.us[:, 16:32], T.ut[:, 0:16], T.ut[:, 16:32], A.add)
-    c = V(cp, T.c7f[:, 0:r + 1], T.c7[:, 0:r + 1], w=(c2,))
-    if r:
-        c = V(tt, T.ne[:, 0:r], T.fi[:, 1:r + 1], T.la[:, 0:r], A.not_equal, w=(c3,))
-    nt = max(2, (nb + 2) // 3)
-    for b in range(nt):
-        u2 = V(tr, T.uu[:, 32 * b:32 * b + 32], T.us[:], w=(u,))
-    c = V(scn, T.sb[:, 0:r + 1], T.c7f[:, 0:r + 1], T.ne[:, 0:r + 1], 0.0, A.add, A.add, w=(c,))
-    sb, sbb = T.sb[:, r:r + 1], T.sbb[:, r:r + 1]
-    kuu = [u2] + [f(T.uu[:, 32 * b:32 * min(b + nt, nb)], T.uu[:, 0:32 * min(nt, nb - b)], w=(u2,))
-                  for f, b in zip((sc, vc), range(nt, nb, nt))]
-    c = ts(T.ro[:], T.rst[:], sb, -4.0, A.add, A.mult, w=(c,))
-    klst = V(cp, T.lst[:], T.uu[:, 0:32 * nb].indirect(T.ro[:, 0:2]), w=(c, *kuu))
-    halves = _halves(core, cores, topo)
-    blocks = [(T.rank_of(d) - r - 1) % N for half in halves for d in half] + [N - 1]
-    at = {b: S * i + (0 if i < 3 else NC) for i, b in enumerate(blocks)}
 
-    def pick(f, bs, w):
-        for b in bs:
-            if b - 1 not in bs:
-                n = next(j for j in range(1, N + 1) if b + j not in bs)
-                c = f(T.ct[:, 4 * at[b]:4 * (at[b] + S * n)], T.xs[:, 0:2048].indirect(T.lst[:, 4 * b:4 * (b + n)]), w=w)
-        return c
+    def product(bank, codes, plane, a, n=NC):
+        (lq, rq), (ls, rs) = codes, plane
+        return done(ten.matmul_mx(T.ps[:, 512 * bank:512 * bank + n], lq, ls, rq[:, a:a + n], rs[:, a:a + n], True, True),
+                    "kt")
 
-    ks1 = pick(sc, blocks[2:3], (klst, kct0, *dx.values()))
-    ks2 = pick(sc, blocks[3:5], ())
-    c = pick(vc, blocks[0:2], (klst, kct0))
-    kqc = V(qz, T.qc[:, 0:NC], T.sc[:, 0:NC], T.ct[:, 0:512], w=(c, ks1))
+    def pick(f, at, a, e, w=()):
+        return f(T.ct[:, at:at + 16 * (e - a)], T.xs[:, 0:2048].indirect(T.lst[:, a:e]), w=w)
+
+    a = 4 * (N - 1 - na)
+    ks1 = pick(sc, 32 * na, a + 2 * na, 28, (klst, *dx.values()))
+    ks2 = pick(sc, 768 - 16 * a, 0, a)
+    c = pick(vc, 0, a, a + 2 * na, (klst,))
+    kqc = V(qz, T.qc[:, 0:NC], T.sc[:, 0:NC], T.ct[:, 0:512], w=(c, ks1, kzero))
     need("g", kqc)
-    exchange(halves[0], T.qc, T.sc, {d: at[(T.rank_of(d) - r - 1) % N] for d in halves[0]}, S, 2 * NC, "e1", "l1")
-    c = pick(vc, blocks[5:8], ())
-    kqc = V(qz, T.qc[:, NC:2 * NC], T.sc[:, NC:2 * NC], T.ct[:, 512:1024], w=(c, ks2))
+    exchange(out[0], -1, T.qc, T.sc, lambda n: S * (na - n), S, "e10", "l1")
+    c = pick(vc, 768, 28, 32)
+    kqc = V(qz, T.qc[:, NC:2 * NC], T.sc[:, NC:2 * NC], T.ct[:, 320:832], w=(c, ks2))
     need("g", kqc)
-    exchange(halves[1], T.qc, T.sc, {d: at[(T.rank_of(d) - r - 1) % N] for d in halves[1]}, S, 2 * NC, "e1", "l1")
+    exchange(out[1], -1, T.qc, T.sc, lambda n: 2 * NC - S * (n - na + 1), S, "e11", "l1")
 
+    def pack_a(i):
+        return V(qz, T.qa[:, 128 * i:128 * i + 128], T.sa[:, 128 * i:128 * i + 128], T.at[:, 512 * i:512 * i + 512],
+                 w=(da[i // 2],))
+
+    si(T.nhs[:], T.hs[:], -256.0 - r, -1.0)
+    for h in (0, 1):
+        klab = si(T.tcs[:, 32 + 8 * h:40 + 8 * h], slots(h, 8, 2), 16.0, -1.0)
+        V(tt, T.tcs[:, 8 * h:8 * h + 8], T.cct[:, 34 + h:50:2], before[h], A.add)
+    c = ts(T.ci[:, 0:r + 1], mi, 4, 255, A.logical_shift_right, A.bitwise_and)
     kqw = V(qz, T.qw[:], T.sw[:], T.wt[:], w=(dw,))
     need("t", kqw, *kqx.values())
-    kwx = done(ten.matmul_mx(T.ps[:, 1024:1536], T.qw[:], T.sw[:], T.qx[:], T.sx[:], True, True), "kt")
-    kwxs = sc(T.wx[:], T.ps[:, 1024:1536], w=(kwx,))
-    kqv = V(qz, T.qv[:], T.sv[:], T.vt[:], w=(dv,))
-    kqa = {}
-    c0 = V(ms, T.tcs[:], 0.0)
+    kwx = product(2, (T.qw[:], T.qx), (T.sw[:], T.sx), 0, 512)
+    kcd = V(tr, T.cdw[:], T.tcs[:], w=(c, klab))
+    c = V(cp, T.cif[:, 0:r + 1], T.ci[:, 0:r + 1])
+    kqa = [pack_a(0)]
     for i in range(4):
-        kqa[i] = V(qz, T.qa[:, 128 * i:128 * i + 128], T.sa[:, 128 * i:128 * i + 128], T.at[:, 512 * i:512 * i + 512],
-                   w=(da[i // 2],))
-    c = ts(T.ci[:, 0:r + 1], T.mi[:, 0:r + 1], 4, 255, A.logical_shift_right, A.bitwise_and)
-    for h in (0, 1):
-        V(tt, T.tcs[:, 8 * h:8 * h + 8], T.cct[:, 34 + h:50:2], T.iw[:, 2 + h:18:2], A.add, w=(c0,))
-        kcd = ts(T.tcs[:, 32 + 8 * h:40 + 8 * h], slots(h, 8, 2), -1.0, 16.0, A.mult, A.add)
-    c = V(cp, T.cif[:, 0:r + 1], T.ci[:, 0:r + 1], w=(c,))
-    kcd = V(tr, T.cdw[:], T.tcs[:], w=(kcd,))
-    c = V(scn, T.sbb[:, 0:r + 1], T.cif[:, 0:r + 1], T.ne[:, 0:r + 1], -128.0, A.add, A.add, w=(c,))
+        kcp = si(T.cd[:, 16 * i:16 * i + 16], T.cdw[:, 16 * (i // 2):16 * (i // 2) + 16], T.nhs[:], 1.0, w=(kcd, klab))
+    kwxs = sc(T.wx[:, 0:CUT], T.ps[:, 1024:1024 + CUT], w=(kwx,))
     if r:
-        ts(T.nx[:], T.ne[:, r - 1:r], 200.0, T.cif[:, r:r + 1], A.mult, A.add)
+        ts(T.nx[:], T.ne[:, r - 1:r], 200.0, T.cif[:, r:r + 1], A.mult, A.add, w=(c,))
     else:
         V(ms, T.nx[:], 999.0)
-    for i in range(4):
-        kcp = ts(T.cd[:, 16 * i:16 * i + 16], T.cdw[:, 16 * (i // 2):16 * (i // 2) + 16], T.hs[:], None, A.subtract,
-                 w=(kcd,))
+    c = V(scn, T.sbb[:, 0:r + 1], T.cif[:, 0:r + 1], T.ne[:, 0:r + 1], -128.0, A.add, A.add, w=(c,))
+    kqa.append(pack_a(1))
     klb1 = ts(T.lb1[:], T.cdw[:, 0:32], T.hs[:], sbb, A.subtract, A.add, w=(c,))
     need("y", klb1)
     done(syn.dma_start(T.lb[0:1, :], T.cdw[0:16, 32:64]), "dl0", 16)
     done(syn.dma_start(T.lb[1:2, :], T.lb1[0:16, :]), "dl1", 16)
+    kqa += [pack_a(2), pack_a(3)]
 
-    need("t", ("e1", arrive["e1"]), kqc)
-    cnt["e1"] = arrive["e1"]
-    kh = []
-    for i in range(4):
-        need("t", kqa[i])
-        o = T.ps[:, 2048 + 512 * i:2048 + 512 * i + NC]
-        m = done(ten.matmul_mx(o, T.qa[:, 128 * i:128 * i + 128], T.sa[:, 128 * i:128 * i + 128],
-                               T.qc[:, 2 * NC - S:3 * NC - S], T.sc[:, 2 * NC - S:3 * NC - S], True, True), "kt")
-        if i % 2 == 0:
-            need("s", m)
-            kh.append(done(sca.activation(T.ht[:, i:512:4], o, AF.Relu, 0.0, 0.05), "ks"))
-        else:
-            kh.append(ts(T.ht[:, i:512:4], o, 0.0, 0.05, A.max, A.mult, w=(m,)))
-    kqh = V(qz, T.qh[:, 0:NC], T.sh[:, 0:NC], T.ht[:], w=kh)
-    need("g", kqh)
-    plan = _plan(core, cores, topo)
-    exchange(plan, T.qh, T.sh, {d: S * ((T.rank_of(d) - r) % N) - 2 for d in plan}, S2, NC, "e2", "l2")
+    wide = [S * (nx + 1), NC - S * (nx + 1) + 2]
+    V(ms, T.ht[:, 4 * wide[0]:896 - 4 * wide[1]], 0.0)
+    kh, kqh = [], []
+    for h in (0, 1):
+        wait("t", "e1%d" % h, kqc)
+        at = 896 - 4 * wide[1] if h else 0
+        for i, bank in enumerate((0, 1, 4, 5) if h else (4, 5, 6, 7)):
+            need("t", kqa[i], *(kh[i - 2:i - 1] if h and i > 1 else ()))
+            m = product(bank, (T.qa[:, 128 * i:128 * i + 128], T.qc), (T.sa[:, 128 * i:128 * i + 128], T.sc),
+                        2 * NC - S if h else NC + S * nx)
+            o, tile = T.ps[:, 512 * bank + NC - wide[h]:512 * bank + NC], T.ht[:, at + i:at + 4 * wide[h]:4]
+            if i % 2 == 0:
+                kh.append(si(tile, o, 0.0, 0.05, AF.Relu, w=(m,)))
+            else:
+                kh.append(ts(tile, o, 0.0, 0.05, A.max, A.mult, w=(m,)))
+        kqh.append(V(qz, T.qh[:, NC * h:NC * h + NC], T.sh[:, NC * h:NC * h + NC], T.ht[:, 384 * h:384 * h + 512],
+                     w=kh[-2:]))
+        need("g", kqh[h])
+        exchange(back[h], 1, T.qh, T.sh, lambda n: NC * h + S * n - 2, S2, "e2%d" % h, "l2")
 
     c = V(tr, T.tc[:], T.cd[:], w=(kcp,))
-    ts(T.ii[:], T.tc[:], 0.125, 0.4375, A.mult, A.add, w=(c,))
-    c = ts(T.t1[:], T.tc[:], sb, float(N - r), A.add, A.add)
-    c2 = ts(T.fx[:], T.tc[:], T.nx[:], 128.0, A.add, A.not_equal)
+    kqv = V(qz, T.qv[:], T.sv[:], T.vt[:], w=(dv,))
+    vq, vs = (T.qv[:], T.qh), (T.sv[:], T.sh)
+    need("t", kqv)
+    m = product(3, vq, vs, 0)
+    c = ts(T.t1[:], T.tc[:], sb, -1.0, A.add, A.mult, w=(c,))
+    ts(T.ii[:], T.tc[:], 0.125, 0.4375 + 0.125 * (256 + r), A.mult, A.add)
+    c2 = ts(T.fx[:], T.tc[:], T.nx[:], -128.0 - r, A.add, A.not_equal)
     c = ts(T.kk[:], T.t1[:], 7, None, A.bitwise_and, w=(c,))
-    need("t", kqh, kqv)
-    m = done(ten.matmul_mx(T.ps[:, 1536:1536 + NC], T.qv[:], T.sv[:], T.qh[:, 0:NC], T.sh[:, 0:NC], True, True), "kt")
-    c = ts(T.k18[:], T.kk[:], float(S2), 1.0, A.mult, A.add, w=(c,))
     c2 = V(tt, T.s1[:], T.ii[:], T.fx[:], A.mult, w=(c2,))
+    c = ts(T.k18[:], T.kk[:], float(S2), 1.0, A.mult, A.add, w=(c,))
+    V(cp, T.vw[:, 2:S2], T.ps[:, 1536:1536 + S], w=(m,))
     c = V(tt, T.s2[:], T.s1[:], T.k18[:], A.add, w=(c, c2))
-    V(cp, T.vw[:, 0:2], T.ps[:, 1536 + NC - 2:1536 + NC], w=(m,))
-    V(cp, T.vw[:, 2:S2], T.ps[:, 1536:1536 + S])
     V(cp, T.fin[:, 0:32:2], T.s2[:, 0:16], w=(c,))
     kfin = V(cp, T.fin[:, 1:32:2], T.s2[:, 32:48])
+    n = S2 * na
+    wait("t", "e20")
+    m = product(6, vq, vs, NC + n)
+    V(cp, T.vw[:, 0:2], T.ps[:, 3072 + NC - n - 2:3072 + NC - n], w=(m,))
+    V(cp, T.vw[:, S2:S2 + n], T.ps[:, 3072 + NC - n:3072 + NC])
 
-    need("t", ("e2", arrive["e2"]))
-    cnt["e2"] = arrive["e2"]
-    m = done(ten.matmul_mx(T.ps[:, 0:128], T.qv[:], T.sv[:], T.qh[:, NC - 2:NC + 126], T.sh[:, NC - 2:NC + 126], True, True), "kt")
-    c = V(cp, T.vw[:, S2:N * S2], T.ps[:, 2:128], w=(m,))
-    for h, (k, e) in enumerate(((0, 128), (128, 320), (320, 512))):
-        c = V(tt, T.yt[:, k:e], T.vw[:, 0:N * S2].indirect(T.fin[:, k // 16:e // 16]), T.wx[:, k:e], A.add,
-              w=(c, kwxs, kfin) if h == 0 else ())
+    wait("t", "e21")
+    m = product(7, vq, vs, 2 * NC - 2)
+    c = V(cp, T.vw[:, S2 + n:N * S2], T.ps[:, 3584 + 2 + n:3584 + NC], w=(m,))
+    ky = sc(T.yg[:], T.vw[:, 0:N * S2].indirect(T.fin[:, CUT // 16:32]), w=(c,))
+    for h, (a, e) in enumerate(((0, CUT // 2), (CUT // 2, CUT), (CUT, 512))):
+        if h < 2:
+            c = V(tt, T.yt[:, a:e], T.vw[:, 0:N * S2].indirect(T.fin[:, a // 16:e // 16]), T.wx[:, a:e], A.add,
+                  w=(c, kwxs) if h == 0 else ())
+        else:
+            c = V(tt, T.yt[:, a:e], T.yg[:], T.ps[:, 1024 + a:1024 + e], A.add, w=(ky,))
         qn = "ysy"[h]
         need(qn, c)
-        done(queue[qn].dma_start(T.y[:, k:e], T.yt[:, k:e]), "dy%d" % h, 16)
+        done(queue[qn].dma_start(T.y[:, a:e], T.yt[:, a:e]), "dy%d" % h, 16)
 
     for s in SEMAPHORES:
         if cnt.get(s) and all(known.get((qn, s), 0) < cnt[s] for qn in queue):

@@ -7,11 +7,10 @@ S2 = 18
 NC = N * S
 ROOM = 136
 GAP = 160
-FW = 19 * GAP
-AHEAD = (1, 4, 3, 3, 3, 3, 4, 4)
-WIDE = (1, 2)
+FW = 130 * GAP
+BOTH = N - 2
 CUT = 320
-UW = 9 * 32
+ROUND = 1.5 * 2.0 ** 28
 
 F32, BF, I32, U16, C8, U8 = "float32", "bfloat16", "int32", "uint16", "float8_e4m3fn_x4", "uint8"
 
@@ -23,34 +22,36 @@ def _sb(n, d):
 SCRATCH = {
     "ps": ("psum", [128, 4096], F32),
     "xs": _sb(2048, BF), "pt": _sb(576, BF), "at": _sb(2048, BF), "wt": _sb(512, BF), "vt": _sb(512, BF),
-    "qx": _sb(512, C8), "sx": _sb(512, U8), "qp": _sb(144, C8), "sp": _sb(144, U8),
+    "qx": _sb(512 + S, C8), "sx": _sb(512 + S, U8), "qp": _sb(144, C8), "sp": _sb(144, U8),
     "qa": _sb(512, C8), "sa": _sb(512, U8), "qw": _sb(128, C8), "sw": _sb(128, U8), "qv": _sb(128, C8), "sv": _sb(128, U8),
     "ct": _sb(832, BF), "qc": _sb(2 * NC + 112, C8), "sc": _sb(2 * NC + 112, U8),
     "ht": _sb(896, BF), "qh": _sb(2 * NC + 126, C8), "sh": _sb(2 * NC + 126, U8),
-    "pi": _sb(1, I32), "pj": _sb(4, I32), "pf": _sb(4, F32), "io32": _sb(32, F32), "trash": _sb(32, F32),
+    "pi": _sb(4, I32), "pj": _sb(4, I32), "pf": _sb(4, F32), "io32": _sb(32, F32), "trash": _sb(32, F32),
     "vali": _sb(128, F32), "val": _sb(128, F32), "prm": _sb(8, U16), "ypi": _sb(128, F32), "yab": _sb(128, F32),
-    "msk": _sb(128, F32), "d0": _sb(128, F32), "c0": _sb(1, F32), "m0": _sb(1, F32), "m31": _sb(1, F32), "k0": _sb(1, F32),
-    "lane": _sb(6, F32), "vb": _sb(1, F32), "uh": _sb(32, F32), "tb": _sb(1, F32), "pb": _sb(4, F32), "nrho": _sb(1, F32),
-    "rst": _sb(2, F32), "reset": _sb(128, F32), "one2": _sb(128, BF), "one": _sb(64, F32),
-    "z": _sb(320, F32), "mx": _sb(256, F32), "nn": _sb(256, BF), "ss": _sb(544, BF), "h2": _sb(64, BF),
-    "fl": _sb(64, F32), "cc": _sb(128, F32), "cct": _sb(96, F32), "zf": _sb(1, F32), "dmt": _sb(65, F32),
-    "hs": _sb(1, F32), "e16": _sb(2, U16), "iw": _sb(25, F32), "nfe": _sb(32, F32), "nfd": _sb(32, F32),
-    "offf": _sb(8, F32), "offl": _sb(8, U16), "ff": _sb(FW, F32),
-    "mk": _sb(128, F32), "sg": _sb(128, F32), "ut": _sb(32, F32), "us": _sb(32, F32), "uu": _sb(UW, F32),
-    "m16": _sb(8, U16), "mi": _sb(8, I32), "fi": _sb(8, I32), "la": _sb(8, I32), "c7": _sb(8, I32), "c7f": _sb(8, F32),
-    "ne": _sb(8, F32), "sb": _sb(8, F32), "ci": _sb(8, I32), "cif": _sb(8, F32), "sbb": _sb(8, F32), "nx": _sb(1, F32),
-    "ro": _sb(2, U16), "lst": _sb(32, U16),
-    "tcs": _sb(64, F32), "cdw": _sb(64, F32), "cd": _sb(64, F32),
+    "msk": _sb(128, F32), "d0": _sb(128, F32), "pb": _sb(9, F32), "qo": _sb(2, U16), "cap": _sb(64, F32),
+    "rst": _sb(2, F32), "reset": _sb(128, F32), "one2": _sb(128, BF), "rab": _sb(17, F32), "rm": _sb(17, F32),
+    "dd": _sb(16, BF), "an": _sb(96, BF), "ao": _sb(96, BF), "as1": _sb(96, F32), "at2": _sb(64, F32),
+    "xb": _sb(512, BF), "qb": _sb(128 + S, C8), "sb": _sb(128 + S, U8), "lr": _sb(32, F32), "lt": _sb(32, F32),
+    "z": _sb(352, F32), "mx": _sb(288, F32), "nn": _sb(288, BF), "ss": _sb(576, BF), "h2": _sb(64, BF),
+    "dz": _sb(32, BF), "d32": _sb(32, BF), "cw": _sb(160, F32), "dm": _sb(97, F32), "nb": _sb(18, BF), "nc": _sb(16, F32), "sf": _sb(17, F32),
+    "nfe": _sb(32, F32), "nfd": _sb(32, F32), "cx": _sb(40, F32), "offl": _sb(16, U16), "ff": _sb(FW, F32),
+    "mk": _sb(128, F32), "sg": _sb(128, F32), "xh": _sb(64, F32), "uu": _sb(64, F32),
+    "md": _sb(16, BF), "dec": _sb(12, F32), "ro": _sb(2, U16), "lst": _sb(32, U16), "ec": _sb(3, F32), "nx": _sb(2, F32),
+    "cd": _sb(64, F32), "lab": _sb(32, F32), "lb1": _sb(32, F32),
     "tc": _sb(64, F32), "ii": _sb(64, I32), "t1": _sb(64, I32), "kk": _sb(64, I32), "k18": _sb(64, F32), "fx": _sb(64, F32),
-    "s1": _sb(64, F32), "s2": _sb(64, F32), "fin": _sb(32, U16), "lb1": _sb(32, F32),
-    "wx": _sb(CUT, F32), "vw": _sb(N * S2, F32), "yt": _sb(512, F32), "yg": _sb(512 - CUT, F32), "nhs": _sb(1, F32),
+    "s1": _sb(64, F32), "s2": _sb(64, F32), "fin": _sb(32, U16),
+    "wx": _sb(CUT, F32), "vw": _sb(N * S2, F32), "yt": _sb(512, F32), "yg": _sb(512 - CUT, F32),
 }
-SEMAPHORES = ["kv", "ks", "kt", "kg", "dp", "dx0", "dx1", "dx2", "dx3", "da0", "da1", "dw", "dv",
-              "dl0", "dl1", "e0", "e10", "e11", "e20", "e21", "l0", "l1", "l2", "dy0", "dy1", "dy2"]
+SEMAPHORES = ["kv", "ks", "kt", "kg", "dp", "dxb", "dx0", "dx1", "dx2", "dx3", "da0", "da1", "dw", "dv",
+              "dl0", "dl1", "eb", "e0", "e10", "e11", "e20", "e21", "lb", "l0", "l1", "l2", "dy0", "dy1", "dy2"]
 
 
 def _mask(es):
     return sum(1 << e for e in es)
+
+
+def _far(core, cores, topo):
+    return [topo.engines(core, d) for d in cores if topo.chip(d) != topo.chip(core)][0]
 
 
 def _near(core, d, off_engines, topo):
@@ -89,9 +90,8 @@ def _beside(core, cores, topo):
 
 def _plan0(core, cores, topo):
     ch = topo.chip(core)
-    eo = [topo.engines(core, d) for d in cores if topo.chip(d) != ch][0]
+    eo = _far(core, cores, topo)
     later = cores[cores.index(core) + 1:]
-    later.sort(key=lambda d: (not _alone(d, cores, topo), _beside(d, cores, topo), -cores.index(d)))
     return {d: _near(core, d, eo, topo)[:2] if topo.chip(d) == ch and core == cores[0] else eo for d in later}
 
 
@@ -99,7 +99,7 @@ def rank_program(g, core, T, topo):
     r = T.rank_of(core)
     if r is None:
         return
-    A, X, AF = AluOpType, AxisListType.X, ActivationFunctionType
+    A, AF = AluOpType, ActivationFunctionType
     cores = list(T.cores)
     vec, sca, ten, syn = g.vector, g.scalar, g.tensor, g.sync
     queue = {"v": vec, "s": sca, "t": ten, "g": g, "y": syn}
@@ -137,201 +137,18 @@ def rank_program(g, core, T, topo):
         need("s", *w)
         return done(sca.activation(out, in_, func, bias, scale), "ks")
 
-    tt, cp, ms, rd, scn, tr, qz = (vec.tensor_tensor, vec.tensor_copy, vec.memset, vec.tensor_reduce,
-                                   vec.tensor_tensor_scan, vec.transpose, vec.quantize_mx)
+    tt, cp, ms, scn, tr, qz = (vec.tensor_tensor, vec.tensor_copy, vec.memset, vec.tensor_tensor_scan, vec.transpose,
+                               vec.quantize_mx)
 
     def vc(out, in_, w=()):
         return V(cp, out, in_, w=w)
 
-    def load(qn, out, in_, sem):
-        return done(queue[qn].dma_start(out, in_), sem, 16)
+    def did(d):
+        rid, pid, _ = topo.addr(d)
+        return DstId(rid=rid, pnc=pid)
 
-    dp = load("s", T.pt[:, 0:64], T.p[:, 0:64], "dp")
-    dx = {i: load("y", T.xs[:, 512 * i:512 * i + 512], T.x[:, 512 * i:512 * i + 512], "dx%d" % i) for i in (1, 3, 0, 2)}
-    da = [load("y", T.at[:, 0:1024], T.a[:, 0:1024], "da0")]
-    dw = load("y", T.wt[:], T.w[:], "dw")
-
-    def later_loads():
-        da.append(load("y", T.at[:, 1024:2048], T.a[:, 1024:2048], "da1"))
-        return load("y", T.vt[:], T.v[:], "dv")
-
-    if r == N - 1:
-        dv = later_loads()
-
-    kpi = io(T.pi[:], [[1, 1]], 0, 1)
-    kio = io(T.io32[:], [[1, 32]], 0, 0)
-    kz = io(T.z[:, 31:192:160], [[0, 2]], 0, 0)
-    io(T.one[:, 1:64], [[0, 63]], 1, 0)
-    kone = io(T.one[:, 0:1], [[0, 1]], -1, 0)
-    kypi = io(T.ypi[:], [[0, 32], [1, 4]], 0, 0)
-    io(T.ne[:], [[0, 8]], 0, 0)
-    io(T.dmt[:, 32:33], [[0, 1]], 0, 0)
-    kfl0 = io(T.fl[:, 32:64], [[0, 32]], 0, 0)
-    io(T.tcs[:], [[0, 64]], 0, 0)
-    kpp = io(T.lane[:, 4:5], [[0, 1]], 0, 1)
-    kval = io(T.vali[:], [[128, 8], [4, 16]], 512, 0)
-    kff = io(T.ff[:, 0:ROOM], [[0, ROOM]], 0, 0)
-    c = V(ms, T.reset[:], 0.0)
-    V(ms, T.ss[:, 15:544:16], 0.0)
-    kp0 = V(ms, T.pt[:, 64:128], 0.0)
-    c = V(ms, T.one2[:], 1.0)
-    ts(T.pj[:, 0:1], T.pi[:], 31, None, A.bitwise_and, w=(kpi,))
-    ts(T.pj[:, 1:2], T.pi[:], 15, None, A.bitwise_and)
-    ts(T.pj[:, 2:3], T.pi[:], 3, None, A.bitwise_and)
-    c2 = ts(T.pj[:, 3:4], T.pi[:], 2, 3, A.logical_shift_right, A.bitwise_and)
-    V(ms, T.reset[:, 0:128:16], -5e29, w=(c,))
-    V(ms, T.ss[:, 47:48], 99.0)
-    cpf = V(cp, T.pf[:], T.pj[:], w=(c2,))
-    p32, p16, tcol, rho = (T.pf[:, i:i + 1] for i in range(4))
-
-    kp = sc(T.pt[:, 256:384], T.pt[:, 0:128], w=(dp, kp0))
-    V(cp, T.pt[:, 128:256], T.pt[:, 0:128], w=(dp,))
-    V(cp, T.pt[:, 384:512], T.pt[:, 0:128])
-    kpv = V(cp, T.pt[:, 512:576], T.pt[:, 0:64])
-
-    turn = N * r + N - 1 + (r + 1) % N
-    nb = (turn + 15) // N
-    kpb = si(T.pb[:, 0:1], p16, 1.0, 8.0, w=(cpf,))
-    si(T.m0[:], p32, 256.0, -256.0, AF.Relu)
-    c = si(T.m31[:], p32, -30.0, 1.0, AF.Relu)
-    c2 = si(T.pb[:, 1:2], p16, -2.0, 1.0, AF.Abs)
-    c3 = si(T.pb[:, 2:3], p32, -1.5, 1.0, AF.Sign)
-    c = si(T.pb[:, 3:4], T.m0[:], T.m31[:], 1.0, w=(c,))
-    si(T.c0[:], T.pb[:, 1:2], 1.0, -1.0, AF.Relu, w=(c2,))
-    si(T.one[:, 32:33], T.pb[:, 2:3], 0.0, 1.0, AF.Relu, w=(c3, kone))
-    si(T.k0[:], T.pb[:, 3:4], 0.0, -1.0, w=(c,))
-    si(T.rst[:, 0:1], p16, -1.0 * turn, -0.25)
-    si(T.rst[:, 1:2], p16, -1.0 * turn - 4.0, -0.25)
-    ktb = si(T.tb[:], p32, 0.0, float(GAP))
-    knr = si(T.nrho[:], rho, 0.0, -1.0)
-    kla = si(T.lane[:, 0:1], p16, tcol, -4.0)
-    ktrash = si(T.trash[:], T.io32[:], T.tb[:], 1.0, w=(kio, ktb))
-    c = si(T.yab[:], T.ypi[:], T.nrho[:], 1.0, AF.Abs, w=(kypi, knr))
-    si(T.d0[:], T.ypi[:], 0.0, 1.0, AF.Sign)
-    si(T.msk[:], T.yab[:], 1.0, -1.0, AF.Relu, w=(c,))
-    si(T.lane[:, 2:3], p32, T.lane[:, 0:1], 4.0, w=(kla,))
-    c = si(T.lane[:, 5:6], T.lane[:, 4:5], -63.5, 1.0, AF.Sign, w=(kpp,))
-    kvb = si(T.vb[:], T.lane[:, 5:6], T.lane[:, 2:3], 512.0, w=(c,))
-
-    kqx, ksc, kch = {}, {}, {}
-
-    def pack(i):
-        b, h = i % 2, i // 2
-        kqx[i] = V(qz, T.qx[:, 128 * i:128 * i + 128], T.sx[:, 128 * i:128 * i + 128], T.xs[:, 512 * i:512 * i + 512],
-                   w=(dx[i],))
-        if "p" not in kch:
-            kch["p"] = V(qz, T.qp[:], T.sp[:], T.pt[:], w=(kpv, kp))
-        need("t", kch["p"], kqx[i])
-        ksc[b] = done(ten.matmul_mx(T.ps[:, 512 * b:512 * b + 128], T.qp[:, 16 * h:16 * h + 128],
-                                    T.sp[:, 16 * h:16 * h + 128], T.qx[:, 128 * i:128 * i + 128],
-                                    T.sx[:, 128 * i:128 * i + 128], h == 0, h == 1), "kt")
-
-    def step(b, n, a=0, e=128):
-        k = slice(128 * b + a, 128 * b + e)
-        z, before = T.z[:, 32 + 160 * b + a:32 + 160 * b + e], T.z[:, 31 + 160 * b + a:31 + 160 * b + e]
-        if n == 0:
-            c = V(tr, z, T.ps[:, 512 * b + a:512 * b + e], w=(ksc[b],))
-        elif n == 1:
-            c = V(scn, T.mx[:, k], before, T.reset[:, a:e], 0.0, A.max, A.add, w=(kch[b, a], kz))
-        elif n == 2:
-            c = V(tt, T.nn[:, k], z, T.mx[:, k], A.is_le, w=(kch[b, a],))
-        else:
-            c = V(scn, T.ss[:, 64 + k.start:64 + k.stop], T.nn[:, k], T.one2[:, a:e], 0.0, A.mult, A.add, w=(kch[b, a],))
-        kch[b, a] = c
-        return c
-
-    def both(n):
-        step(0, n, 0, 64)
-        return step(0, n, 64, 128)
-
-    def slots(first, n, step=1):
-        k = 16 * (first + 4) + 15
-        return T.ss[:, k:k + 16 * step * (n - 1) + 1:16 * step]
-
-    pack(1), pack(3), pack(0), step(1, 0), pack(2), step(1, 1)
-    ts(T.prm[:], T.io32[:, 0:8], T.pb[:, 0:1], None, A.add, w=(kpb, kio))
-    kch[1, 64] = kch[1, 0]
-    step(1, 2, 0, 64), both(0)
-    kch[1, 0] = step(1, 2, 64, 128)
-    both(1), step(1, 3)
-    kch[0, 0] = both(2)
-    ksl = sc(slots(-1, 1), slots(14, 1), w=(kch[1, 0],))
-    kzf = si(T.zf[:], slots(15, 1), T.k0[:], T.m31[:])
-    c = step(0, 3)
-    kz2 = si(T.fl[:, 32:33], slots(0, 1), T.zf[:], T.m0[:], w=(c, kzf, kfl0))
-    kval = si(T.val[:], T.vali[:], T.vb[:], 1.0, w=(kval, kvb))
-    V(tr, T.h2[:, 0:32], slots(-4, 32), w=(c, ksl))
-    c = V(tr, T.h2[:, 32:64], slots(-2, 32))
-    here, prev = T.h2[:, 32:64], T.h2[:, 31:63]
-    before = [T.iw[:, 0:8], T.iw[:, 17:25]]
-    sb, sbb = T.sb[:, r:r + 1], T.sbb[:, r:r + 1]
-    half = (slice(0, 64), slice(64, 128))
-    nt = max(2, (nb + 2) // 3)
-    mo = 4 - r if r in WIDE else 0
-    mi = T.mi[:, mo:mo + r + 1]
-    k = {"h2": c}
-
-    def first_label(out, number, w=()):
-        return ts(out, number, 1.0 / 4096, 0.5 / 4096 - 0.5, A.mult, A.add, w=w)
-
-    def landed():
-        wait("v", "e0")
-        if r in WIDE:
-            if r > 1:
-                ts(T.fi[:, 1:r], T.mi[:, mo + 1:mo + r], 12, None, A.logical_shift_right)
-            return k["own"]
-        c = V(cp, T.mi[:, 0:r], T.m16[:, 0:r])
-        if r > 1:
-            first_label(T.fi[:, 1:r], T.m16[:, 1:r])
-        return c
-
-    def again(f, b):
-        return f(T.uu[:, 32 * b:32 * min(b + nt, nb)], T.uu[:, 0:32 * min(nt, nb - b)], w=(k["uu"],))
-
-    call = {
-        "fl": lambda: V(tt, T.fl[:, 0:32], here, prev, A.not_equal, w=(k["h2"],)),
-        "cs": lambda: V(scn, T.cc[:, 64:128], T.one[:], T.fl[:], T.c0[:], A.mult, A.add, w=(k["fl"], kz2)),
-        "dm": lambda: V(tr, T.dmt[:, 0:32], T.cc[:, 96:128], w=(k["cs"],)),
-        "hs": lambda: V(rd, T.hs[:], T.dmt[:, 0:18], X, A.add, w=(k["dm"],)),
-        "e16": lambda: ts(T.e16[:, 0:1], T.hs[:], 16.0, T.dmt[:, 31:32], A.mult, A.add, w=(k["hs"],)),
-        "nf": lambda: V(tt, T.nfe[:], here, prev, A.is_equal),
-        "nd": lambda: V(tt, T.nfd[:], T.nfe[:], T.trash[:], A.mult, w=(k["nf"], ktrash)),
-        "d2": lambda: V(tr, T.dmt[:, 33:65], T.cc[:, 96:128]),
-        "cx": lambda: V(tt, T.cc[:, 32:64], T.cc[:, 64:96], T.nfd[:], A.max, w=(k["nd"],)),
-        "iw": lambda: V(scn, T.iw[:], T.one[:, 33:58], T.dmt[:, 0:49:2], 128.0, A.mult, A.add, w=(k["d2"],)),
-        "ct": lambda: V(tr, T.cct[:, 0:64], T.cc[:, 32:96], w=(k["cx"],)),
-        "of": lambda: [V(tt, T.offf[p, :], T.cct[p, 2 + h:18:2], T.iw[p, 17 * h:17 * h + 8], A.add, w=(k["ct"], k["iw"]))
-                       for h, p in enumerate(half)][-1],
-        "ol": lambda: ts(T.offl[:], T.offf[:], T.hs[:], None, A.subtract, w=(k["of"],)),
-        "ff": lambda: V(cp, T.ff[:, 0:FW].indirect(T.offl[:]), T.val[:], w=(k["ol"], kff, kval)),
-        "mk": lambda: V(tt, T.mk[:], T.ff[:, 0:ROOM].indirect(T.prm[:, 0:8]), T.msk[:], A.mult, w=(k["ff"],)),
-        "sg": lambda: V(scn, T.sg[:], T.d0[:], T.mk[:], 0.0, A.mult, A.add, w=(k["mk"],)),
-        "uh": lambda: [V(tt, T.uh[p, :], T.sg[0:64, 3:128:4], T.sg[64:128, 3:128:4], A.add, w=(k["sg"],))
-                       for p in half][-1],
-        "ut": lambda: V(tr, T.ut[:], T.uh[:], w=(k["uh"],)),
-        "us": lambda: [V(tt, T.us[:, a:a + 16], T.ut[:, 0:16], T.ut[:, 16:32], A.add, w=(k["ut"],)) for a in (0, 16)][-1],
-        "uu": lambda: [V(tr, T.uu[:, 32 * b:32 * b + 32], T.us[:], w=(k["us"],)) for b in range(nt)][-1],
-        "u2": lambda: again(sc, nt) if nb > nt else k["uu"],
-        "u3": lambda: again(vc, 2 * nt) if nb > 2 * nt else k["uu"],
-        "own": lambda: ts(T.mi[:, mo + r:mo + r + 1], T.hs[:], 16.0, T.dmt[:, 31:32], A.mult, A.add, w=(k["hs"],)),
-        "fo": lambda: ts(T.fi[:, r:r + 1], T.dmt[:, 0:1], 1.0 / 256, None, A.mult),
-        "mi": lambda: landed() if r else k["own"],
-        "la": lambda: ts(T.la[:, 0:r], T.mi[:, mo:mo + r], 15, None, A.bitwise_and, w=(k["mi"],)) if r else k["mi"],
-        "c7": lambda: ts(T.c7[:, 0:r + 1], mi, 4, 7, A.logical_shift_right, A.bitwise_and, w=(k["mi"],)),
-        "ne": lambda: V(tt, T.ne[:, 0:r], T.fi[:, 1:r + 1], T.la[:, 0:r], A.not_equal, w=(k["la"],)) if r else k["la"],
-        "cf": lambda: V(cp, T.c7f[:, 0:r + 1], T.c7[:, 0:r + 1], w=(k["c7"],)),
-        "sb": lambda: V(scn, T.sb[:, 0:r + 1], T.c7f[:, 0:r + 1], T.ne[:, 0:r + 1], 0.0, A.add, A.add, w=(k["cf"],)),
-        "ro": lambda: ts(T.ro[:], T.rst[:], sb, -4.0, A.add, A.mult, w=(k["sb"],)),
-        "lst": lambda: V(cp, T.lst[:], T.uu[:, 0:32 * nb].indirect(T.ro[:, 0:2]), w=(k["ro"], k["u2"], k["u3"])),
-    }
-
-    def run(names):
-        for name in names.split():
-            k[name] = call[name]()
-
-    run("fl nf cs nd dm d2" + (" hs cx e16 own iw ct" if r < 2 else " hs cx e16 iw ct" if r < N - 1 else " cx hs iw ct"))
-
-    arrive = {"e0": 0, "e10": 0, "e11": 0, "e20": 0, "e21": 0}
+    far = _far(core, cores, topo)
+    arrive = {"eb": len(far) * (2 if r == BOTH else 1), "e0": 0, "e10": 0, "e11": 0, "e20": 0, "e21": 0}
     for s in cores:
         if s != core:
             arrive["e0"] += len(_plan0(s, cores, topo).get(core, []))
@@ -343,30 +160,233 @@ def rank_program(g, core, T, topo):
         need(qn, (sem, arrive[sem]), *toks)
         cnt[sem] = arrive[sem]
 
-    def did(d):
-        rid, pid, _ = topo.addr(d)
-        return DstId(rid=rid, pnc=pid)
+    def load(qn, out, in_, sem):
+        return done(queue[qn].dma_start(out, in_), sem, 16)
 
-    for wide in (False, True):
-        groups = {}
-        for d, e in _plan0(core, cores, topo).items():
-            if (T.rank_of(d) in WIDE) == wide:
-                groups.setdefault(tuple(e), []).append(d)
-        if groups:
-            need("g", k["own" if wide else "e16"])
-            src = T.mi[:, mo + r:mo + r + 1] if wide else T.e16[:, 0:1]
-            dst = {d: T.mi[:, 4 - j + r:5 - j + r] if wide else T.m16[:, r:r + 1] for j, d in enumerate(cores)}
-            g.remote_dma_fused([RemoteDMATransfer(dst_ids=[did(d) for d in ds], dma_engine_mask=_mask(e),
-                                                  remote_sem=T.sem.e0, srcs=[src], dsts=[dst[d] for d in ds])
-                                for e, ds in groups.items()], local_sem=T.sem.l0)
-            cnt["l0"] = cnt.get("l0", 0) + sum(len(e) for e in groups)
-    if r < N - 1:
-        need("y", ("l0", cnt["l0"]))
-        dv = later_loads()
+    if r < N - 1 or r > BOTH:
+        dxb = load("y", T.xb[:, 0:16], T.x[:, 0:16] if r > BOTH else T.x[:, 2032:2048], "dxb")
+        V(ms, T.xb[:, 16:512], 0.0)
+    dp = load("s", T.pt[:, 0:64], T.p[:, 0:64], "dp")
+    dx = {i: load("y", T.xs[:, 512 * i:512 * i + 512], T.x[:, 512 * i:512 * i + 512], "dx%d" % i) for i in (1, 3, 0, 2)}
 
     out, back = _parts(core, cores, topo, -1), _parts(core, cores, topo, 1)
     na, nx = len(out[0]), len(back[0])
-    kzero = io(T.ct[:, 64 * na:64 * na + 320], [[0, 320]], 0, 0)
+    c0 = 3.5 - (r + 1)
+    kio = io(T.io32[:], [[1, 32]], 0, 0)
+    for i, shift in enumerate((7, 9, 10, 2)):
+        kpi = io(T.pi[:, i:i + 1], [[1, 1]], 0, 1 << shift)
+    ktr = io(T.trash[:], [[1, 32]], GAP, GAP)
+    kp0 = V(ms, T.pt[:, 64:128], 0.0)
+    c = V(ms, T.reset[:], 0.0)
+    V(ms, T.z[:, 31:224:32], 0.0)
+    V(ms, T.one2[:], 1.0)
+    V(ms, T.reset[:, 0:128:16], -5e29, w=(c,))
+
+    def fill(out, n, number):
+        return si(out, T.io32[:, 0:n], number, 0.0, w=(kio,))
+
+    for out_, n, number in ((T.dd[:, 0:8], 8, 1.0), (T.dd[:, 8:9], 1, 4.0), (T.dd[:, 9:11], 2, 1.0),
+                            (T.md[:, 8:9], 1, 4.0 * c0), (T.md[:, 9:10], 1, ROUND), (T.md[:, 10:11], 1, -ROUND),
+                            (T.cw[:, 128:160], 32, 0.0), (T.dz[:], 32, 0.0), (T.cx[:, 32:40], 8, 0.0)):
+        kdz = fill(out_, n, number)
+
+    kqb = V(qz, T.qb[:, 0:128], T.sb[:, 0:128], T.xb[:], w=(dxb,)) if r < N - 1 or r > BOTH else kp0
+    if r != min(BOTH, N - 1):
+        q, sq, at = (T.qx, T.sx, 512) if r < BOTH else (T.qb, T.sb, 128)
+        need("g", kqb)
+        g.remote_dma_fused([RemoteDMATransfer(dst_ids=[did(cores[r + 1 if r < BOTH else r - 1])], dma_engine_mask=_mask(es),
+                                              remote_sem=T.sem.eb, srcs=[src], dsts=[dst])
+                            for src, dst, es in ((T.qb[:, 0:4].bitcast(dt.uint8), q[:, at:at + 4].bitcast(dt.uint8), far[0::2]),
+                                                 (T.sb[:, 0:S], sq[:, at:at + S], far[1::2]))], local_sem=T.sem["lb"])
+        cnt["lb"] = len(far)
+        need("y", ("lb", cnt["lb"]))
+
+    kp = sc(T.pt[:, 256:384], T.pt[:, 0:128], w=(dp, kp0))
+    V(cp, T.pt[:, 128:256], T.pt[:, 0:128], w=(dp,))
+    V(cp, T.pt[:, 384:512], T.pt[:, 0:128])
+    kpv = V(cp, T.pt[:, 512:576], T.pt[:, 0:64])
+    c = ts(T.pj[:], T.pi[:], 0x780, None, A.bitwise_and, w=(kpi,))
+    kqp = V(qz, T.qp[:], T.sp[:], T.pt[:], w=(kpv, kp))
+    cpf = V(cp, T.pf[:], T.pj[:], w=(c,))
+    kval = io(T.vali[:], [[4, 8], [128, 8], [1024, 2]], 0, 0)
+    kypi = io(T.ypi[:], [[0, 32], [1, 4]], 0, 0)
+    kff = io(T.ff[:, 0:ROOM], [[0, ROOM]], 0, 0)
+
+    row, tcol, rh, quad = (T.pf[:, i:i + 1] for i in range(4))
+    p16, vb = T.pb[:, 4:5], T.pb[:, 7:8]
+    si(T.cap[:, 0:1], row, 0.0, 1e3, w=(cpf,))
+    si(T.pb[:, 0:1], row, 1.0, 1 / 16)
+    si(p16, row, 0.0, 1 / 128)
+    si(T.pb[:, 5:6], row, 0.0, -1 / 512)
+    si(T.pb[:, 8:9], row, 0.0, 1.0, AF.Sign)
+    kpb = si(T.pb[:, 6:7], tcol, 0.0, 1 / 512)
+    si(T.rst[:, 0:1], row, 14.0, 1 / 128)
+    si(T.rst[:, 1:2], row, 30.0, 1 / 128)
+    c = si(T.pb[:, 1:2], rh, p16, 17 / 1024, w=(kpb,))
+    c2 = si(T.pb[:, 2:3], tcol, T.pb[:, 5:6], 1 / 2048)
+    si(vb, quad, T.pb[:, 6:7], 1 / 4)
+    si(T.trash[:, 0:1], T.trash[:, 0:1], 0.0, T.pb[:, 8:9], w=(ktr,))
+    for out_, n, number in ((T.cap[:, 1:33], 32, 1e5), (T.cap[:, 33:64], 31, 1e5), (T.dm[:, 32:33], 1, 0.0),
+                            (T.ss[:, 47:48], 1, 0.0)):
+        kcap = fill(out_, n, number)
+    came = [0, 48][:2 if r == BOTH else 1 if 0 < r < BOTH else 0]
+    for a in came:
+        fill(T.an[:, a + 16:a + 48], 32, 1.0)
+        fill(T.ao[:, a:a + 16], 16, 1.0)
+        kcap = fill(T.ao[:, a + 16:a + 48], 32, 0.0)
+    c = si(T.rab[:], T.io32[:, 0:17], T.pb[:, 1:2], -2.0, AF.Abs, w=(c, kio))
+    krm = si(T.rm[:], T.rab[:], 0.0, 1.0, AF.Sign, w=(c,))
+
+    kqx, ksc, kch = {}, {}, {}
+
+    def scores(bank, h, a, start, stop, q=T.qx, sq=T.sx):
+        return done(ten.matmul_mx(T.ps[:, 512 * bank:512 * bank + 128], T.qp[:, 16 * h:16 * h + 128],
+                                  T.sp[:, 16 * h:16 * h + 128], q[:, a:a + 128], sq[:, a:a + 128], start, stop), "kt")
+
+    def pack(i):
+        kqx[i] = V(qz, T.qx[:, 128 * i:128 * i + 128], T.sx[:, 128 * i:128 * i + 128], T.xs[:, 512 * i:512 * i + 512],
+                   w=(dx[i],))
+        need("t", kqp, kqx[i])
+        first = i % 2 not in ksc
+        ksc[i % 2] = scores(i % 2, i // 2, 128 * i, first, not first)
+
+    def step(b, n, a=0, e=128, w=(), again=0):
+        k = slice(32 + 128 * b + a, 32 + 128 * b + e)
+        z, before = T.z[:, 64 + 160 * b + a:64 + 160 * b + e], T.z[:, 63 + 160 * b + a:63 + 160 * b + e]
+        if n == 0:
+            return V(tr, z, T.ps[:, 512 * b + a:512 * b + e], w=(ksc[b],))
+        if n == 1:
+            return V(scn, T.mx[:, k], before, T.reset[:, a:e], 0.0, A.max, A.add, w=w)
+        if n == 2:
+            return V(tt, T.nn[:, k], z, T.mx[:, k], A.is_le, w=w)
+        return V(scn, T.ss[:, 32 + again + k.start:32 + again + k.stop], T.nn[:, k], T.one2[:, a:e], 0.0,
+                 A.mult, A.add, w=w)
+
+    def slots(first, n):
+        k = 16 * (first + 4) + 15
+        return T.ss[:, k:k + 16 * (n - 1) + 1:16]
+
+    pack(1)
+    da = [load("y", T.at[:, 0:1024], T.a[:, 0:1024], "da0")]
+    dw = load("y", T.wt[:], T.w[:], "dw")
+
+    def later_loads():
+        da.append(load("y", T.at[:, 1024:2048], T.a[:, 1024:2048], "da1"))
+        return load("y", T.vt[:], T.v[:], "dv")
+
+    if r == N - 1:
+        dv = later_loads()
+    kzero = si(T.ct[:, 64 * na:64 * na + 320], T.xs[:, 512:832], 0.0, 0.0, w=(dx[1],))
+
+    pack(3)
+    pack(0)
+    ts(T.qo[:, 0:1], quad, 1 / 16, p16, A.mult, A.add, w=(kpb,))
+    c = step(1, 0)
+    pack(2)
+    if came:
+        wait("t", "eb", kqb)
+        kext = scores(3, 0, 512 + 4 - 128, True, r != BOTH)
+        if r == BOTH:
+            kext = scores(3, 1, 4, False, True, T.qb, T.sb)
+    c = step(1, 1, w=(c,))
+    ts(T.prm[:], T.io32[:, 0:8], T.pb[:, 0:1], None, A.add, w=(kpb, kio))
+    step(1, 2, 0, 64, w=(c,))
+    ca = step(0, 0, 0, 64)
+    cb = step(0, 0, 64, 128)
+    c = step(1, 2, 64, 128)
+    ca = step(0, 1, 0, 64, w=(ca,))
+    cb = step(0, 1, 64, 128, w=(cb,))
+    k1 = step(1, 3, w=(c,))
+    c2 = si(T.pb[:, 3:4], slots(15, 1), 0.0, -1.0, w=(k1,))
+    ksl = sc(slots(-1, 1), slots(14, 1))
+    kd = si(T.dz[:, 17:18], slots(14, 1), T.pb[:, 3:4], 1.0, w=(c2, kdz))
+    kval = si(T.val[:], T.vali[:], vb, 1.0, w=(kval,))
+    step(0, 2, 0, 64, w=(ca,))
+    c = step(0, 2, 64, 128, w=(cb,))
+    step(1, 3, again=256)
+    step(0, 3, w=(c,))
+    cum, inner, own, sfx = T.cw[:, 0:32], T.nc[:, 15:16], T.nb[:, 17:18], T.sf[:, 16:17]
+    m0 = r + (r > BOTH)
+    e4, r4 = T.dec[:, m0:m0 + 1], T.dec[:, m0 + 2:m0 + 3]
+    nk = 16 * len(came)
+    last, first = T.at2[:, 31:32], T.dm[:, 65:66]
+    k = {"s3": step(0, 3, again=256)}
+
+    def decode():
+        if r:
+            wait("v", "e0")
+        return V(scn, T.dec[:, 0:m0 + 3], T.dd[:, 8 - m0:11], T.md[:, 8 - m0:11], own, A.mult, A.add, w=(k["n"],))
+
+    call = {
+        "dd": lambda: V(tr, T.d32[:], T.dz[:], w=(kd,)),
+        "h2": lambda: V(tr, T.h2[:, 32:64], slots(0, 32), w=(k["s3"],)),
+        "h1": lambda: V(tr, T.h2[:, 0:32], slots(-2, 32), w=(ksl,)),
+        "fr": lambda: si(T.cw[:, 64:96], T.cw[:, 128:160], T.h2[:, 32:33], 1.0, w=(k["h2"],)),
+        "fl": lambda: V(tt, T.cw[:, 97:128], T.h2[:, 33:64], T.h2[:, 32:63], A.not_equal, w=(k["h2"],)),
+        "fb": lambda: ts(T.cw[:, 96:97], T.d32[:, 31:32], T.h2[:, 31:32], T.h2[:, 32:33], A.add, A.not_equal, w=(k["h1"],)),
+        "cs": lambda: V(scn, T.cw[:, 0:64], T.cw[:, 96:160], T.cap[:], 0.0, A.add, A.min, w=(k["fb"], kcap)),
+        "dm": lambda: V(tr, T.dm[:, 33:97], T.cw[:, 32:96], w=(k["cs"], k["fr"])),
+        "in": lambda: V(scn, T.nc[:] if came else T.nb[:, 2:18], T.one2[:, 0:16], T.dm[:, 49:65], 0.0 if r else 1.0,
+                        A.mult, A.add, w=(k["dm"],)),
+        "n": lambda: ts(own, last, first, inner, A.not_equal, A.add, w=(k["in"], k["a4"])) if came else k["in"],
+        "b0": lambda: si(T.lr[:], T.cw[:, 128:160], T.h2[:, 63:64], 1.0),
+        "b1": lambda: V(tr, T.lt[:], T.lr[:], w=(k["b0"],)),
+        "b2": lambda: ts(T.nb[:, 16:17], T.at2[:, 60:61], T.lt[:, 15:16], None, A.not_equal, w=(k["a4"], k["b1"])),
+        "a0": lambda: V(tr, T.z[:, 32:64], T.ps[:, 1536 + 96:1536 + 128], w=(kext,)),
+        "a1": lambda: V(scn, T.mx[:, 0:nk], T.z[:, 31:31 + nk], T.reset[:, 0:nk], 0.0, A.max, A.add, w=(k["a0"],)),
+        "a2": lambda: [V(tt, T.an[:, a:a + 16], T.z[:, 32 + a // 3:48 + a // 3], T.mx[:, a // 3:16 + a // 3], A.is_le,
+                         w=(k["a1"],)) for a in came][-1],
+        "a3": lambda: V(scn, T.as1[:, 0:3 * nk], T.an[:, 0:3 * nk], T.ao[:, 0:3 * nk], 0.0, A.mult, A.add, w=(k["a2"],)),
+        "a4": lambda: [V(tr, T.at2[:, 32 * i:32 * i + 32], T.as1[:, a + 16:a + 48], w=(k["a3"],))
+                       for i, a in enumerate(came)][-1],
+        "nf": lambda: si(T.nfe[:], T.cw[:, 96:128], 1.0, -1.0, w=(k["fb"],)),
+        "nd": lambda: V(tt, T.nfd[:], T.nfe[:], T.trash[:], A.mult, w=(k["nf"],)),
+        "d2": lambda: V(tr, T.dm[:, 0:32], T.cw[:, 32:64]),
+        "cx": lambda: V(tt, T.cx[:, 0:32], cum, T.nfd[:], A.max, w=(k["nd"],)),
+        "sf": lambda: V(scn, T.sf[:], T.rm[:], T.dm[:, 16:50:2], 0.0, A.mult, A.add, w=(k["d2"], krm)),
+        "ol": lambda: ts(T.offl[:], T.cx[:, 0:40].indirect(T.qo[:, 0:1]), sfx, 128.0, A.subtract, A.add,
+                         w=(k["cx"], k["sf"])),
+        "ff": lambda: V(cp, T.ff[:, 0:FW].indirect(T.offl[:, 0:8]), T.val[:], w=(k["ol"], kff, kval)),
+        "mk": lambda: V(tt, T.mk[:], T.ff[:, 0:ROOM].indirect(T.prm[:, 0:8]), T.msk[:], A.mult, w=(k["ff"], kmsk)),
+        "sg": lambda: V(scn, T.sg[:], T.d0[:], T.mk[:], 0.0, A.mult, A.add, w=(k["mk"],)),
+        "xh": lambda: [V(tt, T.xh[0:64, a:a + 32], T.sg[0:64, 3:128:4], T.sg[64:128, 3:128:4], A.add, w=(k["sg"],))
+                       for a in (0, 32)][-1],
+        "uu": lambda: V(tt, T.uu[0:32, 0:60], T.xh[0:32, 0:60], T.xh[32:64, 0:60], A.add, w=(k["xh"],)),
+        "u1": lambda: vc(T.uu[32:64, 0:60], T.uu[0:32, 0:60], w=(k["uu"],)),
+        "u2": lambda: sc(T.uu[64:96, 0:60], T.uu[0:32, 0:60], w=(k["uu"],)),
+        "u3": lambda: vc(T.uu[96:128, 0:60], T.uu[0:32, 0:60], w=(k["uu"],)),
+        "dec": decode,
+        "ro": lambda: ts(T.ro[:], T.rst[:], e4, r4, A.subtract, A.add, w=(k["dec"],)),
+        "lst": lambda: V(cp, T.lst[:], T.uu[:, 0:60].indirect(T.ro[:, 0:2]), w=(k["ro"], k["u2"], k["u3"])),
+    }
+
+    def run(names):
+        for name in names.split():
+            if len(came) > "ab".find(name[0]):
+                k[name] = call[name]()
+
+    run("dd h2 h1 a0 fr b0 fl fb nf a1 cs a2 dm b1 a3 in a4 d2 b2 n nd sf cx ol" if r == BOTH else
+        "dd h2 h1 a0 fr fl fb nf a1 cs a2 dm d2 a3 in nd a4 sf n cx ol" if r < N - 1 else
+        "dd h2 h1 fr fl fb nf cs dm d2 nd sf cx in ol")
+
+    c = si(T.yab[:], T.ypi[:], T.pb[:, 2:3], 1.0, AF.Abs, w=(kypi,))
+    si(T.d0[:], T.ypi[:], 0.0, 1.0, AF.Sign)
+    kmsk = si(T.msk[:], T.yab[:], 1.0, -1.0, AF.Relu, w=(c,))
+
+    if r < N - 1:
+        groups = {}
+        for d, e in _plan0(core, cores, topo).items():
+            groups.setdefault(tuple(e), []).append(d)
+        need("g", k["n"])
+        dst = {d: T.md[:, 8 - min(j, BOTH) + r:9 - min(j, BOTH) + r] for j, d in enumerate(cores) if j > r}
+        if r == BOTH:
+            dst = {cores[r + 1]: T.md[:, 0:2]}
+        g.remote_dma_fused([RemoteDMATransfer(dst_ids=[did(d) for d in ds], dma_engine_mask=_mask(e), remote_sem=T.sem.e0,
+                                              srcs=[T.nb[:, 16:18] if r == BOTH else own], dsts=[dst[d] for d in ds])
+                            for e, ds in groups.items()], local_sem=T.sem.l0)
+        cnt["l0"] = sum(len(e) for e in groups)
+        need("y", ("l0", cnt["l0"]))
+        dv = later_loads()
 
     def exchange(part, step, codes, plane, first, width, rsem, lsem):
         for scales in (0, 1):
@@ -383,16 +403,8 @@ def rank_program(g, core, T, topo):
                 cnt[lsem] = cnt.get(lsem, 0) + len(es[scales])
             g.remote_dma_fused(tl, local_sem=T.sem[lsem])
 
-    run("of ol ff fo" if r < 2 else "of ol own ff fo")
-    rest = "mk sg uh ut us uu u2,u3".split()
-    steps = ("mi,la,c7 ne,cf sb ro" if r in WIDE else "mi la,c7 ne,cf sb ro").split()
-    ahead = AHEAD[list(_plan0(cores[1], cores, topo)).index(core) + 2 if r > 1 else r]
-    run(" ".join(rest[:ahead]).replace(",", " "))
-    for i in range(max(len(steps), len(rest) - ahead)):
-        run(" ".join(steps[i:i + 1] + rest[ahead + i:ahead + i + 1]).replace(",", " "))
-    run("lst")
+    run("ff mk sg xh uu u2 u1 dec u3 ro lst" if r < N - 1 else "a0 ff a1 mk a2 sg a3 xh a4 uu u2 u1 n u3 dec ro lst")
     klst = k["lst"]
-
 
     def product(bank, codes, plane, a, n=NC):
         (lq, rq), (ls, rs) = codes, plane
@@ -418,30 +430,30 @@ def rank_program(g, core, T, topo):
         return V(qz, T.qa[:, 128 * i:128 * i + 128], T.sa[:, 128 * i:128 * i + 128], T.at[:, 512 * i:512 * i + 512],
                  w=(da[i // 2],))
 
-    si(T.nhs[:], T.hs[:], -256.0 - r, -1.0)
-    for h in (0, 1):
-        klab = si(T.tcs[:, 32 + 8 * h:40 + 8 * h], slots(h, 8, 2), 16.0, -1.0)
-        V(tt, T.tcs[:, 8 * h:8 * h + 8], T.cct[:, 34 + h:50:2], before[h], A.add)
-    c = ts(T.ci[:, 0:r + 1], mi, 4, 255, A.logical_shift_right, A.bitwise_and)
+    c = si(T.ec[:, 0:1], sfx, 0.0, -1.0)
+    kec = si(T.ec[:, 1:2], e4, -c0 - 1.0, 0.25)
+    si(T.ec[:, 2:3], e4, -c0 - 1.0 - r - 2048.0, 0.25)
+    klab = si(T.lab[:], T.h2[:, 32:64], 16.0, -1.0)
+    for i in range(4):
+        kcp = si(T.cd[:, 16 * i:16 * i + 16], T.cw[:, 16 * (i // 2):16 * (i // 2) + 16], T.ec[:, 0:1], 1.0, w=(c,))
     kqw = V(qz, T.qw[:], T.sw[:], T.wt[:], w=(dw,))
     need("t", kqw, *kqx.values())
     kwx = product(2, (T.qw[:], T.qx), (T.sw[:], T.sx), 0, 512)
-    kcd = V(tr, T.cdw[:], T.tcs[:], w=(c, klab))
-    c = V(cp, T.cif[:, 0:r + 1], T.ci[:, 0:r + 1])
     kqa = [pack_a(0)]
-    for i in range(4):
-        kcp = si(T.cd[:, 16 * i:16 * i + 16], T.cdw[:, 16 * (i // 2):16 * (i // 2) + 16], T.nhs[:], 1.0, w=(kcd, klab))
     kwxs = sc(T.wx[:, 0:CUT], T.ps[:, 1024:1024 + CUT], w=(kwx,))
-    if r:
-        ts(T.nx[:], T.ne[:, r - 1:r], 200.0, T.cif[:, r:r + 1], A.mult, A.add, w=(c,))
+    if came:
+        c = ts(T.nx[:, 1:2], own, inner, 999.0, A.subtract, A.mult)
+        ts(T.nx[:, 0:1], T.nx[:, 1:2], inner, None, A.add, w=(c,))
+    elif r:
+        ts(T.nx[:, 0:1], T.md[:, 0:1], 999.0, own, A.mult, A.add)
     else:
-        V(ms, T.nx[:], 999.0)
-    c = V(scn, T.sbb[:, 0:r + 1], T.cif[:, 0:r + 1], T.ne[:, 0:r + 1], -128.0, A.add, A.add, w=(c,))
+        V(ms, T.nx[:, 0:1], 999.0)
+    klb1 = ts(T.lb1[:], cum, sfx, T.ec[:, 1:2], A.subtract, A.add, w=(kec,))
     kqa.append(pack_a(1))
-    klb1 = ts(T.lb1[:], T.cdw[:, 0:32], T.hs[:], sbb, A.subtract, A.add, w=(c,))
-    need("y", klb1)
-    done(syn.dma_start(T.lb[0:1, :], T.cdw[0:16, 32:64]), "dl0", 16)
-    done(syn.dma_start(T.lb[1:2, :], T.lb1[0:16, :]), "dl1", 16)
+    need("y", klb1, klab)
+    for h in (0, 1):
+        done(syn.dma_start(T.lb[0:1, 256 * h:256 * h + 256], T.lab[h:16:2, :]), "dl0", 16)
+        done(syn.dma_start(T.lb[1:2, 256 * h:256 * h + 256], T.lb1[h:16:2, :]), "dl1", 16)
     kqa += [pack_a(2), pack_a(3)]
 
     wide = [S * (nx + 1), NC - S * (nx + 1) + 2]
@@ -469,16 +481,17 @@ def rank_program(g, core, T, topo):
     vq, vs = (T.qv[:], T.qh), (T.sv[:], T.sh)
     need("t", kqv)
     m = product(3, vq, vs, 0)
-    c = ts(T.t1[:], T.tc[:], sb, -1.0, A.add, A.mult, w=(c,))
-    ts(T.ii[:], T.tc[:], 0.125, 0.4375 + 0.125 * (256 + r), A.mult, A.add)
-    c2 = ts(T.fx[:], T.tc[:], T.nx[:], -128.0 - r, A.add, A.not_equal)
+    c = ts(T.t1[:], T.tc[:], T.ec[:, 2:3], -1.0, A.add, A.mult, w=(c,))
+    ts(T.ii[:], T.tc[:], 0.125, 0.5625 + 0.125 * 127, A.mult, A.add)
+    c2 = ts(T.fx[:], T.tc[:], T.nx[:, 0:1], 0.0, A.add, A.not_equal)
     c = ts(T.kk[:], T.t1[:], 7, None, A.bitwise_and, w=(c,))
     c2 = V(tt, T.s1[:], T.ii[:], T.fx[:], A.mult, w=(c2,))
     c = ts(T.k18[:], T.kk[:], float(S2), 1.0, A.mult, A.add, w=(c,))
     V(cp, T.vw[:, 2:S2], T.ps[:, 1536:1536 + S], w=(m,))
     c = V(tt, T.s2[:], T.s1[:], T.k18[:], A.add, w=(c, c2))
-    V(cp, T.fin[:, 0:32:2], T.s2[:, 0:16], w=(c,))
-    kfin = V(cp, T.fin[:, 1:32:2], T.s2[:, 32:48])
+    for h in (0, 1):
+        for u in (0, 1):
+            kfin = V(cp, T.fin[:, 16 * h + u:16 * h + 16:2], T.s2[:, 32 * u + h:32 * u + 16:2], w=(c,))
     n = S2 * na
     wait("t", "e20")
     m = product(6, vq, vs, NC + n)

from concourse.bass import DstId, RemoteDMATransfer
from concourse.mybir import dt, AluOpType, AxisListType, ActivationFunctionType

N = 8
S = 16
S2 = 18
NC = N * S
ROOM = 136
GAP = 160
FW = 130 * GAP
BOTH = N - 2
CUT = 320
ROUND = 1.5 * 2.0 ** 28

F32, BF, I32, U16, C8, U8 = "float32", "bfloat16", "int32", "uint16", "float8_e4m3fn_x4", "uint8"


def _sb(n, d):
    return ("sbuf", [128, n], d)


SCRATCH = {
    "ps": ("psum", [128, 4096], F32),
    "xs": _sb(2048, BF), "pt": _sb(576, BF), "at": _sb(2048, BF), "wt": _sb(512, BF), "vt": _sb(512, BF),
    "qx": _sb(512 + S, C8), "sx": _sb(512 + S, U8), "qp": _sb(144, C8), "sp": _sb(144, U8),
    "qa": _sb(512, C8), "sa": _sb(512, U8), "qw": _sb(128, C8), "sw": _sb(128, U8), "qv": _sb(128, C8), "sv": _sb(128, U8),
    "ct": _sb(832, BF), "qc": _sb(2 * NC + 112, C8), "sc": _sb(2 * NC + 112, U8),
    "ht": _sb(896, BF), "qh": _sb(2 * NC + 126, C8), "sh": _sb(2 * NC + 126, U8),
    "pi": _sb(4, I32), "pj": _sb(4, I32), "pf": _sb(4, F32), "io32": _sb(32, F32), "trash": _sb(32, F32),
    "vali": _sb(128, F32), "val": _sb(128, F32), "prm": _sb(8, U16), "ypi": _sb(128, F32), "yab": _sb(128, F32),
    "msk": _sb(128, F32), "d0": _sb(128, F32), "pb": _sb(9, F32), "qo": _sb(2, U16), "cap": _sb(64, F32),
    "rst": _sb(2, F32), "reset": _sb(128, F32), "one2": _sb(128, BF), "rab": _sb(17, F32), "rm": _sb(17, F32),
    "dd": _sb(16, BF), "an": _sb(96, BF), "ao": _sb(96, BF), "as1": _sb(96, F32), "at2": _sb(64, F32),
    "xb": _sb(512, BF), "qb": _sb(128 + S, C8), "sb": _sb(128 + S, U8), "lr": _sb(32, F32), "lt": _sb(32, F32),
    "z": _sb(352, F32), "mx": _sb(288, F32), "nn": _sb(288, BF), "ss": _sb(576, BF), "h2": _sb(64, BF),
    "dz": _sb(32, BF), "d32": _sb(32, BF), "cw": _sb(160, F32), "dm": _sb(97, F32), "nb": _sb(18, BF), "nc": _sb(16, F32), "sf": _sb(17, F32),
    "nfe": _sb(32, F32), "nfd": _sb(32, F32), "cx": _sb(40, F32), "offl": _sb(16, U16), "ff": _sb(FW, F32),
    "mk": _sb(128, F32), "sg": _sb(128, F32), "xh": _sb(64, F32), "uu": _sb(64, F32),
    "md": _sb(16, BF), "dec": _sb(12, F32), "ro": _sb(2, U16), "lst": _sb(32, U16), "ec": _sb(3, F32), "nx": _sb(2, F32),
    "cd": _sb(64, F32), "lab": _sb(32, F32), "lb1": _sb(32, F32),
    "tc": _sb(64, F32), "ii": _sb(64, I32), "t1": _sb(64, I32), "kk": _sb(64, I32), "k18": _sb(64, F32), "fx": _sb(64, F32),
    "s1": _sb(64, F32), "s2": _sb(64, F32), "fin": _sb(32, U16),
    "wx": _sb(CUT, F32), "vw": _sb(N * S2, F32), "yt": _sb(512, F32), "yg": _sb(512 - CUT, F32),
}
SEMAPHORES = ["kv", "ks", "kt", "kg", "dp", "dxb", "dx0", "dx1", "dx2", "dx3", "da0", "da1", "dw", "dv",
              "dl0", "dl1", "eb", "e0", "e10", "e11", "e20", "e21", "lb", "l0", "l1", "l2", "dy0", "dy1", "dy2"]


def _mask(es):
    return sum(1 << e for e in es)


def _far(core, cores, topo):
    return [topo.engines(core, d) for d in cores if topo.chip(d) != topo.chip(core)][0]


def _near(core, d, off_engines, topo):
    return [e for e in topo.engines(core, d) if e not in off_engines][::2]


def _early(core, cores, topo):
    r = cores.index(core)
    order = [cores[r - i] for i in range(1, len(cores))]
    off = [d for d in order if topo.chip(d) != topo.chip(core)]
    return order[:order.index(off[1 if r == len(cores) - 1 else 3]) + 1]


def _parts(core, cores, topo, step):
    r = cores.index(core)
    order = [cores[(r + step * i) % len(cores)] for i in range(1, len(cores))]
    parts = []
    for first in (True, False):
        ds = [d for d in order if first == (d in _early(core, cores, topo) if step < 0 else core in _early(d, cores, topo))]
        off = [d for d in ds if topo.chip(d) != topo.chip(core)]
        eo = topo.engines(core, off[0])
        a, b, n = eo[0::2], eo[1::2], len(eo) // len(off)
        shares = [(a[:2], b[:2]), (a[2:], b[2:]), (b, a)] if len(off) == 3 else [(eo[n * i:][:n],) * 2 for i in range(len(off))]
        parts.append({d: shares[off.index(d)] if d in off else (_near(core, d, eo, topo)[:2 if first else 4],) * 2
                      for d in ds})
    return parts


def _alone(core, cores, topo):
    return all(topo.chip(d) == topo.chip(core) for d in cores[cores.index(core) + 1:])


def _beside(core, cores, topo):
    return any(topo.chip(d) == topo.chip(core) for d in cores[cores.index(core) + 1:])


def _plan0(core, cores, topo):
    ch = topo.chip(core)
    eo = _far(core, cores, topo)
    later = cores[cores.index(core) + 1:]
    return {d: _near(core, d, eo, topo)[:2] if topo.chip(d) == ch and core == cores[0] else eo for d in later}


def rank_program(g, core, T, topo):
    r = T.rank_of(core)
    if r is None:
        return
    A, AF = AluOpType, ActivationFunctionType
    cores = list(T.cores)
    vec, sca, ten, syn = g.vector, g.scalar, g.tensor, g.sync
    queue = {"v": vec, "s": sca, "t": ten, "g": g, "y": syn}
    cnt, known = {}, {}

    def done(ins, sem, n=1):
        ins.then_inc(T.sem[sem], n)
        cnt[sem] = cnt.get(sem, 0) + n
        return (sem, cnt[sem])

    def need(qn, *toks):
        for s, v in toks:
            if known.get((qn, s), 0) < v:
                queue[qn].wait_ge(T.sem[s], v)
                known[(qn, s)] = v

    def V(f, *args, w=()):
        need("v", *w)
        return done(f(*args), "kv")

    def ts(out, i, a, b, o0, o1=None, w=()):
        need("v", *w)
        if o1 is None:
            return done(vec.tensor_scalar(out, i, a, None, o0), "kv")
        return done(vec.tensor_scalar(out, i, a, b, o0, o1), "kv")

    def io(out, pattern, base, cm):
        return done(g.iota(out, pattern, base, cm, allow_small_or_imprecise_dtypes=True), "kg")

    def sc(out, in_, w=()):
        need("s", *w)
        return done(sca.activation(out, in_, AF.Copy), "ks")

    def si(out, in_, bias, scale, func=AF.Identity, w=()):
        need("s", *w)
        return done(sca.activation(out, in_, func, bias, scale), "ks")

    tt, cp, ms, scn, tr, qz = (vec.tensor_tensor, vec.tensor_copy, vec.memset, vec.tensor_tensor_scan, vec.transpose,
                               vec.quantize_mx)

    def vc(out, in_, w=()):
        return V(cp, out, in_, w=w)

    def did(d):
        rid, pid, _ = topo.addr(d)
        return DstId(rid=rid, pnc=pid)

    far = _far(core, cores, topo)
    arrive = {"eb": len(far) * (2 if r == BOTH else 1), "e0": 0, "e10": 0, "e11": 0, "e20": 0, "e21": 0}
    for s in cores:
        if s != core:
            arrive["e0"] += len(_plan0(s, cores, topo).get(core, []))
            for name, step in (("e1", -1), ("e2", 1)):
                for h, part in enumerate(_parts(s, cores, topo, step)):
                    arrive[name + str(h)] += sum(len(es) for es in part.get(core, ()))

    def wait(qn, sem, *toks):
        need(qn, (sem, arrive[sem]), *toks)
        cnt[sem] = arrive[sem]

    def load(qn, out, in_, sem):
        return done(queue[qn].dma_start(out, in_), sem, 16)

    if r < N - 1 or r > BOTH:
        dxb = load("y", T.xb[:, 0:16], T.x[:, 0:16] if r > BOTH else T.x[:, 2032:2048], "dxb")
        V(ms, T.xb[:, 16:512], 0.0)
    dp = load("s", T.pt[:, 0:64], T.p[:, 0:64], "dp")
    dx = {i: load("y", T.xs[:, 512 * i:512 * i + 512], T.x[:, 512 * i:512 * i + 512], "dx%d" % i) for i in (1, 3, 0, 2)}

    out, back = _parts(core, cores, topo, -1), _parts(core, cores, topo, 1)
    na, nx = len(out[0]), len(back[0])
    c0 = 3.5 - (r + 1)
    kio = io(T.io32[:], [[1, 32]], 0, 0)
    for i, shift in enumerate((7, 9, 10, 2)):
        kpi = io(T.pi[:, i:i + 1], [[1, 1]], 0, 1 << shift)
    ktr = io(T.trash[:], [[1, 32]], GAP, GAP)
    kp0 = V(ms, T.pt[:, 64:128], 0.0)
    c = V(ms, T.reset[:], 0.0)
    V(ms, T.z[:, 31:224:32], 0.0)
    V(ms, T.one2[:], 1.0)
    V(ms, T.reset[:, 0:128:16], -5e29, w=(c,))

    def fill(out, n, number):
        return si(out, T.io32[:, 0:n], number, 0.0, w=(kio,))

    for out_, n, number in ((T.dd[:, 0:8], 8, 1.0), (T.dd[:, 8:9], 1, 4.0), (T.dd[:, 9:11], 2, 1.0),
                            (T.md[:, 8:9], 1, 4.0 * c0), (T.md[:, 9:10], 1, ROUND), (T.md[:, 10:11], 1, -ROUND),
                            (T.cw[:, 128:160], 32, 0.0), (T.dz[:], 32, 0.0), (T.cx[:, 32:40], 8, 0.0)):
        kdz = fill(out_, n, number)

    kqb = V(qz, T.qb[:, 0:128], T.sb[:, 0:128], T.xb[:], w=(dxb,)) if r < N - 1 or r > BOTH else kp0
    if r != min(BOTH, N - 1):
        q, sq, at = (T.qx, T.sx, 512) if r < BOTH else (T.qb, T.sb, 128)
        need("g", kqb)
        g.remote_dma_fused([RemoteDMATransfer(dst_ids=[did(cores[r + 1 if r < BOTH else r - 1])], dma_engine_mask=_mask(es),
                                              remote_sem=T.sem.eb, srcs=[src], dsts=[dst])
                            for src, dst, es in ((T.qb[:, 0:4].bitcast(dt.uint8), q[:, at:at + 4].bitcast(dt.uint8), far[0::2]),
                                                 (T.sb[:, 0:S], sq[:, at:at + S], far[1::2]))], local_sem=T.sem["lb"])
        cnt["lb"] = len(far)
        need("y", ("lb", cnt["lb"]))

    kp = sc(T.pt[:, 256:384], T.pt[:, 0:128], w=(dp, kp0))
    V(cp, T.pt[:, 128:256], T.pt[:, 0:128], w=(dp,))
    V(cp, T.pt[:, 384:512], T.pt[:, 0:128])
    kpv = V(cp, T.pt[:, 512:576], T.pt[:, 0:64])
    c = ts(T.pj[:], T.pi[:], 0x780, None, A.bitwise_and, w=(kpi,))
    kqp = V(qz, T.qp[:], T.sp[:], T.pt[:], w=(kpv, kp))
    cpf = V(cp, T.pf[:], T.pj[:], w=(c,))
    kval = io(T.vali[:], [[4, 8], [128, 8], [1024, 2]], 0, 0)
    kypi = io(T.ypi[:], [[0, 32], [1, 4]], 0, 0)
    kff = io(T.ff[:, 0:ROOM], [[0, ROOM]], 0, 0)

    row, tcol, rh, quad = (T.pf[:, i:i + 1] for i in range(4))
    p16, vb = T.pb[:, 4:5], T.pb[:, 7:8]
    si(T.cap[:, 0:1], row, 0.0, 1e3, w=(cpf,))
    si(T.pb[:, 0:1], row, 1.0, 1 / 16)
    si(p16, row, 0.0, 1 / 128)
    si(T.pb[:, 5:6], row, 0.0, -1 / 512)
    si(T.pb[:, 8:9], row, 0.0, 1.0, AF.Sign)
    kpb = si(T.pb[:, 6:7], tcol, 0.0, 1 / 512)
    si(T.rst[:, 0:1], row, 14.0, 1 / 128)
    si(T.rst[:, 1:2], row, 30.0, 1 / 128)
    c = si(T.pb[:, 1:2], rh, p16, 17 / 1024, w=(kpb,))
    c2 = si(T.pb[:, 2:3], tcol, T.pb[:, 5:6], 1 / 2048)
    si(vb, quad, T.pb[:, 6:7], 1 / 4)
    si(T.trash[:, 0:1], T.trash[:, 0:1], 0.0, T.pb[:, 8:9], w=(ktr,))
    for out_, n, number in ((T.cap[:, 1:33], 32, 1e5), (T.cap[:, 33:64], 31, 1e5), (T.dm[:, 32:33], 1, 0.0),
                            (T.ss[:, 47:48], 1, 0.0)):
        kcap = fill(out_, n, number)
    came = [0, 48][:2 if r == BOTH else 1 if 0 < r < BOTH else 0]
    for a in came:
        fill(T.an[:, a + 16:a + 48], 32, 1.0)
        fill(T.ao[:, a:a + 16], 16, 1.0)
        kcap = fill(T.ao[:, a + 16:a + 48], 32, 0.0)
    c = si(T.rab[:], T.io32[:, 0:17], T.pb[:, 1:2], -2.0, AF.Abs, w=(c, kio))
    krm = si(T.rm[:], T.rab[:], 0.0, 1.0, AF.Sign, w=(c,))

    kqx, ksc, kch = {}, {}, {}

    def scores(bank, h, a, start, stop, q=T.qx, sq=T.sx):
        return done(ten.matmul_mx(T.ps[:, 512 * bank:512 * bank + 128], T.qp[:, 16 * h:16 * h + 128],
                                  T.sp[:, 16 * h:16 * h + 128], q[:, a:a + 128], sq[:, a:a + 128], start, stop), "kt")

    def pack(i):
        kqx[i] = V(qz, T.qx[:, 128 * i:128 * i + 128], T.sx[:, 128 * i:128 * i + 128], T.xs[:, 512 * i:512 * i + 512],
                   w=(dx[i],))
        need("t", kqp, kqx[i])
        first = i % 2 not in ksc
        ksc[i % 2] = scores(i % 2, i // 2, 128 * i, first, not first)

    def step(b, n, a=0, e=128, w=(), again=0):
        k = slice(32 + 128 * b + a, 32 + 128 * b + e)
        z, before = T.z[:, 64 + 160 * b + a:64 + 160 * b + e], T.z[:, 63 + 160 * b + a:63 + 160 * b + e]
        if n == 0:
            return V(tr, z, T.ps[:, 512 * b + a:512 * b + e], w=(ksc[b],))
        if n == 1:
            return V(scn, T.mx[:, k], before, T.reset[:, a:e], 0.0, A.max, A.add, w=w)
        if n == 2:
            return V(tt, T.nn[:, k], z, T.mx[:, k], A.is_le, w=w)
        return V(scn, T.ss[:, 32 + again + k.start:32 + again + k.stop], T.nn[:, k], T.one2[:, a:e], 0.0,
                 A.mult, A.add, w=w)

    def slots(first, n):
        k = 16 * (first + 4) + 15
        return T.ss[:, k:k + 16 * (n - 1) + 1:16]

    pack(1)
    da = [load("y", T.at[:, 0:1024], T.a[:, 0:1024], "da0")]
    dw = load("y", T.wt[:], T.w[:], "dw")

    def later_loads():
        da.append(load("y", T.at[:, 1024:2048], T.a[:, 1024:2048], "da1"))
        return load("y", T.vt[:], T.v[:], "dv")

    if r == N - 1:
        dv = later_loads()
    kzero = si(T.ct[:, 64 * na:64 * na + 320], T.xs[:, 512:832], 0.0, 0.0, w=(dx[1],))

    pack(3)
    pack(0)
    ts(T.qo[:, 0:1], quad, 1 / 16, p16, A.mult, A.add, w=(kpb,))
    c = step(1, 0)
    pack(2)
    if came:
        wait("t", "eb", kqb)
        kext = scores(3, 0, 512 + 4 - 128, True, r != BOTH)
        if r == BOTH:
            kext = scores(3, 1, 4, False, True, T.qb, T.sb)
    c = step(1, 1, w=(c,))
    ts(T.prm[:], T.io32[:, 0:8], T.pb[:, 0:1], None, A.add, w=(kpb, kio))
    step(1, 2, 0, 64, w=(c,))
    ca = step(0, 0, 0, 64)
    cb = step(0, 0, 64, 128)
    c = step(1, 2, 64, 128)
    ca = step(0, 1, 0, 64, w=(ca,))
    cb = step(0, 1, 64, 128, w=(cb,))
    k1 = step(1, 3, w=(c,))
    c2 = si(T.pb[:, 3:4], slots(15, 1), 0.0, -1.0, w=(k1,))
    ksl = sc(slots(-1, 1), slots(14, 1))
    kd = si(T.dz[:, 17:18], slots(14, 1), T.pb[:, 3:4], 1.0, w=(c2, kdz))
    kval = si(T.val[:], T.vali[:], vb, 1.0, w=(kval,))
    step(0, 2, 0, 64, w=(ca,))
    c = step(0, 2, 64, 128, w=(cb,))
    step(1, 3, again=256)
    step(0, 3, w=(c,))
    cum, inner, own, sfx = T.cw[:, 0:32], T.nc[:, 15:16], T.nb[:, 17:18], T.sf[:, 16:17]
    m0 = r + (r > BOTH)
    e4, r4 = T.dec[:, m0:m0 + 1], T.dec[:, m0 + 2:m0 + 3]
    nk = 16 * len(came)
    last, first = T.at2[:, 31:32], T.dm[:, 65:66]
    k = {"s3": step(0, 3, again=256)}

    def decode():
        if r:
            wait("v", "e0")
        return V(scn, T.dec[:, 0:m0 + 3], T.dd[:, 8 - m0:11], T.md[:, 8 - m0:11], own, A.mult, A.add, w=(k["n"],))

    call = {
        "dd": lambda: V(tr, T.d32[:], T.dz[:], w=(kd,)),
        "h2": lambda: V(tr, T.h2[:, 32:64], slots(0, 32), w=(k["s3"],)),
        "h1": lambda: V(tr, T.h2[:, 0:32], slots(-2, 32), w=(ksl,)),
        "fr": lambda: si(T.cw[:, 64:96], T.cw[:, 128:160], T.h2[:, 32:33], 1.0, w=(k["h2"],)),
        "fl": lambda: V(tt, T.cw[:, 97:128], T.h2[:, 33:64], T.h2[:, 32:63], A.not_equal, w=(k["h2"],)),
        "fb": lambda: ts(T.cw[:, 96:97], T.d32[:, 31:32], T.h2[:, 31:32], T.h2[:, 32:33], A.add, A.not_equal, w=(k["h1"],)),
        "cs": lambda: V(scn, T.cw[:, 0:64], T.cw[:, 96:160], T.cap[:], 0.0, A.add, A.min, w=(k["fb"], kcap)),
        "dm": lambda: V(tr, T.dm[:, 33:97], T.cw[:, 32:96], w=(k["cs"], k["fr"])),
        "in": lambda: V(scn, T.nc[:] if came else T.nb[:, 2:18], T.one2[:, 0:16], T.dm[:, 49:65], 0.0 if r else 1.0,
                        A.mult, A.add, w=(k["dm"],)),
        "n": lambda: ts(own, last, first, inner, A.not_equal, A.add, w=(k["in"], k["a4"])) if came else k["in"],
        "b0": lambda: si(T.lr[:], T.cw[:, 128:160], T.h2[:, 63:64], 1.0),
        "b1": lambda: V(tr, T.lt[:], T.lr[:], w=(k["b0"],)),
        "b2": lambda: ts(T.nb[:, 16:17], T.at2[:, 60:61], T.lt[:, 15:16], None, A.not_equal, w=(k["a4"], k["b1"])),
        "a0": lambda: V(tr, T.z[:, 32:64], T.ps[:, 1536 + 96:1536 + 128], w=(kext,)),
        "a1": lambda: V(scn, T.mx[:, 0:nk], T.z[:, 31:31 + nk], T.reset[:, 0:nk], 0.0, A.max, A.add, w=(k["a0"],)),
        "a2": lambda: [V(tt, T.an[:, a:a + 16], T.z[:, 32 + a // 3:48 + a // 3], T.mx[:, a // 3:16 + a // 3], A.is_le,
                         w=(k["a1"],)) for a in came][-1],
        "a3": lambda: V(scn, T.as1[:, 0:3 * nk], T.an[:, 0:3 * nk], T.ao[:, 0:3 * nk], 0.0, A.mult, A.add, w=(k["a2"],)),
        "a4": lambda: [V(tr, T.at2[:, 32 * i:32 * i + 32], T.as1[:, a + 16:a + 48], w=(k["a3"],))
                       for i, a in enumerate(came)][-1],
        "nf": lambda: si(T.nfe[:], T.cw[:, 96:128], 1.0, -1.0, w=(k["fb"],)),
        "nd": lambda: V(tt, T.nfd[:], T.nfe[:], T.trash[:], A.mult, w=(k["nf"],)),
        "d2": lambda: V(tr, T.dm[:, 0:32], T.cw[:, 32:64]),
        "cx": lambda: V(tt, T.cx[:, 0:32], cum, T.nfd[:], A.max, w=(k["nd"],)),
        "sf": lambda: V(scn, T.sf[:], T.rm[:], T.dm[:, 16:50:2], 0.0, A.mult, A.add, w=(k["d2"], krm)),
        "ol": lambda: ts(T.offl[:], T.cx[:, 0:40].indirect(T.qo[:, 0:1]), sfx, 128.0, A.subtract, A.add,
                         w=(k["cx"], k["sf"])),
        "ff": lambda: V(cp, T.ff[:, 0:FW].indirect(T.offl[:, 0:8]), T.val[:], w=(k["ol"], kff, kval)),
        "mk": lambda: V(tt, T.mk[:], T.ff[:, 0:ROOM].indirect(T.prm[:, 0:8]), T.msk[:], A.mult, w=(k["ff"], kmsk)),
        "sg": lambda: V(scn, T.sg[:], T.d0[:], T.mk[:], 0.0, A.mult, A.add, w=(k["mk"],)),
        "xh": lambda: [V(tt, T.xh[0:64, a:a + 32], T.sg[0:64, 3:128:4], T.sg[64:128, 3:128:4], A.add, w=(k["sg"],))
                       for a in (0, 32)][-1],
        "uu": lambda: V(tt, T.uu[0:32, 0:60], T.xh[0:32, 0:60], T.xh[32:64, 0:60], A.add, w=(k["xh"],)),
        "u1": lambda: vc(T.uu[32:64, 0:60], T.uu[0:32, 0:60], w=(k["uu"],)),
        "u2": lambda: sc(T.uu[64:96, 0:60], T.uu[0:32, 0:60], w=(k["uu"],)),
        "u3": lambda: vc(T.uu[96:128, 0:60], T.uu[0:32, 0:60], w=(k["uu"],)),
        "dec": decode,
        "ro": lambda: ts(T.ro[:], T.rst[:], e4, r4, A.subtract, A.add, w=(k["dec"],)),
        "lst": lambda: V(cp, T.lst[:], T.uu[:, 0:60].indirect(T.ro[:, 0:2]), w=(k["ro"], k["u2"], k["u3"])),
    }

    def run(names):
        for name in names.split():
            if len(came) > "ab".find(name[0]):
                k[name] = call[name]()

    run("dd h2 h1 a0 fr b0 fl fb nf a1 cs a2 dm b1 a3 in a4 d2 b2 n nd sf cx ol" if r == BOTH else
        "dd h2 h1 a0 fr fl fb nf a1 cs a2 dm d2 a3 in nd a4 sf n cx ol" if r < N - 1 else
        "dd h2 h1 fr fl fb nf cs dm d2 nd sf cx in ol")

    c = si(T.yab[:], T.ypi[:], T.pb[:, 2:3], 1.0, AF.Abs, w=(kypi,))
    si(T.d0[:], T.ypi[:], 0.0, 1.0, AF.Sign)
    kmsk = si(T.msk[:], T.yab[:], 1.0, -1.0, AF.Relu, w=(c,))

    if r < N - 1:
        groups = {}
        for d, e in _plan0(core, cores, topo).items():
            groups.setdefault(tuple(e), []).append(d)
        need("g", k["n"])
        dst = {d: T.md[:, 8 - min(j, BOTH) + r:9 - min(j, BOTH) + r] for j, d in enumerate(cores) if j > r}
        if r == BOTH:
            dst = {cores[r + 1]: T.md[:, 0:2]}
        g.remote_dma_fused([RemoteDMATransfer(dst_ids=[did(d) for d in ds], dma_engine_mask=_mask(e), remote_sem=T.sem.e0,
                                              srcs=[T.nb[:, 16:18] if r == BOTH else own], dsts=[dst[d] for d in ds])
                            for e, ds in groups.items()], local_sem=T.sem.l0)
        cnt["l0"] = sum(len(e) for e in groups)
        need("y", ("l0", cnt["l0"]))
        dv = later_loads()

    def exchange(part, step, codes, plane, first, width, rsem, lsem):
        for scales in (0, 1):
            tl = []
            for d, es in part.items():
                n = step * (T.rank_of(d) - r) % N
                k, slot = first(n), 2 * NC + width * (n - 1)
                if scales:
                    src, dst = plane[:, k:k + width], plane[:, slot:slot + width]
                else:
                    src, dst = codes[:, k:k + width].bitcast(dt.uint8), codes[:, slot:slot + width].bitcast(dt.uint8)
                tl.append(RemoteDMATransfer(dst_ids=[did(d)], dma_engine_mask=_mask(es[scales]), remote_sem=T.sem[rsem],
                                            srcs=[src], dsts=[dst]))
                cnt[lsem] = cnt.get(lsem, 0) + len(es[scales])
            g.remote_dma_fused(tl, local_sem=T.sem[lsem])

    run("ff mk sg xh uu u2 u1 dec u3 ro lst" if r < N - 1 else "a0 ff a1 mk a2 sg a3 xh a4 uu u2 u1 n u3 dec ro lst")
    klst = k["lst"]

    def product(bank, codes, plane, a, n=NC):
        (lq, rq), (ls, rs) = codes, plane
        return done(ten.matmul_mx(T.ps[:, 512 * bank:512 * bank + n], lq, ls, rq[:, a:a + n], rs[:, a:a + n], True, True),
                    "kt")

    def pick(f, at, a, e, w=()):
        return f(T.ct[:, at:at + 16 * (e - a)], T.xs[:, 0:2048].indirect(T.lst[:, a:e]), w=w)

    a = 4 * (N - 1 - na)
    ks1 = pick(sc, 32 * na, a + 2 * na, 28, (klst, *dx.values()))
    ks2 = pick(sc, 768 - 16 * a, 0, a)
    c = pick(vc, 0, a, a + 2 * na, (klst,))
    kqc = V(qz, T.qc[:, 0:NC], T.sc[:, 0:NC], T.ct[:, 0:512], w=(c, ks1, kzero))
    need("g", kqc)
    exchange(out[0], -1, T.qc, T.sc, lambda n: S * (na - n), S, "e10", "l1")
    c = pick(vc, 768, 28, 32)
    kqc = V(qz, T.qc[:, NC:2 * NC], T.sc[:, NC:2 * NC], T.ct[:, 320:832], w=(c, ks2))
    need("g", kqc)
    exchange(out[1], -1, T.qc, T.sc, lambda n: 2 * NC - S * (n - na + 1), S, "e11", "l1")

    def pack_a(i):
        return V(qz, T.qa[:, 128 * i:128 * i + 128], T.sa[:, 128 * i:128 * i + 128], T.at[:, 512 * i:512 * i + 512],
                 w=(da[i // 2],))

    c = si(T.ec[:, 0:1], sfx, 0.0, -1.0)
    kec = si(T.ec[:, 1:2], e4, -c0 - 1.0, 0.25)
    si(T.ec[:, 2:3], e4, -c0 - 1.0 - r - 2048.0, 0.25)
    klab = si(T.lab[:], T.h2[:, 32:64], 16.0, -1.0)
    for i in range(4):
        kcp = si(T.cd[:, 16 * i:16 * i + 16], T.cw[:, 16 * (i // 2):16 * (i // 2) + 16], T.ec[:, 0:1], 1.0, w=(c,))
    kqw = V(qz, T.qw[:], T.sw[:], T.wt[:], w=(dw,))
    need("t", kqw, *kqx.values())
    kwx = product(2, (T.qw[:], T.qx), (T.sw[:], T.sx), 0, 512)
    kqa = [pack_a(0)]
    kwxs = sc(T.wx[:, 0:CUT], T.ps[:, 1024:1024 + CUT], w=(kwx,))
    if came:
        c = ts(T.nx[:, 1:2], own, inner, 999.0, A.subtract, A.mult)
        ts(T.nx[:, 0:1], T.nx[:, 1:2], inner, None, A.add, w=(c,))
    elif r:
        ts(T.nx[:, 0:1], T.md[:, 0:1], 999.0, own, A.mult, A.add)
    else:
        V(ms, T.nx[:, 0:1], 999.0)
    klb1 = ts(T.lb1[:], cum, sfx, T.ec[:, 1:2], A.subtract, A.add, w=(kec,))
    kqa.append(pack_a(1))
    need("y", klb1, klab)
    for h in (0, 1):
        done(syn.dma_start(T.lb[0:1, 256 * h:256 * h + 256], T.lab[h:16:2, :]), "dl0", 16)
        done(syn.dma_start(T.lb[1:2, 256 * h:256 * h + 256], T.lb1[h:16:2, :]), "dl1", 16)
    kqa += [pack_a(2), pack_a(3)]

    wide = [S * (nx + 1), NC - S * (nx + 1) + 2]
    V(ms, T.ht[:, 4 * wide[0]:896 - 4 * wide[1]], 0.0)
    kh, kqh = [], []
    for h in (0, 1):
        wait("t", "e1%d" % h, kqc)
        at = 896 - 4 * wide[1] if h else 0
        for i, bank in enumerate((0, 1, 4, 5) if h else (4, 5, 6, 7)):
            need("t", kqa[i], *(kh[i - 2:i - 1] if h and i > 1 else ()))
            m = product(bank, (T.qa[:, 128 * i:128 * i + 128], T.qc), (T.sa[:, 128 * i:128 * i + 128], T.sc),
                        2 * NC - S if h else NC + S * nx)
            o, tile = T.ps[:, 512 * bank + NC - wide[h]:512 * bank + NC], T.ht[:, at + i:at + 4 * wide[h]:4]
            if i % 2 == 0:
                kh.append(si(tile, o, 0.0, 0.05, AF.Relu, w=(m,)))
            else:
                kh.append(ts(tile, o, 0.0, 0.05, A.max, A.mult, w=(m,)))
        kqh.append(V(qz, T.qh[:, NC * h:NC * h + NC], T.sh[:, NC * h:NC * h + NC], T.ht[:, 384 * h:384 * h + 512],
                     w=kh[-2:]))
        need("g", kqh[h])
        exchange(back[h], 1, T.qh, T.sh, lambda n: NC * h + S * n - 2, S2, "e2%d" % h, "l2")

    c = V(tr, T.tc[:], T.cd[:], w=(kcp,))
    kqv = V(qz, T.qv[:], T.sv[:], T.vt[:], w=(dv,))
    vq, vs = (T.qv[:], T.qh), (T.sv[:], T.sh)
    need("t", kqv)
    m = product(3, vq, vs, 0)
    c = ts(T.t1[:], T.tc[:], T.ec[:, 2:3], -1.0, A.add, A.mult, w=(c,))
    ts(T.ii[:], T.tc[:], 0.125, 0.5625 + 0.125 * 127, A.mult, A.add)
    c2 = ts(T.fx[:], T.tc[:], T.nx[:, 0:1], 0.0, A.add, A.not_equal)
    c = ts(T.kk[:], T.t1[:], 7, None, A.bitwise_and, w=(c,))
    c2 = V(tt, T.s1[:], T.ii[:], T.fx[:], A.mult, w=(c2,))
    c = ts(T.k18[:], T.kk[:], float(S2), 1.0, A.mult, A.add, w=(c,))
    V(cp, T.vw[:, 2:S2], T.ps[:, 1536:1536 + S], w=(m,))
    c = V(tt, T.s2[:], T.s1[:], T.k18[:], A.add, w=(c, c2))
    for h in (0, 1):
        for u in (0, 1):
            kfin = V(cp, T.fin[:, 16 * h + u:16 * h + 16:2], T.s2[:, 32 * u + h:32 * u + 16:2], w=(c,))
    n = S2 * na
    wait("t", "e20")
    m = product(6, vq, vs, NC + n)
    V(cp, T.vw[:, 0:2], T.ps[:, 3072 + NC - n - 2:3072 + NC - n], w=(m,))
    V(cp, T.vw[:, S2:S2 + n], T.ps[:, 3072 + NC - n:3072 + NC])

    wait("t", "e21")
    m = product(7, vq, vs, 2 * NC - 2)
    c = V(cp, T.vw[:, S2 + n:N * S2], T.ps[:, 3584 + 2 + n:3584 + NC], w=(m,))
    ky = sc(T.yg[:], T.vw[:, 0:N * S2].indirect(T.fin[:, CUT // 16:32]), w=(c,))
    for h, (a, e) in enumerate(((0, CUT // 2), (CUT // 2, CUT), (CUT, 512))):
        if h < 2:
            c = V(tt, T.yt[:, a:e], T.vw[:, 0:N * S2].indirect(T.fin[:, a // 16:e // 16]), T.wx[:, a:e], A.add,
                  w=(c, kwxs) if h == 0 else ())
        else:
            c = V(tt, T.yt[:, a:e], T.yg[:], T.ps[:, 1024 + a:1024 + e], A.add, w=(ky,))
        qn = "ysy"[h]
        need(qn, c)
        done(queue[qn].dma_start(T.y[:, a:e], T.yt[:, a:e]), "dy%d" % h, 16)

    for s in SEMAPHORES:
        if cnt.get(s) and all(known.get((qn, s), 0) < cnt[s] for qn in queue):
            need("g", (s, cnt[s]))
